import numpy as np, ml_dtypes
CORES = [66,74,82,90,194,202,210,218]
N = 8
BF = ml_dtypes.bfloat16
def gentries(a):
    return np.ascontiguousarray(a.reshape(8, 16, -1).transpose(0, 2, 1)).reshape(8, -1)
def gtable(e):
    e = np.asarray(e); return np.ascontiguousarray(e.reshape(8, -1, 16).transpose(0, 2, 1)).reshape(128, -1).astype(np.int32)
P, H, S, ST, RO, CAP = 2048, 768, 192, 2, 2, 32
def parts(rng):
    x = rng.integers(0, 256, (N, 8, 16, P)); l = rng.integers(0, P, (N, 8, 16, H)); w = rng.integers(0, H, (N, 8, P))
    hs = np.ascontiguousarray(np.argsort(rng.random((N, 8, RO, H)), axis=-1)[..., :S])
    a = rng.choice(np.array([0.5, 0.7, 0.9, 1.1]), (N, 8, 1, RO, 1)) + 0.4 * (rng.random((N, 8, 1, RO, S)) - 0.5)
    d = np.minimum((256 * rng.random((N, 8, 16, RO, S)) ** a).astype(np.int64), 255)
    return x, l, w, hs, d
def lanes(rng, l, w, hs):
    K = (P - 2) // ((ST + 1) * S); steps = np.zeros((N, 8, ST + 1, S, K), np.int64)
    for q in range(N):
        for g in range(8):
            o = (4 + rng.permutation(H - 8)[:(ST + 1) * S]).reshape(ST + 1, S)
            c = (1 + rng.permutation(P - 2)[:(ST + 1) * S * K]).reshape(ST + 1, S, K)
            u = rng.integers(0, K, (16, ST + 1, S))
            l[q, g][:, o] = c[np.arange(ST + 1)[:, None], np.arange(S), u]
            w[q, g][c[:ST]] = o[1:, :, None]
            hs[q, g, 0] = o[0]; steps[q, g] = c
    return steps
def levels(rng):
    x = rng.integers(0, 100, (N, 8, 16, P)); x[1::2] += 150
    x[:, 4:] = rng.integers(0, 30, (N, 4, 16, P)); x[1::2, 4:] += 225
    return x
def pack(x, l, w, hs, d):
    return {"xs": x.reshape(N, 128, P).astype(np.float32).astype(BF), "hl": np.ascontiguousarray(l.reshape(N, 128, H)).astype(np.int32), "wr": np.ascontiguousarray(w).astype(np.int32),
            "ho": np.stack([gtable(a.reshape(8, -1)) for a in hs]), "dm": d.reshape(N, 128, RO * S).astype(np.float32).astype(BF)}
def setup_inputs(rng):
    return pack(*parts(rng))
def setup_inputs_room(rng):
    x, l, w, hs, d = parts(rng); x = levels(rng); c = lanes(rng, l, w, hs)
    for q in range(N):
        for g in range(8):
            n = int(rng.choice(np.array([0, 1, CAP - 1, CAP, CAP + 1, S])))
            if q == 0: n = (CAP, CAP + 1, S, CAP - 1, 1, 0, CAP, CAP + 1)[g]
            v = d[q, g, :, 0]; v[:] = 0
            v[:, rng.permutation(S)[:n]] = rng.integers(100, 150, (16, n)) if q % 2 == 0 else 255
            if q == 2 and g < 4:
                i = 1 + rng.permutation(S) % ST; v[:] = rng.integers(100, 150, (16, S))
                x[q, g][:, c[q, g][i, np.arange(S)]] += 150
    return pack(x, l, w, hs, d)
def setup_inputs_trade(rng):
    x, l, w, hs, d = parts(rng); x = levels(rng); c = lanes(rng, l, w, hs); ends = np.array([0, 1, 2, 3, H - 4, H - 3, H - 2, H - 1])
    for q in range(N):
        for g in range(8):
            last = c[q, g, ST]; w[q, g][last] = rng.choice(ends, last.shape)
            m = rng.random(S) < 0.5; m[:3] = True
            if q % 2 == 1 and g >= 6: m[CAP // 2:] = False
            d[q, g, :, 0] = np.where(m, rng.integers(100, 150, (16, S)) if q % 2 == 0 else 255, 0)
            if g >= 4: w[q, g][last[:3]] = np.array([1, H - 1, 0])[:, None]
            if q % 2 == 1:
                own = l[q, g][0, hs[q, g, 0]][m]
                l[q, g][:, ends] = rng.permutation(np.concatenate([rng.choice(own, 64), rng.integers(0, P, 64)])).reshape(16, 8)
                if g >= 4:
                    l[q, g][:, np.array([1, H - 1, 0])] = np.array([own[0], P - 1, 0])
                    hs[q, g, 1] = hs[q, g, 0]
                    d[q, g, :, 1] = np.where(m, 255, 0) if q % 4 == 1 else 0
                    if q % 4 == 3: x[q, g][:, own[0]] = 255
    return pack(x, l, w, hs, d)
def setup_inputs_ties(rng):
    x, l, w, hs, d = parts(rng); pal = rng.integers(0, 255, (N, 8, 16, 7))
    x = np.take_along_axis(pal, rng.integers(0, 7, (N, 8, 1, P)), 3)
    for t in range(RO):
        e = np.take_along_axis(l[:, :, t], hs[:, :, t], 2); v = np.take_along_axis(x, e[:, :, None, :], 3)
        o = np.argsort(rng.random((N, 8, 16, S)), axis=2)
        d[:, :, :, t] = v + (o >= rng.integers(8, 11, (N, 8, 1, S)))
    if RO > 2:
        q = int(rng.integers(0, N)); d[q, :, :, :2] = 255; d[q, 0, :, 0, 0] = 0
        w[q, 0, l[q, 0, 0, hs[q, 0, 0, 0]]] = np.setdiff1d(np.arange(H), hs[q, 0, 0])[0]
    return pack(x, l, w, hs, d)
def setup_inputs_alike(rng):
    x, l, w, hs, d = parts(rng)
    w[:, 0] = rng.choice(rng.permutation(H)[:40], (N, P))
    l[:, 2] = rng.choice(np.concatenate([np.array([0, P - 1]), 1 + rng.permutation(P - 2)[:60]]), (N, 16, H))
    x[:, 3] = rng.integers(0, 16, (N, 16, P)); v = rng.integers(0, 256, x[1::2, 3].shape)
    x[1::2, 3] = np.where(np.argsort(rng.random(v.shape), axis=1) < 12, 255, v); d[::2, 3, :, 0] = 0
    w[:, 4] = np.take_along_axis(hs[:, 4, 0], rng.integers(0, S, (N, P)), 1)
    x[:, 5] = rng.choice(np.array([0, 1, 254, 255]), (N, 16, P))
    for q in range(N):
        e = l[q, 6][0, hs[q, 6, 0]]
        l[q, 6][rng.integers(1, 16, S), w[q, 6][e]] = e
    w[:, 7, ::2] = rng.choice(np.array([0, H - 1]), (N, (P + 1) // 2))
    return pack(x, l, w, hs, d)
def setup_inputs_spread(rng):
    x, l, w, hs, d = parts(rng)
    x = np.minimum(np.exp2(8 * rng.random((N, 8, 1, P))) * (0.25 + 1.5 * rng.random((N, 8, 16, P))), 255).astype(np.int64)
    d = np.minimum(np.exp2(8 * rng.random((N, 8, 1, RO, S))) * (0.25 + 1.5 * rng.random((N, 8, 16, RO, S))), 255).astype(np.int64)
    w = np.minimum((H * rng.random((N, 8, P)) ** 2).astype(np.int64), H - 1)
    q = rng.permutation(N); d[q[0]] = 0; d[q[1]] = 255
    return pack(x, l, w, hs, d)
def check_inputs(d):
    bad = []
    for k in ("xs", "dm"):
        v = np.asarray(d[k]).astype(np.float32)
        if not np.all((v >= 0) & (v <= 255) & (v == np.floor(v))): bad.append("whole numbers of " + k)
    for k, hi in (("hl", P - 1), ("wr", H - 1), ("ho", H - 1)):
        if np.min(d[k]) < 0 or np.max(d[k]) > hi: bad.append("range of " + k)
    e = np.sort(np.stack([gentries(a) for a in d["ho"]]).reshape(N, 8, RO, S), axis=-1)
    if np.any(e[..., 1:] == e[..., :-1]): bad.append("different holders of a round in ho")
    return bad
def nearest(x, lc, x0):
    dist = np.add.reduce(np.abs(x[:, lc] - x0[:, None, :]), axis=0)
    j = np.argmin(dist, axis=0)
    return j, lc[j, np.arange(lc.shape[1])]
def lowest(key, on, size):
    k = np.arange(key.shape[0]); first = np.full(size, key.shape[0]); np.minimum.at(first, key[on], k[on])
    return on & (first[key] == k)
def climb(x, l, w, h0, d, t, need):
    k = np.arange(S); e0 = l[t, h0]; x0 = x[:, e0]
    vouched = np.zeros(H, bool); vouched[h0] = True
    hv, jv, ev = [h0], [np.full(S, t)], [e0]
    up = np.ones(S, bool); m = np.zeros(S, np.int64); h = w[e0]
    for i in range(1, ST + 1):
        up = lowest(h, up, H) & ~vouched[h]
        vouched[h[up]] = True
        j, e = nearest(x, l[:, h], x0)
        able = up & (np.add.reduce((x[:, e] >= d).astype(np.int64), axis=0) >= need)
        m[able] = i; up = up & ~able
        hv.append(h); jv.append(j); ev.append(e); h = w[e]
    for i in range(ST + 1):
        c = (m > 0) & (m >= i)
        v = np.where(m > i, ev[min(i + 1, ST)], e0)
        l[jv[i][c], hv[i][c]] = v[c]
        if i > 0: w[ev[i][m > i]] = hv[i][m > i]
    c = m > 0
    w[e0[c]] = np.stack(hv)[m, k][c]
    u = np.flatnonzero(up)[:CAP]
    return int(np.count_nonzero(c)), (e0[u], x0[:, u], d[:, u], h[u])
def reference(xs, hl, wr, ho, dm):
    x = xs.astype(np.float32).astype(np.int64).reshape(N, 8, 16, P); l = hl.astype(np.int64).reshape(N, 8, 16, H); w = wr.astype(np.int64)
    hs = np.stack([gentries(a) for a in ho]).astype(np.int64).reshape(N, 8, RO, S); d = dm.astype(np.float32).astype(np.int64).reshape(N, 8, 16, RO, S)
    odd = [0] * N
    for t in range(RO):
        paid = [0] * N; sent = {}
        for a in range(N):
            for g in range(8):
                n, sent[a, g] = climb(x[a, g], l[a, g], w[a, g], hs[a, g, t], d[a, g, :, t], t, 9 + odd[a])
                paid[a] += n
        swaps = []
        for a in range(N):
            b = (a + 1 + t % (N - 1)) % N
            for g in range(8):
                e0, x0, dd, h = sent[a, g]
                j, e1 = nearest(x[b, g], l[b, g][:, h], x0)
                able = np.add.reduce((x[b, g][:, e1] >= dd).astype(np.int64), axis=0) >= 9 + odd[b]
                ok = lowest(e1, able & ~np.isin(e1, sent[b, g][0]), P)
                swaps.append((a, b, g, e0[ok], e1[ok]))
        for a, b, g, e0, e1 in swaps:
            va, vb = x[a, g][:, e0], x[b, g][:, e1]
            x[a, g][:, e0] = vb; x[b, g][:, e1] = va
        odd = [n & 1 for n in paid]
    return {"yx": x.reshape(N, 128, P).astype(np.float32).astype(BF), "yl": l.reshape(N, 128, H).astype(np.float32), "yw": w.astype(np.float32)}

@@ -1,0 +1,775 @@
+from concourse.mybir import AluOpType, AxisListType, ActivationFunctionType
+
+ALU = AluOpType
+ACT = ActivationFunctionType
+NP, NH, NS, RO, CAP = 2048, 768, 192, 2, 32
+HS = NS // 2
+B = 4096.0
+BE = 5184.0
+HOP = 110
+PE = 2.0
+FLY = 2000
+SPLIT = {(1, 0): 48, (1, 1): 64, (2, 0): 64, (2, 1): 48}
+WIDE = {(1, 0): False, (1, 1): True, (2, 0): True, (2, 1): True}
+XSPLIT = 16
+PIECE = 32
+XEG = (16, 0)
+SEED, JITTER, PASSES = 1, 200, 3000
+ARENA = {"f": ("af", "float32"), "b": ("ab", "bfloat16"), "h": ("ah", "float16"), "u": ("au", "uint16"), "i": ("ai", "int32")}
+
+
+def sub(v, a, b, step=1, p0=None, p1=None):
+    return (v[0], v[1] + a, v[1] + b, step, v[4] if p0 is None else p0, v[5] if p1 is None else p1)
+
+
+def part(v, p0, p1):
+    return (v[0], v[1], v[2], v[3], p0, p1)
+
+
+def width(v):
+    return (v[2] - v[1] + v[3] - 1) // v[3]
+
+
+def is_ps(v):
+    return v[0][0] == "p"
+
+
+def plan():
+    ops = []
+    size = {k: 0 for k in ARENA}
+
+    def new(k, n):
+        lo = size[k]
+        size[k] = lo + (n + 15) // 16 * 16
+        return (ARENA[k][0], lo, lo + n, 1, 0, 128)
+
+    def two(*vs):
+        return all(v[0] in ("ab", "ah", "au") for v in vs)
+
+    def add(eng, fn, r, w, cost, kind="c", extra=None):
+        r = [v for v in r if isinstance(v, tuple)]
+        ops.append({"eng": eng, "fn": fn, "r": r, "w": list(w), "cost": cost, "kind": kind, "extra": extra})
+
+    def S(A, s):
+        return A(s) if isinstance(s, tuple) else s
+
+    def vcost(n, half):
+        return max(64, n // 2 if half else n)
+
+    def memset(o, c):
+        add("v", lambda E, A: E.memset(A(o), c), [], [o], vcost(width(o), two(o)))
+
+    def copy(o, i):
+        add("v", lambda E, A: E.tensor_copy(A(o), A(i)), [i], [o], vcost(width(o), two(o, i)))
+
+    def ts(o, i, s1, op0, s2=None, op1=None):
+        if op1 is None:
+            fn = lambda E, A: E.tensor_scalar(A(o), A(i), S(A, s1), None, op0)
+        else:
+            fn = lambda E, A: E.tensor_scalar(A(o), A(i), S(A, s1), S(A, s2), op0, op1)
+        add("v", fn, [i, s1, s2], [o], vcost(width(o), two(o, i)))
+
+    def tt(o, a, b, op):
+        n = width(o) * (1 if is_ps(a) or is_ps(b) else 2)
+        add("v", lambda E, A: E.tensor_tensor(A(o), A(a), A(b), op), [a, b], [o], max(64, n))
+
+    def scan(o, d0, d1, init, op0, op1):
+        add("v", lambda E, A: E.tensor_tensor_scan(A(o), A(d0), A(d1), S(A, init), op0, op1), [d0, d1, init], [o],
+            vcost(width(o), two(o, d0, d1)))
+
+    def act(o, i, f, bias=None, scale=None, acc=None):
+        def fn(E, A):
+            kw = {}
+            if bias is not None:
+                kw["bias"] = S(A, bias)
+            if scale is not None:
+                kw["scale"] = S(A, scale)
+            if acc is not None:
+                kw["accum_out"] = A(acc)
+            return E.activation(A(o), A(i), f, **kw)
+        add("a", fn, [i, bias, scale], [o] + ([acc] if acc else []), max(64, width(o)) + 30)
+
+    def gcost(n):
+        return 60 + int(1.56 * n)
+
+    def gather(eng, o, win, off, f=None, bias=None):
+        if eng == "v":
+            fn = lambda E, A: E.tensor_copy(A(o), A(win).indirect(A(off)))
+        elif bias is None:
+            fn = lambda E, A: E.activation(A(o), A(win).indirect(A(off)), ACT.Copy)
+        else:
+            fn = lambda E, A: E.activation(A(o), A(win).indirect(A(off)), f, bias=bias)
+        add(eng, fn, [win, off], [o], gcost(width(o)))
+
+    def gtt(o, win, off, b, op):
+        add("v", lambda E, A: E.tensor_tensor(A(o), A(win).indirect(A(off)), A(b), op), [win, off, b], [o], gcost(width(o)))
+
+    def scatter(win, off, i, b=None):
+        if b is None:
+            fn = lambda E, A: E.tensor_copy(A(win).indirect(A(off)), A(i))
+        else:
+            fn = lambda E, A: E.tensor_tensor(A(win).indirect(A(off)), A(i), A(b), ALU.add)
+        add("v", fn, [off, i, b], [win], 60 + int(3.8 * width(i)))
+
+    def mark(win, off, i):
+        add("a", lambda E, A: E.activation(A(win).indirect(A(off)), A(i), ACT.Tanh), [off, i], [win], 80 + int(3.8 * width(i)))
+
+    def mm(items, first=True, last=True, each=0):
+        def fn(E, A):
+            ins = None
+            for n, (o, l, r) in enumerate(items):
+                if each:
+                    st, sp = n % each == 0, n % each == each - 1
+                else:
+                    st, sp = first and n == 0, last and n == len(items) - 1
+                ins = E.matmul(A(o), A(l), A(r), st, sp)
+            return ins
+        c = int(sum(max(min(64, width(l)), width(r)) for o, l, r in items) / PE) + 40
+        add("t", fn, [x for o, l, r in items for x in (l, r)], [o for o, l, r in items], c)
+
+    def iota(o, pat, base, cm):
+        if o[0] == "ai":
+            fn = lambda E, A: E.iota(A(o), pat, base, cm)
+        else:
+            fn = lambda E, A: E.iota(A(o), pat, base, cm, allow_small_or_imprecise_dtypes=True)
+        add("g", fn, [], [o], 150 + 2 * width(o))
+
+    def asel(o, i, pat, op, base, cm):
+        add("g", lambda E, A: E.affine_select(A(o), A(i), pat, op, 0.0, base, cm), [i], [o], 200 + 2 * width(o))
+
+    def dma(eng, fn, r, w, nbytes):
+        add(eng, fn, r, w, nbytes, kind="dma")
+
+    def message(src, dst, t, k):
+        tok = ("msg", 2 * t + k, 2 * t + k + 1, 1, 0, 128)
+        add("g", None, [src], [tok], 500, kind="send", extra=(src, dst, t, k))
+        add("x", None, [tok], [dst], FLY, kind="recv", extra=(t, k))
+
+    PD = [("pa", 0, 1024, 1, 0, 128), ("pb", 0, 1024, 1, 0, 128)]
+    BK = [sub(PD[q // 2], 512 * (q % 2), 512 * (q % 2) + 512) for q in range(4)]
+    P4, P5, P6, P7 = [("p%d" % k, 0, 512, 1, 0, 128) for k in (4, 5, 6, 7)]
+
+    ho32, wr32, hl32 = new("i", 24), part(new("i", 512), 0, 32), new("i", NH)
+    X, DM = new("b", NP + 64), new("b", 416)
+    HL, W, V = new("f", 1152), new("f", NP + NS), new("f", NH + NS)
+    Xg, HLg, Wg, Vg = sub(X, 0, NP), sub(HL, 0, NH), sub(W, 0, NP), sub(V, 0, NH)
+    dma("s", lambda E, A, T: E.dma_start(A(wr32), T.wr[:]), [], [wr32], 65536)
+    dma("a", lambda E, A, T: E.dma_start(A(ho32), T.ho[:]), [], [ho32], 12288)
+    dma("s", lambda E, A, T: E.dma_start(A(hl32), T.hl[:]), [], [hl32], 393216)
+    dma("s", lambda E, A, T: E.dma_start(A(Xg), T.xs[:]), [], [Xg], 524288)
+    for t in range(RO):
+        dma("s", lambda E, A, T, t=t: E.dma_start(A(sub(DM, 208 * t, 208 * t + NS)), T.dm[:, NS * t:NS * (t + 1)]), [],
+            [sub(DM, 208 * t, 208 * t + NS)], 49152)
+
+    ones = new("b", 512)
+    memset(ones, 1.0)
+    o128 = sub(ones, 0, 128)
+
+    def fill(o, c):
+        act(o, sub(ones, 0, width(o)), ACT.Copy, scale=float(c))
+
+    def scaled(m, c):
+        o = new("b", width(m))
+        act(o, m, ACT.Copy, scale=c)
+        return o
+    kg, qb, kc = new("b", 128), new("b", NS), new("b", 128)
+    iota(kg, [[-16, 8], [0, 16]], 0, 1)
+    iota(qb, [[0, 12], [1, 16]], 0, 0)
+    pid, pmi, pm = new("i", 1), new("i", 1), new("f", 1)
+    iota(pid, [[0, 1]], 0, 1)
+    selW = part(new("b", 512), 0, 32)
+    asel(selW, part(ones, 0, 32), [[-1, 4], [-4, 8], [0, 16]], ALU.is_equal, 0, 1)
+    q128 = sub(qb, 0, 128)
+    rs = [new("b", 128) for t in range(RO)]
+    I, blk, c16, kb = new("b", 128), new("b", 128), new("f", 16), new("b", 32)
+    for t in range(RO):
+        ts(rs[t], kg, float(t), ALU.is_equal)
+    tt(I, kg, q128, ALU.is_equal)
+    ts(kc, kg, 0.0, ALU.max, 15.0, ALU.min)
+    tt(blk, kg, kc, ALU.is_equal)
+    ts(c16, sub(qb, 0, 16), 16.0, ALU.mult)
+    copy(sub(kb, 0, 16), sub(qb, 0, 16))
+    ts(sub(kb, 16, 32), sub(qb, 0, 16), 16.0, ALU.add)
+    ts(pmi, pid, 15, ALU.bitwise_and)
+    copy(pm, pmi)
+    ho16 = new("u", 24)
+    copy(ho16, ho32)
+    MH, ME, mt, mt2 = new("f", NS), new("f", NS), new("b", NS), new("b", NS)
+    ts(mt2, qb, pm, ALU.is_lt, -B, ALU.mult)
+    ts(mt, qb, pm, ALU.is_equal, B, ALU.mult)
+    tt(ME, mt2, mt, ALU.add)
+    copy(MH, ME)
+    ts(sub(MH, 15, NS, 16), sub(MH, 15, NS, 16), -2 * B, ALU.add)
+    ts(sub(ME, 15, NS, 16), sub(ME, 15, NS, 16), -B - BE, ALU.add)
+    wr16 = part(new("h", 512), 0, 32)
+    copy(wr16, wr32)
+    for q in range(4):
+        mm([(BK[q], sub(selW, 128 * q, 128 * q + 128), wr16)])
+        act(sub(W, 512 * q, 512 * q + 512), BK[q], ACT.Copy)
+    copy(HLg, hl32)
+    fill(sub(V, 0, 480), 0)
+    fill(sub(V, 480, 960), 0)
+    fill(sub(HL, NH, 1152), 0)
+    fill(sub(W, NP, NP + NS), 0)
+    memset(sub(X, NP, NP + 64), 0.0)
+    for t in range(RO):
+        memset(sub(DM, 208 * t + NS, 208 * t + 208), 512.0)
+    tin = [new("f", NS) for t in range(RO)]
+    fill(tin[0], 1)
+    fill(tin[1], 4)
+    nI, I32, nI32, bigI = scaled(I, -1.0), scaled(I, 32.0), scaled(I, -32.0), new("b", 128)
+    I2k, I3k, nI3k = scaled(I, 2048.0), scaled(I, 3072.0), scaled(I, -3072.0)
+    ts(bigI, I, 2.0 ** 60, ALU.mult, 2.0 ** 60, ALU.mult)
+    nblk, blk32 = scaled(blk, -1.0), scaled(blk, 32.0)
+    nrs = [scaled(rs[t], -1.0) for t in range(RO)]
+    G8 = scaled(sub(blk, 0, 128, 16), 16.0)
+    o16 = new("b", 128)
+    memset(o16, 0.0625)
+    rm = new("f", 16)
+    ts(rm, sub(qb, 0, 16), pm, ALU.is_equal)
+    half, wb, thr = new("b", NS), new("f", NS), new("f", NS)
+    memset(half, 0.5)
+    scan(wb, half, sub(ones, 0, NS), 2.0 ** 97, ALU.mult, ALU.mult)
+    act(thr, wb, ACT.Copy, scale=2.5)
+    w16, w0, wcol = new("f", 16), new("f", 1), new("f", 12)
+    tt(w16, sub(wb, 0, 16), rm, ALU.mult)
+    add("v", lambda E, A: E.tensor_reduce(A(w0), A(w16), AxisListType.X, ALU.add), [w16], [w0], 64)
+    ts(w0, w0, 2.0 ** -66, ALU.mult)
+    ts(wcol, sub(wb, 0, NS, 16), 2.0 ** -30, ALU.mult, w0, ALU.mult)
+    WC = new("b", 12 * 128)
+    for c in range(12):
+        act(sub(WC, 128 * c, 128 * c + 128), blk, ACT.Copy, scale=sub(wcol, c, c + 1))
+    RK = new("b", 128)
+    ts(RK, q128, 0.0, ALU.is_equal, 131072.0, ALU.mult)
+    xoff = new("u", 8)
+    ts(xoff, sub(c16, 0, 8), 15.0, ALU.add)
+    sw = new("b", 12)
+    ts(sw, sub(c16, 0, 12), pm, ALU.add)
+    srow = part(new("f", NS), 0, 1)
+    iota(srow, [[1, NS]], 0, 0)
+    spare = [part(new("h", NS), 0, 1) for n in range(3)]
+    for n, c in enumerate((768.0 - 2048.0, 960.0, 992.0)):
+        ts(spare[n], srow, c, ALU.add)
+    zrow = part(new("b", 512), 0, 1)
+    memset(zrow, 0.0)
+    C4, kcol, TRI = new("f", 2), new("f", 2), new("b", 64)
+    ts(C4, sub(sw, 0, 2), 2048.0 - BE, ALU.add)
+    ts(kcol, sub(sw, 0, 2), 0.5, ALU.add)
+    for c in range(2):
+        ts(sub(TRI, 32 * c, 32 * c + 32), kb, sub(sw, c, c + 1), ALU.is_le, B, ALU.mult)
+    EQ, SM, KS = [[new(k, 128) for h in range(2)] for k in "bff"]
+    one1 = part(o128, 0, 1)
+    need, nneed, nneedB = 9.0, -9.0, -9.0 - B
+    Ag, Ab, XE = new("b", 3072), new("b", 3072), new("b", 3072)
+    Ebuf = new("b", 1248)
+    junk = new("b", NS)
+
+    def wrap(src, M, off, s=None, u=None):
+        n = width(src)
+        if s is None:
+            s = new("f", n)
+        scan(s, src, sub(M, 0, n), -B, ALU.max, ALU.add)
+        sw_ = sub(s, 15, n, 16)
+        if off is None:
+            return sw_, None
+        if u is None:
+            u = new("u", n // 16)
+        ts(u, sw_, off, ALU.add)
+        return sw_, u
+
+    def flagwrap(o, scale, flag, row):
+        mm([(o, one1, row), (o, scale, flag)])
+        return wrap(o, MH, None)[0]
+
+    def dedupe(hb, hcols, vb, dead):
+        Sp = sub(P7, 0, NS)
+        items, pos = [], 0
+        for c in range(12):
+            e = sub(Ebuf, pos, pos + NS - 16 * c)
+            pos += NS - 16 * c
+            ts(e, sub(hb, 16 * c, NS), hcols(c), ALU.subtract, B, ALU.is_equal)
+            items.append((sub(Sp, 16 * c, NS), sub(WC, 128 * c, 128 * c + 128), e))
+        items.append((Sp, bigI, vb))
+        if dead is not None:
+            items.append((Sp, bigI, dead))
+        mm(items)
+        ns = new("b", NS)
+        tt(ns, Sp, thr, ALU.is_ge)
+        return ns
+
+    def hv(v, h, n=HS):
+        return sub(v, n * h, n * h + n)
+
+    def distances(h, Lu, x0, step):
+        key, k = sub((P4, P5)[h], 0, 128), SPLIT[step, h]
+        ag, ab, xe = hv(Ag, h, 1536), hv(Ab, h, 1536), hv(XE, h, 1536)
+        mm([(key, one1, part(q128, 0, 1))], last=False)
+        close = [(key, one1, sub(zrow, 0, 128))]
+        if not WIDE[step, h]:
+            for eng, a, b in (("v", 0, k), ("a", k, HS)):
+                gather(eng, sub(ag, 16 * a, 16 * b), Xg, sub(Lu, HS * h + a, HS * h + b))
+            for q in range(4):
+                items = []
+                for j in range(4):
+                    o = sub(BK[q], HS * j, HS * j + HS)
+                    items += [(o, nI, hv(x0, h)), (o, I, sub(ag, 4 * q + j, 1536, 16))]
+                mm(items, each=2)
+                act(sub(ab, 384 * q, 384 * q + 384), sub(BK[q], 0, 384), ACT.Abs)
+                items = [(sub(key, 4 * q + j, 128, 16, 0, HS), sub(ab, 384 * q + HS * j, 384 * q + HS * j + HS), G8) for j in range(4)]
+                mm(items + (close if q == 3 else []), first=False, last=(q == 3))
+            return
+        cuts = [("v", a, min(a + PIECE, k)) for a in range(0, k, PIECE)] + [("a", a, min(a + 32, HS)) for a in range(k, HS, 32)]
+        q = 2 * h
+        for eng, a, b in cuts:
+            lu, src = sub(Lu, HS * h + a, HS * h + b), sub(ag, 16 * a, 16 * b)
+            if eng == "v":
+                gtt(src, Xg, lu, sub(xe, 16 * a, 16 * b), ALU.subtract)
+            else:
+                gather("a", src, Xg, lu)
+                o = sub(BK[q % 4], 0, 16 * (b - a))
+                q += 1
+                mm([(o, nI, sub(xe, 16 * a, 16 * b)), (o, I, src)])
+                src = o
+            act(sub(ab, 16 * a, 16 * b), src, ACT.Abs)
+        mm([(sub(key, j, 128, 16, 0, HS), sub(ab, j, 1536, 16), G8) for j in range(16)] + close, first=False)
+
+    def pick(h, n, Lf, prod):
+        bank = (P4, P5)[h]
+        key, oh, ep = sub(bank, 0, 128), sub(bank, 128, 128 + n), sub(bank, 256, 256 + n)
+        copy(KS[h], key)
+        scan(SM[h], RK, key, 0.0, ALU.add, ALU.min)
+        gtt(EQ[h], SM[h], xoff, KS[h], ALU.is_equal)
+        mm([(oh, part(EQ[h], 0, n), sub(I, 0, n, 1, 0, n))])
+        tt(prod, oh, Lf, ALU.mult)
+        mm([(ep, blk, prod)])
+        return oh, ep
+
+    for t in range(RO):
+        h0 = sub(ho16, 12 * t, 12 * t + 12)
+        dm = sub(DM, 208 * t, 208 * t + NS)
+        vbias = (-0.1, -0.9)[t]
+        Lf, ohs, offL = [new("f", 288) for h in range(2)], [new("b", 288) for h in range(2)], [new("u", 18) for h in range(2)]
+        for h in range(2):
+            ts(hv(ohs[h], 0), sub(ones, 0, HS), sub(rm, t, t + 1), ALU.mult)
+            copy(sub(offL[h], 0, 6), sub(ho32, 12 * t + 6 * h, 12 * t + 6 * h + 6))
+        mark(V, h0, tin[t])
+        L0h = new("h", NS)
+        gather("v", L0h, hl32 if t == 0 else HLg, h0)
+        for h in range(2):
+            gather("a", hv(Lf[h], 0), HLg, hv(h0, h, 6))
+        e0p = sub(P6, 0, NS)
+        mm([(e0p, rs[t], L0h)])
+        s0 = new("f", NS)
+        es0, e0u = wrap(e0p, ME, BE, s0)
+        e0b = new("f", 208)
+        memset(sub(e0b, NS, 208), 4000.0)
+        act(sub(e0b, 0, NS), e0p, ACT.Copy)
+        hb1 = new("h", NS)
+        gather("v", hb1, Wg, e0u)
+        hs1, h1u = wrap(hb1, MH, B)
+        L1u = new("u", NS)
+        gather("v", L1u, hl32 if t == 0 else HLg, h1u)
+        for h in range(2):
+            gather("a", hv(Lf[h], 1), HLg, hv(h1u, h, 6))
+        vb1 = new("b", NS)
+        gather("a", vb1, Vg, h1u, ACT.Relu, vbias)
+        ns1 = dedupe(hb1, lambda c: sub(hs1, 16 * c, 16 * c + 1), vb1, None)
+        pw = flagwrap(sub(P7, 256, 256 + NS), I2k, ns1, spare[0])
+        tw, offM = new("f", 12), new("u", 12)
+        tt(tw, pw, hs1, ALU.max)
+        ts(offM, tw, B, ALU.add)
+        mark(V, offM, tin[t])
+        for h in range(2):
+            copy(sub(offL[h], 6, 12), hv(offM, h, 6))
+        x0w = new("b", 208)
+        x0 = sub(x0w, 0, NS)
+        memset(sub(x0w, NS, 208), 0.0)
+        for h in range(2):
+            gather("a", hv(x0, h), Xg, hv(e0u, h, 6))
+        for h in range(2):
+            for j in range(16):
+                o = sub(hv(XE, h, 1536), j, 1536, 16)
+                if j < XEG[h]:
+                    asel(o, hv(x0, h), [[0, HS]], ALU.is_ge, 0, 0)
+                else:
+                    copy(o, hv(x0, h))
+        prod1, prod2, hb2 = new("h", NS), new("h", NS), new("h", NS)
+        s1, s2, sh = new("f", NS), new("f", NS), new("f", NS)
+        e1u, e2u, h2u, L2u = new("u", 12), new("u", 12), new("u", 12), new("u", NS)
+        ge1, ge2, vb2 = new("b", NS), new("b", NS), new("b", NS)
+        h3w = new("f", 208)
+        memset(sub(h3w, NS, 208), 0.0)
+        for h in range(2):
+            distances(h, L1u, x0, 1)
+        for h in range(2):
+            oh, ep = pick(h, HS, hv(Lf[h], 1), hv(prod1, h))
+            wrap(ep, ME, BE, hv(s1, h), hv(e1u, h, 6))
+            act(hv(ohs[h], 1), oh, ACT.Copy)
+            gather("v", hv(hb2, h), Wg, hv(e1u, h, 6))
+            wrap(hv(hb2, h), MH, B, hv(sh, h), hv(h2u, h, 6))
+            gather("v", hv(L2u, h), HLg, hv(h2u, h, 6))
+            gather("a", hv(Lf[h], 2), HLg, hv(h2u, h, 6))
+            distances(h, L2u, x0, 2)
+        gtt(ge1, Xg, e1u, dm, ALU.is_ge)
+        cp, cn = sub(P6, 0, NS), sub(P6, 256, 256 + NS)
+        mm([(cp, blk, ge1), (cp, I32, ns1), (cn, blk, ge1), (cn, nI32, ns1)], each=2)
+        dead1, m1n = new("b", NS), new("b", NS)
+        ts(dead1, cp, need, ALU.is_ge)
+        ts(m1n, cn, need, ALU.is_ge, -1.0, ALU.mult)
+        hm = sub(P7, 256, 256 + NS)
+        mm([(hm, I, hb2), (hm, I2k, dead1)])
+        hm = wrap(hm, MH, None)[0]
+        gather("a", vb2, Vg, h2u, ACT.Relu, vbias)
+        ns2 = dedupe(hb2, lambda c: sub(hm, 16 * c, 16 * c + 1), vb2, dead1)
+        pA = sub(P6, 0, NS)
+        mm([(pA, blk, prod1), (pA, nrs[t], L0h)])
+        pA1 = new("h", NS)
+        tt(pA1, pA, m1n, ALU.mult)
+        failed, pos, m2n = new("b", NS), new("b", NS), new("b", NS)
+        pA2, pB2, offW = new("h", NS), new("h", NS), new("u", 24)
+        m1s, m1r, acc, sidx = new("h", 96), new("h", 96), new("f", 2), new("u", 2)
+        tw2 = new("f", 24)
+        for h in range(2):
+            oh, ep = pick(h, HS, hv(Lf[h], 2), hv(prod2, h))
+            wrap(ep, ME, BE, hv(s2, h), hv(e2u, h, 6))
+            act(hv(ohs[h], 2), oh, ACT.Copy)
+            gtt(hv(ge2, h), Xg, hv(e2u, h, 6), hv(dm, h), ALU.is_ge)
+            gather("a", hv(h3w, h), Wg, hv(e2u, h, 6))
+            cp, cn = sub(P6, 0, HS), sub(P7, 0, HS)
+            mm([(cp, I32, hv(ns2, h)), (cp, blk, hv(ge2, h))])
+            mm([(cn, nI32, hv(ns2, h)), (cn, blk, hv(ge2, h))])
+            ts(hv(failed, h), cp, need, ALU.is_lt)
+            scan(hv(pos, h), hv(failed, h), hv(failed, h), sub(pos, HS - 1, HS) if h else 0.0, ALU.add, ALU.max)
+            if h:
+                for c in range(2):
+                    act(junk, pos, ACT.Sign, bias=sub(kcol, c, c + 1), scale=-1.0, acc=sub(acc, c, c + 1))
+                ts(sidx, acc, 0.5, ALU.mult, 96.0, ALU.add)
+                gather("v", sub(m1s, 0, 32), x0w, sidx)
+                gather("v", sub(m1s, 32, 64), sub(DM, 208 * t, 208 * t + 208), sidx)
+                gather("v", sub(m1s, 64, 96), h3w, sidx)
+                message(m1s, m1r, t, 0)
+            ts(hv(m2n, h), cn, need, ALU.is_ge, -1.0, ALU.mult)
+            bank = (P4, P5)[h]
+            pA, pB = sub(bank, 0, HS), sub(bank, HS, 2 * HS)
+            mm([(pA, blk, hv(prod1, h)), (pA, nrs[t], hv(L0h, h)), (pB, nblk, hv(prod1, h)), (pB, blk, hv(prod2, h))], each=2)
+            tt(hv(pA2, h), pA, hv(m2n, h), ALU.mult)
+            tt(hv(pB2, h), pB, hv(m2n, h), ALU.mult)
+            dl = sub(bank, 192, 480)
+            a1, a2, b2 = hv(pA1, h), hv(pA2, h), hv(pB2, h)
+            mm([(hv(dl, 0), nI, a1), (hv(dl, 0), nI, a2), (hv(dl, 1), I, a1), (hv(dl, 1), nI, b2), (hv(dl, 2), I, a2), (hv(dl, 2), I, b2)], each=2)
+            Tl = new("f", 288)
+            tt(Tl, dl, ohs[h], ALU.mult)
+            pw = flagwrap(sub(P7, 256, 256 + HS), I3k, hv(m2n, h), hv(spare[1], h))
+            tw = new("f", 6)
+            tt(tw, pw, sub(hv(sh, h), 15, HS, 16), ALU.max)
+            ts(sub(offL[h], 12, 18), tw, B, ALU.add)
+            scatter(HL, offL[h], Tl, Lf[h])
+            tt(hv(tw2, h, 6), pw, sub(hv(s0, h), 15, HS, 16), ALU.max)
+            tt(hv(tw2, 2 + h, 6), pw, sub(hv(s1, h), 15, HS, 16), ALU.max)
+        ts(offW, tw2, BE, ALU.add)
+        e0c, x0c = new("f", 32), new("b", 32)
+        gather("a", e0c, e0b, sidx)
+        gather("a", x0c, x0w, sidx)
+        esc, _u = wrap(e0c, ME, None)
+        tc, offa = new("f", 2), new("u", 2)
+        tt(tc, esc, C4, ALU.min)
+        ts(offa, tc, BE, ALU.add)
+        x0m, dmm, h3m = sub(m1r, 0, 32), sub(m1r, 32, 64), sub(m1r, 64, 96)
+        _s, h3u = wrap(h3m, MH, B)
+        nv = 16 * XSPLIT
+        xb = BK[2]
+        mm([(xb, one1, zrow)] + [(sub(xb, j, 512, 16), nI, x0m) for j in range(16)], last=False)
+        key = sub(P4, 0, 128)
+        mm([(key, one1, part(q128, 0, 1))], last=False)
+        Lxu, Lxf = new("u", 32), new("f", 32)
+        gather("v", Lxu, HLg, h3u)
+        gather("a", Lxf, HLg, h3u)
+        if t == RO - 1:
+            dma("s", lambda E, A, T: E.dma_start(T.yl[:], A(HLg)), [HLg], [], 393216)
+        gather("v", sub(Ag, 0, nv), Xg, sub(Lxu, 0, XSPLIT))
+        gather("a", sub(Ag, nv, 512), Xg, sub(Lxu, XSPLIT, 32))
+        mm([(xb, I, sub(Ag, 0, 512))], first=False)
+        act(sub(Ab, 0, 512), xb, ACT.Abs)
+        mm([(sub(key, j, 128, 16, 0, 32), sub(Ab, j, 512, 16), G8) for j in range(16)] + [(key, one1, sub(zrow, 0, 128))], first=False)
+        prodx = new("h", 32)
+        oh, fp = pick(0, 32, Lxf, prodx)
+        ftri = sub(P7, 0, 64)
+        mm([(sub(ftri, 0, 32), blk, prodx), (sub(ftri, 0, 32), I, sub(TRI, 0, 32)),
+            (sub(ftri, 32, 64), blk, prodx), (sub(ftri, 32, 64), I, sub(TRI, 32, 64))], each=2)
+        fs, fu = wrap(fp, ME, BE)
+        gex, dif = new("b", 32), new("b", 32)
+        gtt(gex, Xg, fu, dmm, ALU.is_ge)
+        Eo, E1, E2 = new("b", 64), new("b", 64), new("b", 64)
+        for c in range(2):
+            ts(sub(Eo, 32 * c, 32 * c + 32), fp, sub(esc, 16 * c, 16 * c + 1), ALU.subtract, BE, ALU.is_equal)
+        pv, pg = sub(P5, 0, 32), sub(P6, 0, 32)
+        base = [(nblk, gex), (blk32, sub(Eo, 0, 32)), (blk32, sub(Eo, 32, 64))]
+        mm([(pv, l, r) for l, r in base])
+        mm([(pg, l, r) for l, r in base], last=False)
+        for c in range(2):
+            ts(sub(E1, 32 * c, 32 * c + 32), sub(ftri, 32 * c, 32 * c + 32), sub(fs, 16 * c, 16 * c + 1), ALU.subtract, BE, ALU.is_equal)
+        gtt(dif, Xg, fu, x0m, ALU.subtract)
+        vs, _u = wrap(pv, MH, None)
+        for c in range(2):
+            ts(sub(E2, 32 * c, 32 * c + 32), sub(E1, 32 * c, 32 * c + 32), sub(vs, 16 * c, 16 * c + 1), ALU.mult, nneedB, ALU.is_le)
+        mm([(pg, blk32, sub(E2, 0, 32)), (pg, blk32, sub(E2, 32, 64))], first=False)
+        grant = new("b", 32)
+        m2s, m2r = new("b", 32), new("b", 32)
+        ts(grant, pg, nneed, ALU.is_le)
+        tt(m2s, grant, dif, ALU.mult)
+        message(m2s, m2r, t, 1)
+        pw = flagwrap(sub(P7, 256, 288), nI3k, grant, sub(spare[2], 0, 32))
+        tb, offb = new("f", 2), new("u", 2)
+        tt(tb, pw, fs, ALU.max)
+        ts(offb, tb, BE, ALU.add)
+        scatter(X, offb, x0m)
+        scatter(W, sub(offW, 0, 12), hb2)
+        scatter(W, sub(offW, 12, 24), hb1)
+        if t == RO - 1:
+            dma("s", lambda E, A, T: E.dma_start(T.yw[:], T.af[0:128:16, W[1]:W[1] + NP]), [Wg], [], 65536)
+        else:
+            pc = sub(P5, 256, 256 + NS)
+            mm([(pc, o16, m1n), (pc, o16, m2n)])
+            cnt, ci, cj, bf_, nd = new("f", 1), new("i", 1), new("i", 1), new("f", 1), new("f", 3)
+            act(junk, pc, ACT.Copy, scale=-1.0, acc=cnt)
+            copy(ci, cnt)
+            ts(cj, ci, 1, ALU.bitwise_and)
+            copy(bf_, cj)
+            ts(sub(nd, 0, 1), bf_, 9.0, ALU.add)
+            ts(sub(nd, 1, 2), bf_, -1.0, ALU.mult, -9.0, ALU.add)
+            ts(sub(nd, 2, 3), bf_, -1.0, ALU.mult, -9.0 - B, ALU.add)
+            need, nneed, nneedB = sub(nd, 0, 1), sub(nd, 1, 2), sub(nd, 2, 3)
+        scatter(X, offa, x0c, m2r)
+    for k, eng in enumerate(("s", "a")):
+        dma(eng, lambda E, A, T, k=k: E.dma_start(T.yx[:, 1024 * k:1024 * k + 1024], A(sub(X, 1024 * k, 1024 * k + 1024))),
+            [sub(X, 1024 * k, 1024 * k + 1024)], [], 262144)
+    return ops, size
+
+
+def depend(ops):
+    log = {}
+    for n, op in enumerate(ops):
+        acc = []
+        for wr, vs in ((False, op["r"]), (True, op["w"])):
+            for v in vs:
+                if is_ps(v):
+                    for bk in range(v[1] // 512, (v[2] - 1) // 512 + 1):
+                        acc.append(((v[0], bk), 0, 1, wr, 1))
+                else:
+                    acc.append((v[0], v[1], v[2], wr, v[3]))
+        deps = set()
+        for key, lo, hi, wr, st in acc:
+            for (m, l2, h2, w2, s2) in log.get(key, []):
+                clash = wr or w2 or (key[0][0] == "p" and ops[m]["eng"] != op["eng"])
+                if l2 < hi and lo < h2 and clash and m != n and not (st == s2 and (lo - l2) % st):
+                    deps.add(m)
+        for key, lo, hi, wr, st in acc:
+            lst = log.setdefault(key, [])
+            if wr and st == 1:
+                lst[:] = [x for x in lst if not (lo <= x[1] and x[2] <= hi)]
+            lst.append((n, lo, hi, wr, st))
+        op["deps"] = sorted(deps)
+
+
+def schedule(ops, seed, jitter):
+    n = len(ops)
+    dur, occ, bus = [0] * n, [0] * n, 1900
+    for i, op in enumerate(ops):
+        if op["kind"] == "dma":
+            bus = (bus if not op["deps"] else 1900) + op["cost"] // 200
+            dur[i], occ[i] = bus, 60
+        else:
+            dur[i], occ[i] = op["cost"], 0 if op["eng"] == "x" else op["cost"]
+    pred = [[(d, 0 if op["eng"] == "t" and ops[d]["eng"] == "t" else HOP) for d in op["deps"]] for op in ops]
+    loads = [i for i, op in enumerate(ops) if op["eng"] == "s" and not op["deps"]]
+    for a, b in zip(loads, loads[1:]):
+        pred[b].append((a, occ[a] - dur[a]))
+    succ = [[] for _ in ops]
+    for i in range(n):
+        for d, h in pred[i]:
+            succ[d].append((i, h))
+
+    def place(rank, before, after, back):
+        left = [len(b) for b in before]
+        ready = sorted((rank[i], i) for i in range(n) if left[i] == 0)
+        busy = {e: [] for e in "vatgsx"}
+        start = [0] * n
+        while ready:
+            i = ready.pop(0)[1]
+            t = max([0] + [start[d] + dur[d] + h for d, h in before[i]])
+            lead = dur[i] - occ[i] if back else 0
+            if occ[i]:
+                lst, k = busy[ops[i]["eng"]], 0
+                for a, b in lst:
+                    if t + lead + occ[i] <= a:
+                        break
+                    t = max(t, b - lead)
+                    k += 1
+                lst.insert(k, (t + lead, t + lead + occ[i]))
+            start[i] = t
+            for s, h in after[i]:
+                left[s] -= 1
+                if left[s] == 0:
+                    ready.append((rank[s], s))
+                    ready.sort()
+        return start
+
+    def score(start):
+        return max(start[i] + dur[i] for i in range(n)) + sum(start) / (20.0 * n)
+
+    prio, r = [0] * n, [seed]
+
+    def rnd(m):
+        r[0] = (r[0] * 1103515245 + 12345) % 2147483648
+        return (r[0] >> 8) % m
+    for i in range(n - 1, -1, -1):
+        prio[i] = dur[i] + max([prio[s] + h for s, h in succ[i]] + [0])
+    start = place([-p for p in prio], pred, succ, False)
+    best = (score(start), start)
+    for it in range(PASSES):
+        if it % 50 < 2:
+            back = place([-(best[1][i] + dur[i]) for i in range(n)], succ, pred, True)
+            rank = [-(back[i] + dur[i]) + rnd(jitter + 1) for i in range(n)]
+        elif it % 3:
+            st = best[1]
+            ends = {(ops[i]["eng"], st[i] + occ[i]): i for i in range(n) if occ[i]}
+            i, held = max(range(n), key=lambda c: st[c] + dur[c]), []
+            while st[i] > 0:
+                tight = [d for d, h in pred[i] if st[d] + dur[d] + h == st[i]]
+                if tight:
+                    i = tight[rnd(len(tight))]
+                else:
+                    p = ends[ops[i]["eng"], st[i]]
+                    held.append((p, i))
+                    i = p
+            rank = list(st)
+            for _ in range(1 + rnd(2)):
+                p, i = held[rnd(len(held))]
+                if rnd(2):
+                    rank[p] = st[i] + 1 + rnd(600)
+                else:
+                    rank[i] = st[p] - 1 - rnd(600)
+        else:
+            mid, wide, amp = rnd(int(best[0])), 1000 + rnd(5000), 200 + rnd(2500)
+            rank = [b + (rnd(amp) if abs(b - mid) < wide and rnd(4) == 0 else 0) for b in best[1]]
+        start = place(rank, pred, succ, False)
+        if score(start) <= best[0]:
+            best = (score(start), start)
+    start = best[1]
+    order = sorted(range(n), key=lambda i: (start[i], i))
+    return order, start, [start[i] + dur[i] for i in range(n)]
+
+
+def signals(ops, order):
+    token, known, after, count, nd = {}, {e: {} for e in "vatgs"}, {}, {e: 0 for e in "vatg"}, 0
+    waits = {}
+    seq = {e: 0 for e in "vatg"}
+    for i in order:
+        op = ops[i]
+        if op["kind"] == "c":
+            seq[op["eng"]] += 1
+            token[i] = (op["eng"], seq[op["eng"]])
+        elif op["kind"] == "dma":
+            token[i] = ("d%d" % nd, 1)
+            nd += 1
+        elif op["kind"] == "recv":
+            token[i] = ("r%d%d" % op["extra"], 1)
+        else:
+            token[i] = ("l%d%d" % op["extra"][2:], 1)
+    used = set()
+    for i in order:
+        op = ops[i]
+        e = op["eng"]
+        if e == "x":
+            after[i] = {token[i][0]: 1}
+            continue
+        k = known[e]
+        ws = {}
+        for d in sorted(op["deps"], key=lambda d: -token[d][1]):
+            s, c = token[d]
+            if e == "t" and s == "t":
+                continue
+            if k.get(s, 0) < c:
+                ws[s] = max(ws.get(s, 0), c)
+                used.add(d)
+                for s2, c2 in after[d].items():
+                    if k.get(s2, 0) < c2:
+                        k[s2] = c2
+        waits[i] = ws
+        a = dict(k)
+        a[token[i][0]] = token[i][1]
+        after[i] = a
+    val = {}
+    for i in order:
+        if ops[i]["kind"] == "c" and i in used:
+            count[ops[i]["eng"]] += 1
+            val[token[i]] = count[ops[i]["eng"]]
+    return token, waits, used, val, nd
+
+
+OPS, SIZE = plan()
+depend(OPS)
+ORDER, START, FIN = schedule(OPS, SEED, JITTER)
+TOKEN, WAITS, USED, VAL, NDMA = signals(OPS, ORDER)
+
+SCRATCH = {ARENA[k][0]: ("sbuf", [128, SIZE[k]], ARENA[k][1]) for k in ARENA}
+SCRATCH["pa"] = ("psum", [128, 1024], "float32")
+SCRATCH["pb"] = ("psum", [128, 1024], "float32")
+for _k in (4, 5, 6, 7):
+    SCRATCH["p%d" % _k] = ("psum", [128, 512], "float32")
+SEMAPHORES = (["qv", "qa", "qt", "qg"] + ["d%d" % k for k in range(NDMA)]
+              + ["%s%d%d" % (a, t, k) for a in "rl" for t in range(RO) for k in range(2)])
+
+
+def rank_program(g, core, T, topo):
+    rank = T.rank_of(core)
+    if rank is None:
+        return
+    n = len(T.cores)
+    Q = {"v": g.vector, "a": g.scalar, "t": g.tensor, "g": g, "s": g.sync}
+
+    def A(v):
+        if v[3] == 1:
+            return T[v[0]][v[4]:v[5], v[1]:v[2]]
+        return T[v[0]][v[4]:v[5], v[1]:v[2]:v[3]]
+
+    def peer(t, k):
+        d = 1 + t % (n - 1)
+        return T.cores[(rank + d) % n] if k == 0 else T.cores[(rank - d) % n]
+
+    def amount(s, c):
+        if s in ("v", "a", "t", "g"):
+            return T.sem["q" + s], VAL[(s, c)]
+        if s[0] == "d":
+            return T.sem[s], 16
+        t, k = int(s[1]), int(s[2])
+        if s[0] == "r":
+            return T.sem[s], len(topo.engines(peer(t, 1 - k), core))
+        return T.sem[s], len(topo.engines(core, peer(t, k)))
+
+    waited = set()
+    for i in ORDER:
+        op = OPS[i]
+        if op["kind"] == "recv":
+            continue
+        E = Q[op["eng"]]
+        for s, c in WAITS[i].items():
+            sem, v = amount(s, c)
+            E.wait_ge(sem, v)
+            waited.add(s)
+        if op["kind"] == "c":
+            ins = op["fn"](E, A)
+            if i in USED:
+                ins.then_inc(T.sem["q" + op["eng"]], 1)
+        elif op["kind"] == "dma":
+            op["fn"](E, A, T).then_inc(T.sem[TOKEN[i][0]], 16)
+        else:
+            src, dst, t, k = op["extra"]
+            to = peer(t, k)
+            rid, pid = topo.addr(to, core)
+            g.remote_dma(A(dst), A(src), T.sem["r%d%d" % (t, k)], T.sem["l%d%d" % (t, k)], pid, rid, topo.mask(core, to))
+    for i in ORDER:
+        s = TOKEN[i][0]
+        if OPS[i]["kind"] != "c" and s not in waited:
+            sem, v = amount(s, 1)
+            g.sync.wait_ge(sem, v)

@@ -6,15 +6,16 @@ NP, NH, NS, RO, CAP = 2048, 768, 192, 2, 32
 HS = NS // 2
 B = 4096.0
 BE = 5184.0
-HOP = 110
+HOP = 240
 PE = 2.0
-FLY = 2000
+FLY = 3000
 SPLIT = {(1, 0): 48, (1, 1): 64, (2, 0): 64, (2, 1): 48}
 WIDE = {(1, 0): False, (1, 1): True, (2, 0): True, (2, 1): True}
+CASES = ((200, 3000, 1.25),)
 XSPLIT = 16
 PIECE = 32
 XEG = (16, 0)
-SEED, JITTER, PASSES = 1, 200, 3000
+SEED, JITTER, PASSES = 1, 200, 4600
 ARENA = {"f": ("af", "float32"), "b": ("ab", "bfloat16"), "h": ("ah", "float16"), "u": ("au", "uint16"), "i": ("ai", "int32")}
 
 
@@ -99,20 +100,20 @@ def plan():
             fn = lambda E, A: E.activation(A(o), A(win).indirect(A(off)), ACT.Copy)
         else:
             fn = lambda E, A: E.activation(A(o), A(win).indirect(A(off)), f, bias=bias)
-        add(eng, fn, [win, off], [o], gcost(width(o)))
+        add(eng, fn, [win, off], [o], gcost(width(o)), extra="index")
 
     def gtt(o, win, off, b, op):
-        add("v", lambda E, A: E.tensor_tensor(A(o), A(win).indirect(A(off)), A(b), op), [win, off, b], [o], gcost(width(o)))
+        add("v", lambda E, A: E.tensor_tensor(A(o), A(win).indirect(A(off)), A(b), op), [win, off, b], [o], gcost(width(o)), extra="index")
 
     def scatter(win, off, i, b=None):
         if b is None:
             fn = lambda E, A: E.tensor_copy(A(win).indirect(A(off)), A(i))
         else:
             fn = lambda E, A: E.tensor_tensor(A(win).indirect(A(off)), A(i), A(b), ALU.add)
-        add("v", fn, [off, i, b], [win], 60 + int(3.8 * width(i)))
+        add("v", fn, [off, i, b], [win], 60 + int(3.8 * width(i)), extra="index")
 
     def mark(win, off, i):
-        add("a", lambda E, A: E.activation(A(win).indirect(A(off)), A(i), ACT.Tanh), [off, i], [win], 80 + int(3.8 * width(i)))
+        add("a", lambda E, A: E.activation(A(win).indirect(A(off)), A(i), ACT.Tanh), [off, i], [win], 80 + int(3.8 * width(i)), extra="index")
 
     def mm(items, first=True, last=True, each=0):
         def fn(E, A):
@@ -141,8 +142,8 @@ def plan():
         add(eng, fn, r, w, nbytes, kind="dma")
 
     def message(src, dst, t, k):
-        tok = ("msg", 2 * t + k, 2 * t + k + 1, 1, 0, 128)
-        add("g", None, [src], [tok], 500, kind="send", extra=(src, dst, t, k))
+        tok = ("msg", 3 * t + k, 3 * t + k + 1, 1, 0, 128)
+        add("g", None, [src], [tok], 3000 if k == 2 else 500, kind="send", extra=(src, dst, t, k))
         add("x", None, [tok], [dst], FLY, kind="recv", extra=(t, k))
 
     PD = [("pa", 0, 1024, 1, 0, 128), ("pb", 0, 1024, 1, 0, 128)]
@@ -155,11 +156,18 @@ def plan():
     Xg, HLg, Wg, Vg = sub(X, 0, NP), sub(HL, 0, NH), sub(W, 0, NP), sub(V, 0, NH)
     dma("s", lambda E, A, T: E.dma_start(A(wr32), T.wr[:]), [], [wr32], 65536)
     dma("a", lambda E, A, T: E.dma_start(A(ho32), T.ho[:]), [], [ho32], 12288)
+
+    def load_dm(t):
+        dma("s" if t else "a", lambda E, A, T: E.dma_start(A(sub(DM, 208 * t, 208 * t + NS)), T.dm[:, NS * t:NS * (t + 1)]), [],
+            [sub(DM, 208 * t, 208 * t + NS)], 49152)
+    load_dm(0)
     dma("s", lambda E, A, T: E.dma_start(A(hl32), T.hl[:]), [], [hl32], 393216)
     dma("s", lambda E, A, T: E.dma_start(A(Xg), T.xs[:]), [], [Xg], 524288)
-    for t in range(RO):
-        dma("s", lambda E, A, T, t=t: E.dma_start(A(sub(DM, 208 * t, 208 * t + NS)), T.dm[:, NS * t:NS * (t + 1)]), [],
-            [sub(DM, 208 * t, 208 * t + NS)], 49152)
+    load_dm(1)
+    DR = new("b", 208)
+    message(sub(DM, 0, NS), sub(DR, 0, NS), 0, 2)
+    memset(sub(DR, NS, 208), 512.0)
+    snum = new("b", 208)
 
     ones = new("b", 512)
     memset(ones, 1.0)
@@ -207,7 +215,8 @@ def plan():
         mm([(BK[q], sub(selW, 128 * q, 128 * q + 128), wr16)])
         act(sub(W, 512 * q, 512 * q + 512), BK[q], ACT.Copy)
     copy(HLg, hl32)
-    fill(sub(V, 0, 480), 0)
+    act(sub(V, 0, 480), sub(ones, 0, 480), ACT.Tanh, scale=0.0)
+    ops[-1]["cost"] += 1600
     fill(sub(V, 480, 960), 0)
     fill(sub(HL, NH, 1152), 0)
     fill(sub(W, NP, NP + NS), 0)
@@ -245,8 +254,8 @@ def plan():
     ts(xoff, sub(c16, 0, 8), 15.0, ALU.add)
     sw = new("b", 12)
     ts(sw, sub(c16, 0, 12), pm, ALU.add)
-    srow = part(new("f", NS), 0, 1)
-    iota(srow, [[1, NS]], 0, 0)
+    iota(snum, [[1, 208]], 0, 0)
+    srow = part(sub(snum, 0, NS), 0, 1)
     spare = [part(new("h", NS), 0, 1) for n in range(3)]
     for n, c in enumerate((768.0 - 2048.0, 960.0, 992.0)):
         ts(spare[n], srow, c, ALU.add)
@@ -262,7 +271,7 @@ def plan():
     need, nneed, nneedB = 9.0, -9.0, -9.0 - B
     Ag, Ab, XE = new("b", 3072), new("b", 3072), new("b", 3072)
     Ebuf = new("b", 1248)
-    junk = new("b", NS)
+    junk = new("b", 2 * NS)
 
     def wrap(src, M, off, s=None, u=None):
         n = width(src)
@@ -442,10 +451,10 @@ def plan():
             scan(hv(pos, h), hv(failed, h), hv(failed, h), sub(pos, HS - 1, HS) if h else 0.0, ALU.add, ALU.max)
             if h:
                 for c in range(2):
-                    act(junk, pos, ACT.Sign, bias=sub(kcol, c, c + 1), scale=-1.0, acc=sub(acc, c, c + 1))
+                    act(hv(junk, c, NS), pos, ACT.Sign, bias=sub(kcol, c, c + 1), scale=-1.0, acc=sub(acc, c, c + 1))
                 ts(sidx, acc, 0.5, ALU.mult, 96.0, ALU.add)
                 gather("v", sub(m1s, 0, 32), x0w, sidx)
-                gather("v", sub(m1s, 32, 64), sub(DM, 208 * t, 208 * t + 208), sidx)
+                gather("v", sub(m1s, 32, 64), sub(DM, 208 * t, 208 * t + 208) if t else snum, sidx)
                 gather("v", sub(m1s, 64, 96), h3w, sidx)
                 message(m1s, m1r, t, 0)
             ts(hv(m2n, h), cn, need, ALU.is_ge, -1.0, ALU.mult)
@@ -476,6 +485,10 @@ def plan():
         ts(offa, tc, BE, ALU.add)
         x0m, dmm, h3m = sub(m1r, 0, 32), sub(m1r, 32, 64), sub(m1r, 64, 96)
         _s, h3u = wrap(h3m, MH, B)
+        if t == 0:
+            _s, su = wrap(dmm, MH, B)
+            dmm = new("b", 32)
+            gather("a", dmm, DR, su)
         nv = 16 * XSPLIT
         xb = BK[2]
         mm([(xb, one1, zrow)] + [(sub(xb, j, 512, 16), nI, x0m) for j in range(16)], last=False)
@@ -531,7 +544,7 @@ def plan():
             pc = sub(P5, 256, 256 + NS)
             mm([(pc, o16, m1n), (pc, o16, m2n)])
             cnt, ci, cj, bf_, nd = new("f", 1), new("i", 1), new("i", 1), new("f", 1), new("f", 3)
-            act(junk, pc, ACT.Copy, scale=-1.0, acc=cnt)
+            act(hv(junk, 0, NS), pc, ACT.Copy, scale=-1.0, acc=cnt)
             copy(ci, cnt)
             ts(cj, ci, 1, ALU.bitwise_and)
             copy(bf_, cj)
@@ -541,8 +554,7 @@ def plan():
             need, nneed, nneedB = sub(nd, 0, 1), sub(nd, 1, 2), sub(nd, 2, 3)
         scatter(X, offa, x0c, m2r)
     for k, eng in enumerate(("s", "a")):
-        dma(eng, lambda E, A, T, k=k: E.dma_start(T.yx[:, 1024 * k:1024 * k + 1024], A(sub(X, 1024 * k, 1024 * k + 1024))),
-            [sub(X, 1024 * k, 1024 * k + 1024)], [], 262144)
+        dma(eng, lambda E, A, T, k=k: E.dma_start(T.yx[64 * k:64 * k + 64, :], A(part(Xg, 64 * k, 64 * k + 64))), [Xg], [], 262144)
     return ops, size
 
 
@@ -614,8 +626,21 @@ def schedule(ops, seed, jitter):
                     ready.sort()
         return start
 
-    def score(start):
-        return max(start[i] + dur[i] for i in range(n)) + sum(start) / (20.0 * n)
+    def replay(order, hop, fly, slow):
+        fin, free = [0] * n, {e: 0 for e in "vatgsx"}
+        for i in order:
+            e = ops[i]["eng"]
+            t = max([free[e]] + [fin[d] + (hop if h == HOP else h) for d, h in pred[i]])
+            fin[i] = t + (fly if e == "x" else dur[i] * slow if ops[i]["extra"] == "index" else dur[i])
+            free[e] = fin[i] if occ[i] == dur[i] else t + occ[i]
+        return max(fin)
+
+    def score(start, bound=None):
+        span = max(start[i] + dur[i] for i in range(n))
+        if bound is not None and span > bound + 900:
+            return None
+        order = sorted(range(n), key=lambda i: (start[i], i))
+        return (span + sum(replay(order, *c) for c in CASES)) / (1.0 + len(CASES)) + sum(start) / (20.0 * n), span
 
     prio, r = [0] * n, [seed]
 
@@ -650,11 +675,12 @@ def schedule(ops, seed, jitter):
                 else:
                     rank[i] = st[p] - 1 - rnd(600)
         else:
-            mid, wide, amp = rnd(int(best[0])), 1000 + rnd(5000), 200 + rnd(2500)
+            mid, wide, amp = rnd(int(best[0][1])), 1000 + rnd(5000), 200 + rnd(2500)
             rank = [b + (rnd(amp) if abs(b - mid) < wide and rnd(4) == 0 else 0) for b in best[1]]
         start = place(rank, pred, succ, False)
-        if score(start) <= best[0]:
-            best = (score(start), start)
+        sc = score(start, best[0][1])
+        if sc is not None and sc[0] <= best[0][0]:
+            best = (sc, start)
     start = best[1]
     order = sorted(range(n), key=lambda i: (start[i], i))
     return order, start, [start[i] + dur[i] for i in range(n)]
@@ -718,7 +744,7 @@ SCRATCH["pb"] = ("psum", [128, 1024], "float32")
 for _k in (4, 5, 6, 7):
     SCRATCH["p%d" % _k] = ("psum", [128, 512], "float32")
 SEMAPHORES = (["qv", "qa", "qt", "qg"] + ["d%d" % k for k in range(NDMA)]
-              + ["%s%d%d" % (a, t, k) for a in "rl" for t in range(RO) for k in range(2)])
+              + ["%s%d%d" % (a, t, k) for a in "rl" for t, k in ((0, 0), (0, 1), (0, 2), (1, 0), (1, 1))])
 
 
 def rank_program(g, core, T, topo):
@@ -735,7 +761,7 @@ def rank_program(g, core, T, topo):
 
     def peer(t, k):
         d = 1 + t % (n - 1)
-        return T.cores[(rank + d) % n] if k == 0 else T.cores[(rank - d) % n]
+        return T.cores[(rank + d) % n] if k != 1 else T.cores[(rank - d) % n]
 
     def amount(s, c):
         if s in ("v", "a", "t", "g"):
@@ -744,7 +770,7 @@ def rank_program(g, core, T, topo):
             return T.sem[s], 16
         t, k = int(s[1]), int(s[2])
         if s[0] == "r":
-            return T.sem[s], len(topo.engines(peer(t, 1 - k), core))
+            return T.sem[s], len(topo.engines(peer(t, 0 if k == 1 else 1), core))
         return T.sem[s], len(topo.engines(core, peer(t, k)))
 
     waited = set()

@@ -3,20 +3,20 @@ from concourse.mybir import AluOpType, AxisListType, ActivationFunctionType
 ALU = AluOpType
 ACT = ActivationFunctionType
 NP, NH, NS, RO, CAP = 2048, 768, 192, 2, 32
-HS = NS // 2
 B = 4096.0
 BE = 5184.0
 HOP = 240
 PE = 2.0
 FLY = 3000
-SPLIT = {(1, 0): 48, (1, 1): 64, (2, 0): 64, (2, 1): 48}
-WIDE = {(1, 0): False, (1, 1): True, (2, 0): True, (2, 1): True}
+PARTS = ((0, 64), (64, 128), (128, 192))
+PIECES = {(1, 0): "w32 a32", (1, 1): "v40 a24", (1, 2): "v40 a24", (2, 0): "v40 a24", (2, 1): "v40 a24", (2, 2): "v32 a32"}
+FOLD = (("g", 0, 40), ("v", 64, 168))
 CASES = ((200, 3000, 1.25),)
+PAY = ((0, 128), (128, 192))
 XSPLIT = 16
-PIECE = 32
-XEG = (16, 0)
-SEED, JITTER, PASSES = 1, 200, 4600
+SEED, JITTER, PASSES = 1, 200, 3200
 ARENA = {"f": ("af", "float32"), "b": ("ab", "bfloat16"), "h": ("ah", "float16"), "u": ("au", "uint16"), "i": ("ai", "int32")}
+BACK = (4, 5)
 
 
 def sub(v, a, b, step=1, p0=None, p1=None):
@@ -27,8 +27,12 @@ def part(v, p0, p1):
     return (v[0], v[1], v[2], v[3], p0, p1)
 
 
+def grid(name, row, a, b, step, c0, c1):
+    return (name, row * a, row * b, 0, 0, 128, (slice(a, b, step), slice(c0, c1)), (b - a + step - 1) // step * (c1 - c0))
+
+
 def width(v):
-    return (v[2] - v[1] + v[3] - 1) // v[3]
+    return v[7] if len(v) > 6 else (v[2] - v[1] + v[3] - 1) // v[3]
 
 
 def is_ps(v):
@@ -45,7 +49,7 @@ def plan():
         return (ARENA[k][0], lo, lo + n, 1, 0, 128)
 
     def two(*vs):
-        return all(v[0] in ("ab", "ah", "au") for v in vs)
+        return all(v[0] in ("ab", "ah", "au", "ab3", "tt3") for v in vs)
 
     def add(eng, fn, r, w, cost, kind="c", extra=None):
         r = [v for v in r if isinstance(v, tuple)]
@@ -141,33 +145,39 @@ def plan():
     def dma(eng, fn, r, w, nbytes):
         add(eng, fn, r, w, nbytes, kind="dma")
 
-    def message(src, dst, t, k):
-        tok = ("msg", 3 * t + k, 3 * t + k + 1, 1, 0, 128)
-        add("g", None, [src], [tok], 3000 if k == 2 else 500, kind="send", extra=(src, dst, t, k))
-        add("x", None, [tok], [dst], FLY, kind="recv", extra=(t, k))
+    sent = []
 
-    PD = [("pa", 0, 1024, 1, 0, 128), ("pb", 0, 1024, 1, 0, 128)]
-    BK = [sub(PD[q // 2], 512 * (q % 2), 512 * (q % 2) + 512) for q in range(4)]
-    P4, P5, P6, P7 = [("p%d" % k, 0, 512, 1, 0, 128) for k in (4, 5, 6, 7)]
+    def message(src, dst, t, k):
+        tok = ("msg", len(sent), len(sent) + 1, 1, 0, 128)
+        add("g", None, [src, ("msg", 0, 1, 1, 0, 128) if len(sent) == 1 else None], [tok], 500 if sent else 3000, kind="send",
+            extra=(src, dst, t, k))
+        add("x", None, [tok], [dst], FLY + 2 * width(src), kind="recv", extra=(t, k))
+        sent.append((t, k))
+
+    BK = [("p%d" % k, 0, 512, 1, 0, 128) for k in range(3)]
+    KB = [("p%d" % k, 0, 512, 1, 0, 128) for k in (3, 4)]
+    M0, M1 = [("p%d" % k, 0, 512, 1, 0, 128) for k in (5, 6)]
+    turn = {"s": 0, "k": 0}
 
     ho32, wr32, hl32 = new("i", 24), part(new("i", 512), 0, 32), new("i", NH)
-    X, DM = new("b", NP + 64), new("b", 416)
-    HL, W, V = new("f", 1152), new("f", NP + NS), new("f", NH + NS)
+    X = new("b", NP + 64)
+    PRE, PRR = [new("b", 416) for t in range(RO)], [new("b", 416) for t in range(RO)]
+    HL, W, V, FT = new("f", 1152), new("f", NP + NS), new("f", NH + NS), new("f", NP + 64)
     Xg, HLg, Wg, Vg = sub(X, 0, NP), sub(HL, 0, NH), sub(W, 0, NP), sub(V, 0, NH)
     dma("s", lambda E, A, T: E.dma_start(A(wr32), T.wr[:]), [], [wr32], 65536)
     dma("a", lambda E, A, T: E.dma_start(A(ho32), T.ho[:]), [], [ho32], 12288)
 
     def load_dm(t):
-        dma("s" if t else "a", lambda E, A, T: E.dma_start(A(sub(DM, 208 * t, 208 * t + NS)), T.dm[:, NS * t:NS * (t + 1)]), [],
-            [sub(DM, 208 * t, 208 * t + NS)], 49152)
+        o = sub(PRE[t], 208, 208 + NS)
+        dma("s" if t else "a", lambda E, A, T: E.dma_start(A(o), T.dm[:, NS * t:NS * (t + 1)]), [], [o], 49152)
     load_dm(0)
     dma("s", lambda E, A, T: E.dma_start(A(hl32), T.hl[:]), [], [hl32], 393216)
     dma("s", lambda E, A, T: E.dma_start(A(Xg), T.xs[:]), [], [Xg], 524288)
     load_dm(1)
-    DR = new("b", 208)
-    message(sub(DM, 0, NS), sub(DR, 0, NS), 0, 2)
-    memset(sub(DR, NS, 208), 512.0)
-    snum = new("b", 208)
+    for t in range(RO):
+        memset(sub(PRE[t], 400, 416), 512.0)
+        memset(sub(PRE[t], NS, 208), 0.0)
+    message(sub(PRE[0], 208, 416), sub(PRR[0], 208, 416), 0, 0)
 
     ones = new("b", 512)
     memset(ones, 1.0)
@@ -211,9 +221,9 @@ def plan():
     ts(sub(ME, 15, NS, 16), sub(ME, 15, NS, 16), -B - BE, ALU.add)
     wr16 = part(new("h", 512), 0, 32)
     copy(wr16, wr32)
-    for q in range(4):
-        mm([(BK[q], sub(selW, 128 * q, 128 * q + 128), wr16)])
-        act(sub(W, 512 * q, 512 * q + 512), BK[q], ACT.Copy)
+    for q, bank in enumerate(BK + KB[:1]):
+        mm([(bank, sub(selW, 128 * q, 128 * q + 128), wr16)])
+        act(sub(W, 512 * q, 512 * q + 512), bank, ACT.Copy)
     copy(HLg, hl32)
     act(sub(V, 0, 480), sub(ones, 0, 480), ACT.Tanh, scale=0.0)
     ops[-1]["cost"] += 1600
@@ -221,17 +231,14 @@ def plan():
     fill(sub(HL, NH, 1152), 0)
     fill(sub(W, NP, NP + NS), 0)
     memset(sub(X, NP, NP + 64), 0.0)
-    for t in range(RO):
-        memset(sub(DM, 208 * t + NS, 208 * t + 208), 512.0)
     tin = [new("f", NS) for t in range(RO)]
     fill(tin[0], 1)
     fill(tin[1], 4)
-    nI, I32, nI32, bigI = scaled(I, -1.0), scaled(I, 32.0), scaled(I, -32.0), new("b", 128)
-    I2k, I3k, nI3k = scaled(I, 2048.0), scaled(I, 3072.0), scaled(I, -3072.0)
+    nI, bigI = scaled(I, -1.0), new("b", 128)
+    I2k, nI2k, I3k = scaled(I, 2048.0), scaled(I, -2048.0), scaled(I, 3072.0)
     ts(bigI, I, 2.0 ** 60, ALU.mult, 2.0 ** 60, ALU.mult)
-    nblk, blk32 = scaled(blk, -1.0), scaled(blk, 32.0)
+    nblk = scaled(blk, -1.0)
     nrs = [scaled(rs[t], -1.0) for t in range(RO)]
-    G8 = scaled(sub(blk, 0, 128, 16), 16.0)
     o16 = new("b", 128)
     memset(o16, 0.0625)
     rm = new("f", 16)
@@ -245,31 +252,69 @@ def plan():
     add("v", lambda E, A: E.tensor_reduce(A(w0), A(w16), AxisListType.X, ALU.add), [w16], [w0], 64)
     ts(w0, w0, 2.0 ** -66, ALU.mult)
     ts(wcol, sub(wb, 0, NS, 16), 2.0 ** -30, ALU.mult, w0, ALU.mult)
-    WC = new("b", 12 * 128)
-    for c in range(12):
-        act(sub(WC, 128 * c, 128 * c + 128), blk, ACT.Copy, scale=sub(wcol, c, c + 1))
-    RK = new("b", 128)
-    ts(RK, q128, 0.0, ALU.is_equal, 131072.0, ALU.mult)
-    xoff = new("u", 8)
-    ts(xoff, sub(c16, 0, 8), 15.0, ALU.add)
     sw = new("b", 12)
     ts(sw, sub(c16, 0, 12), pm, ALU.add)
-    iota(snum, [[1, 208]], 0, 0)
-    srow = part(sub(snum, 0, NS), 0, 1)
-    spare = [part(new("h", NS), 0, 1) for n in range(3)]
-    for n, c in enumerate((768.0 - 2048.0, 960.0, 992.0)):
+    srow = part(new("b", NS), 0, 1)
+    iota(srow, [[1, NS]], 0, 0)
+    spare = [part(new("h", NS), 0, 1) for n in range(2)]
+    for n, c in enumerate((768.0 - 2048.0, 960.0)):
         ts(spare[n], srow, c, ALU.add)
     zrow = part(new("b", 512), 0, 1)
     memset(zrow, 0.0)
-    C4, kcol, TRI = new("f", 2), new("f", 2), new("b", 64)
-    ts(C4, sub(sw, 0, 2), 2048.0 - BE, ALU.add)
-    ts(kcol, sub(sw, 0, 2), 0.5, ALU.add)
-    for c in range(2):
-        ts(sub(TRI, 32 * c, 32 * c + 32), kb, sub(sw, c, c + 1), ALU.is_le, B, ALU.mult)
-    EQ, SM, KS = [[new(k, 128) for h in range(2)] for k in "bff"]
     one1 = part(o128, 0, 1)
-    need, nneed, nneedB = 9.0, -9.0, -9.0 - B
-    Ag, Ab, XE = new("b", 3072), new("b", 3072), new("b", 3072)
+    Z = new("b", 143)
+    memset(Z, 0.0)
+    act(sub(Z, 15, 143, 16), sub(blk, 0, 128, 16), ACT.Copy, scale=16.0)
+    odi, odd, evn = new("i", 1), new("f", 2), new("f", 2)
+    ts(odi, pid, 4, ALU.arith_shift_right, 1, ALU.bitwise_and)
+    copy(sub(odd, 0, 1), odi)
+    ts(sub(odd, 1, 2), sub(odd, 0, 1), -1.0, ALU.mult)
+    ts(sub(evn, 0, 1), sub(odd, 0, 1), -1.0, ALU.mult, 1.0, ALU.add)
+    ts(sub(evn, 1, 2), sub(odd, 0, 1), -1.0, ALU.add)
+    IS = new("b", 640)
+    memset(IS, 0.0)
+    for n in range(4):
+        act(sub(IS, 160 * n + 16, 160 * n + 144), I, ACT.Copy, scale=sub((evn, odd)[n // 2], n % 2, n % 2 + 1))
+    p32i, p32, sq, R = new("i", 1), new("f", 1), new("b", 512), new("b", 512)
+    ts(p32i, pid, 31, ALU.bitwise_and)
+    copy(p32, p32i)
+    iota(sq, [[1, 32], [0, 16]], 0, 0)
+    ts(R, sq, p32, ALU.is_equal, -1.0, ALU.mult)
+    top = 17 * max(b - a for a, b in PARTS) // 16
+    RK, DJ = new("b", top), new("b", 204)
+    memset(RK, -1.0)
+    memset(sub(RK, 0, top, 17), 131072.0)
+    memset(DJ, -1.0)
+    memset(sub(DJ, 16, 204, 17), 15.0)
+    drow = [part(new("b", top), 0, 1) for n in range(2)]
+    for n, c in enumerate((-BE, B)):
+        memset(drow[n], 0.0)
+        memset(sub(drow[n], 16, top, 17), c)
+    memset(grid("ab3", 17, 0, NS, 1, 16, 17), 255.0)
+    iota(FT, [[1, NP + 64]], 0, 0)
+    C4, SP, kcol, TRI, tri, D0, d0 = new("f", 2), new("f", 2), new("f", 2), new("b", 66), new("b", 66), new("b", 66), new("b", 66)
+    ts(C4, sub(sw, 0, 2), 2048.0 - BE, ALU.add)
+    ts(SP, sub(sw, 0, 2), 2048.0, ALU.add)
+    ts(kcol, sub(sw, 0, 2), 0.5, ALU.add)
+    memset(tri, 128.0)
+    memset(d0, 4095.0)
+    for c in range(2):
+        ts(sub(tri, 33 * c, 33 * c + 32), kb, sub(sw, c, c + 1), ALU.is_gt, 128.0, ALU.mult)
+        ts(sub(d0, 33 * c, 33 * c + 32), kb, sub(sw, c, c + 1), ALU.is_equal, -2.0, ALU.mult)
+    ts(TRI, tri, 64.0, ALU.add)
+    ts(D0, d0, 1.0, ALU.add)
+    memset(sub(D0, 32, 66, 33), B)
+    memset(sub(D0, 0, 66, 33), 0.0)
+    gex, TE, own = new("b", 33), new("b", 66), new("f", 32)
+    memset(sub(gex, 32, 33), 0.0)
+    memset(sub(TE, 32, 66, 33), 0.0)
+    memset(own, 4000.0)
+    NFH, DH, UH = new("b", 416), new("h", 193), new("h", 416)
+    memset(sub(NFH, 0, 416, 208), 0.0)
+    memset(sub(NFH, 192, 416, 208), 1.0)
+    memset(sub(DH, 0, 1), 0.0)
+    need, room = 9.0, 55.0
+    Ag, XE = new("b", 3072), new("b", 3072)
     Ebuf = new("b", 1248)
     junk = new("b", 2 * NS)
 
@@ -291,13 +336,14 @@ def plan():
         return wrap(o, MH, None)[0]
 
     def dedupe(hb, hcols, vb, dead):
-        Sp = sub(P7, 0, NS)
-        items, pos = [], 0
+        Sp = sub(M1, 0, NS)
+        items, pos, hc = [], 0, new("f", 12)
+        ts(hc, hcols, B, ALU.add)
         for c in range(12):
             e = sub(Ebuf, pos, pos + NS - 16 * c)
             pos += NS - 16 * c
-            ts(e, sub(hb, 16 * c, NS), hcols(c), ALU.subtract, B, ALU.is_equal)
-            items.append((sub(Sp, 16 * c, NS), sub(WC, 128 * c, 128 * c + 128), e))
+            ts(e, sub(hb, 16 * c, NS), sub(hc, c, c + 1), ALU.is_equal, sub(wcol, c, c + 1), ALU.mult)
+            items.append((sub(Sp, 16 * c, NS), blk, e))
         items.append((Sp, bigI, vb))
         if dead is not None:
             items.append((Sp, bigI, dead))
@@ -306,256 +352,273 @@ def plan():
         tt(ns, Sp, thr, ALU.is_ge)
         return ns
 
-    def hv(v, h, n=HS):
-        return sub(v, n * h, n * h + n)
+    def steps(Lh, r0, row):
+        n = width(Lh) // 32
+        t3 = grid("tt3", 16, r0, r0 + 2 * n, 1, 0, 16)
+        add("v", lambda E, A: E.transpose(A(t3), A(Lh)), [Lh], [t3], vcost(32 * n, True))
+        whole = grid("pd", 34, 0, n, 1, 0, 34)
+        items = [(whole, one1, sub(row, 0, 34 * n))]
+        for a in range(2):
+            for b in range(2):
+                for s in range(2):
+                    lo = 160 * (2 * a + s) + 16 * (1 + a - b)
+                    items.append((grid("pd", 34, 0, n, 1, 17 * a + 1 - s, 17 * a + 17 - s), sub(IS, lo, lo + 128),
+                                  grid("tt3", 16, r0 + b, r0 + 2 * n, 2, 0, 16)))
+        mm(items + [(whole, one1, sub(zrow, 0, 34 * n))])
+        d = new("f", 34 * n)
+        act(d, whole, ACT.Copy)
+        return d
 
-    def distances(h, Lu, x0, step):
-        key, k = sub((P4, P5)[h], 0, 128), SPLIT[step, h]
-        ag, ab, xe = hv(Ag, h, 1536), hv(Ab, h, 1536), hv(XE, h, 1536)
-        mm([(key, one1, part(q128, 0, 1))], last=False)
-        close = [(key, one1, sub(zrow, 0, 128))]
-        if not WIDE[step, h]:
-            for eng, a, b in (("v", 0, k), ("a", k, HS)):
-                gather(eng, sub(ag, 16 * a, 16 * b), Xg, sub(Lu, HS * h + a, HS * h + b))
-            for q in range(4):
-                items = []
-                for j in range(4):
-                    o = sub(BK[q], HS * j, HS * j + HS)
-                    items += [(o, nI, hv(x0, h)), (o, I, sub(ag, 4 * q + j, 1536, 16))]
-                mm(items, each=2)
-                act(sub(ab, 384 * q, 384 * q + 384), sub(BK[q], 0, 384), ACT.Abs)
-                items = [(sub(key, 4 * q + j, 128, 16, 0, HS), sub(ab, 384 * q + HS * j, 384 * q + HS * j + HS), G8) for j in range(4)]
-                mm(items + (close if q == 3 else []), first=False, last=(q == 3))
-            return
-        cuts = [("v", a, min(a + PIECE, k)) for a in range(0, k, PIECE)] + [("a", a, min(a + 32, HS)) for a in range(k, HS, 32)]
-        q = 2 * h
-        for eng, a, b in cuts:
-            lu, src = sub(Lu, HS * h + a, HS * h + b), sub(ag, 16 * a, 16 * b)
-            if eng == "v":
-                gtt(src, Xg, lu, sub(xe, 16 * a, 16 * b), ALU.subtract)
-            else:
-                gather("a", src, Xg, lu)
-                o = sub(BK[q % 4], 0, 16 * (b - a))
-                q += 1
-                mm([(o, nI, sub(xe, 16 * a, 16 * b)), (o, I, src)])
-                src = o
-            act(sub(ab, 16 * a, 16 * b), src, ACT.Abs)
-        mm([(sub(key, j, 128, 16, 0, HS), sub(ab, j, 1536, 16), G8) for j in range(16)] + close, first=False)
+    def pick(a, b, d, nf, u, eu, off):
+        n = 17 * (b - a) // 16
+        key, sm = sub(KB[turn["k"] % 2], 0, n), new("f", n)
+        turn["k"] += 1
+        mm([(key, sub(Z, 15 - p, 143 - p), grid("ab3", 17, a + p, b, 16, 0, 17)) for p in range(16)])
+        scan(sm, sub(RK, 0, n), key, 0.0, ALU.add, ALU.min)
+        tt(nf, key, sm, ALU.not_equal)
+        scan(u, d, nf, 0.0, ALU.add, ALU.mult)
+        ts(eu, sub(u, 16, n, 17), off, ALU.add)
 
-    def pick(h, n, Lf, prod):
-        bank = (P4, P5)[h]
-        key, oh, ep = sub(bank, 0, 128), sub(bank, 128, 128 + n), sub(bank, 256, 256 + n)
-        copy(KS[h], key)
-        scan(SM[h], RK, key, 0.0, ALU.add, ALU.min)
-        gtt(EQ[h], SM[h], xoff, KS[h], ALU.is_equal)
-        mm([(oh, part(EQ[h], 0, n), sub(I, 0, n, 1, 0, n))])
-        tt(prod, oh, Lf, ALU.mult)
-        mm([(ep, blk, prod)])
-        return oh, ep
+    def distances(step, h, Lu, x0T):
+        a = a0 = PARTS[h][0]
+        for word in PIECES[step, h].split():
+            end = a + int(word[1:])
+            while a < end:
+                b = min(end, (a - a0) // 32 * 32 + 32 + a0)
+                lu, src = sub(Lu, a, b), sub(Ag, 16 * a, 16 * b)
+                if word[0] == "v":
+                    gtt(src, Xg, lu, sub(XE, 16 * a, 16 * b), ALU.subtract)
+                else:
+                    q = (a - a0) // 32 * 32
+                    o = sub(BK[turn["s"] % 3], 0, 16 * (b - a))
+                    turn["s"] += 1
+                    mm([(o, part(x0T[h], q, q + 32), sub(R, 16 * (a - a0 - q), 16 * (b - a0 - q), 1, q, q + 32))], last=False)
+                    gather("a" if word[0] == "a" else "v", src, Xg, lu)
+                    mm([(o, I, src)], first=False)
+                    src = o
+                act(grid("ab3", 17, a, b, 1, 0, 16), src, ACT.Abs)
+                a = b
+
+    def slots(nf):
+        n = width(nf)
+        uj, ju = new("b", n), new("u", n // 17)
+        scan(uj, sub(DJ, 0, n), nf, 0.0, ALU.add, ALU.mult)
+        copy(ju, sub(uj, 16, n, 17))
+        return ju
+
+    def w16_(v, a, b, n=16):
+        return sub(v, a * n // 16, b * n // 16)
 
     for t in range(RO):
         h0 = sub(ho16, 12 * t, 12 * t + 12)
-        dm = sub(DM, 208 * t, 208 * t + NS)
+        x0, dm = sub(PRE[t], 0, NS), sub(PRE[t], 208, 208 + NS)
         vbias = (-0.1, -0.9)[t]
-        Lf, ohs, offL = [new("f", 288) for h in range(2)], [new("b", 288) for h in range(2)], [new("u", 18) for h in range(2)]
-        for h in range(2):
-            ts(hv(ohs[h], 0), sub(ones, 0, HS), sub(rm, t, t + 1), ALU.mult)
-            copy(sub(offL[h], 0, 6), sub(ho32, 12 * t + 6 * h, 12 * t + 6 * h + 6))
         mark(V, h0, tin[t])
+        HLs = hl32 if t == 0 else HLg
         L0h = new("h", NS)
-        gather("v", L0h, hl32 if t == 0 else HLg, h0)
-        for h in range(2):
-            gather("a", hv(Lf[h], 0), HLg, hv(h0, h, 6))
-        e0p = sub(P6, 0, NS)
+        gather("v", L0h, HLs, h0)
+        e0p = sub(M0, 0, NS)
         mm([(e0p, rs[t], L0h)])
         s0 = new("f", NS)
-        es0, e0u = wrap(e0p, ME, BE, s0)
+        e0u = wrap(e0p, ME, BE, s0)[1]
         e0b = new("f", 208)
         memset(sub(e0b, NS, 208), 4000.0)
         act(sub(e0b, 0, NS), e0p, ACT.Copy)
         hb1 = new("h", NS)
         gather("v", hb1, Wg, e0u)
         hs1, h1u = wrap(hb1, MH, B)
-        L1u = new("u", NS)
-        gather("v", L1u, hl32 if t == 0 else HLg, h1u)
-        for h in range(2):
-            gather("a", hv(Lf[h], 1), HLg, hv(h1u, h, 6))
+        L1u, L1h, L2u, L2h = new("u", NS), new("h", NS), new("u", NS), new("h", NS)
+        gather("v", L1u, HLs, h1u)
+        copy(L1h, L1u)
+        d1 = [steps(sub(L1h, a, b), a // 16, drow[0]) for a, b in PARTS]
         vb1 = new("b", NS)
         gather("a", vb1, Vg, h1u, ACT.Relu, vbias)
-        ns1 = dedupe(hb1, lambda c: sub(hs1, 16 * c, 16 * c + 1), vb1, None)
-        pw = flagwrap(sub(P7, 256, 256 + NS), I2k, ns1, spare[0])
-        tw, offM = new("f", 12), new("u", 12)
-        tt(tw, pw, hs1, ALU.max)
-        ts(offM, tw, B, ALU.add)
+        ns1 = dedupe(hb1, hs1, vb1, None)
+        pw = flagwrap(sub(M1, 256, 256 + NS), I2k, ns1, spare[0])
+        twM, offM = new("f", 12), new("u", 12)
+        tt(twM, pw, hs1, ALU.max)
+        ts(offM, twM, B, ALU.add)
         mark(V, offM, tin[t])
-        for h in range(2):
-            copy(sub(offL[h], 6, 12), hv(offM, h, 6))
-        x0w = new("b", 208)
-        x0 = sub(x0w, 0, NS)
-        memset(sub(x0w, NS, 208), 0.0)
-        for h in range(2):
-            gather("a", hv(x0, h), Xg, hv(e0u, h, 6))
-        for h in range(2):
+        x0T = []
+        for a, b in PARTS:
+            gather("a", sub(x0, a, b), Xg, w16_(e0u, a, b, 1))
+            o, xt = part(sub(M0, 0, 128), 0, b - a), part(new("b", 128), 0, b - a)
+            mm([(o, sub(x0, a, b), I)])
+            act(xt, o, ACT.Copy)
+            x0T.append(xt)
+        for eng, a, b in FOLD:
             for j in range(16):
-                o = sub(hv(XE, h, 1536), j, 1536, 16)
-                if j < XEG[h]:
-                    asel(o, hv(x0, h), [[0, HS]], ALU.is_ge, 0, 0)
+                o = sub(XE, 16 * a + j, 16 * b, 16)
+                if eng == "g":
+                    asel(o, sub(x0, a, b), [[0, b - a]], ALU.is_ge, 0, 0)
                 else:
-                    copy(o, hv(x0, h))
-        prod1, prod2, hb2 = new("h", NS), new("h", NS), new("h", NS)
-        s1, s2, sh = new("f", NS), new("f", NS), new("f", NS)
-        e1u, e2u, h2u, L2u = new("u", 12), new("u", 12), new("u", 12), new("u", NS)
+                    copy(o, sub(x0, a, b))
+        if t == 0:
+            message(sub(PRE[t], 0, 208), sub(PRR[t], 0, 208), t, 1)
+        else:
+            message(PRE[t], PRR[t], t, 1)
+        hb2, sh, h3w = new("h", NS), new("f", NS), new("h", 193)
+        nf1, nf2, u1, u2 = new("b", 204), new("b", 204), new("f", 204), new("f", 204)
+        e1u, e2u, h2u = new("u", 12), new("u", 12), new("u", 12)
         ge1, ge2, vb2 = new("b", NS), new("b", NS), new("b", NS)
-        h3w = new("f", 208)
-        memset(sub(h3w, NS, 208), 0.0)
-        for h in range(2):
-            distances(h, L1u, x0, 1)
-        for h in range(2):
-            oh, ep = pick(h, HS, hv(Lf[h], 1), hv(prod1, h))
-            wrap(ep, ME, BE, hv(s1, h), hv(e1u, h, 6))
-            act(hv(ohs[h], 1), oh, ACT.Copy)
-            gather("v", hv(hb2, h), Wg, hv(e1u, h, 6))
-            wrap(hv(hb2, h), MH, B, hv(sh, h), hv(h2u, h, 6))
-            gather("v", hv(L2u, h), HLg, hv(h2u, h, 6))
-            gather("a", hv(Lf[h], 2), HLg, hv(h2u, h, 6))
-            distances(h, L2u, x0, 2)
+        memset(sub(h3w, NS, 193), 0.0)
+        d2 = []
+        for h in range(len(PARTS)):
+            distances(1, h, L1u, x0T)
+        for h, (a, b) in enumerate(PARTS):
+            pick(a, b, d1[h], w16_(nf1, a, b, 17), w16_(u1, a, b, 17), w16_(e1u, a, b, 1), BE)
+            gather("v", sub(hb2, a, b), Wg, w16_(e1u, a, b, 1))
+            wrap(sub(hb2, a, b), MH, B, sub(sh, a, b), w16_(h2u, a, b, 1))
+            gather("v", sub(L2u, a, b), HLs, w16_(h2u, a, b, 1))
+            copy(sub(L2h, a, b), sub(L2u, a, b))
+            d2.append(steps(sub(L2h, a, b), 12 + a // 16, drow[0]))
+            distances(2, h, L2u, x0T)
         gtt(ge1, Xg, e1u, dm, ALU.is_ge)
-        cp, cn = sub(P6, 0, NS), sub(P6, 256, 256 + NS)
-        mm([(cp, blk, ge1), (cp, I32, ns1), (cn, blk, ge1), (cn, nI32, ns1)], each=2)
-        dead1, m1n = new("b", NS), new("b", NS)
+        cp = sub(M0, 0, NS)
+        mm([(cp, blk, ge1), (cp, I2k, ns1)])
+        dead1 = new("b", NS)
         ts(dead1, cp, need, ALU.is_ge)
-        ts(m1n, cn, need, ALU.is_ge, -1.0, ALU.mult)
-        hm = sub(P7, 256, 256 + NS)
+        hm = sub(M1, 256, 256 + NS)
         mm([(hm, I, hb2), (hm, I2k, dead1)])
         hm = wrap(hm, MH, None)[0]
         gather("a", vb2, Vg, h2u, ACT.Relu, vbias)
-        ns2 = dedupe(hb2, lambda c: sub(hm, 16 * c, 16 * c + 1), vb2, dead1)
-        pA = sub(P6, 0, NS)
-        mm([(pA, blk, prod1), (pA, nrs[t], L0h)])
-        pA1 = new("h", NS)
-        tt(pA1, pA, m1n, ALU.mult)
-        failed, pos, m2n = new("b", NS), new("b", NS), new("b", NS)
-        pA2, pB2, offW = new("h", NS), new("h", NS), new("u", 24)
-        m1s, m1r, acc, sidx = new("h", 96), new("h", 96), new("f", 2), new("u", 2)
-        tw2 = new("f", 24)
-        for h in range(2):
-            oh, ep = pick(h, HS, hv(Lf[h], 2), hv(prod2, h))
-            wrap(ep, ME, BE, hv(s2, h), hv(e2u, h, 6))
-            act(hv(ohs[h], 2), oh, ACT.Copy)
-            gtt(hv(ge2, h), Xg, hv(e2u, h, 6), hv(dm, h), ALU.is_ge)
-            gather("a", hv(h3w, h), Wg, hv(e2u, h, 6))
-            cp, cn = sub(P6, 0, HS), sub(P7, 0, HS)
-            mm([(cp, I32, hv(ns2, h)), (cp, blk, hv(ge2, h))])
-            mm([(cn, nI32, hv(ns2, h)), (cn, blk, hv(ge2, h))])
-            ts(hv(failed, h), cp, need, ALU.is_lt)
-            scan(hv(pos, h), hv(failed, h), hv(failed, h), sub(pos, HS - 1, HS) if h else 0.0, ALU.add, ALU.max)
-            if h:
-                for c in range(2):
-                    act(hv(junk, c, NS), pos, ACT.Sign, bias=sub(kcol, c, c + 1), scale=-1.0, acc=sub(acc, c, c + 1))
-                ts(sidx, acc, 0.5, ALU.mult, 96.0, ALU.add)
-                gather("v", sub(m1s, 0, 32), x0w, sidx)
-                gather("v", sub(m1s, 32, 64), sub(DM, 208 * t, 208 * t + 208) if t else snum, sidx)
-                gather("v", sub(m1s, 64, 96), h3w, sidx)
-                message(m1s, m1r, t, 0)
-            ts(hv(m2n, h), cn, need, ALU.is_ge, -1.0, ALU.mult)
-            bank = (P4, P5)[h]
-            pA, pB = sub(bank, 0, HS), sub(bank, HS, 2 * HS)
-            mm([(pA, blk, hv(prod1, h)), (pA, nrs[t], hv(L0h, h)), (pB, nblk, hv(prod1, h)), (pB, blk, hv(prod2, h))], each=2)
-            tt(hv(pA2, h), pA, hv(m2n, h), ALU.mult)
-            tt(hv(pB2, h), pB, hv(m2n, h), ALU.mult)
-            dl = sub(bank, 192, 480)
-            a1, a2, b2 = hv(pA1, h), hv(pA2, h), hv(pB2, h)
-            mm([(hv(dl, 0), nI, a1), (hv(dl, 0), nI, a2), (hv(dl, 1), I, a1), (hv(dl, 1), nI, b2), (hv(dl, 2), I, a2), (hv(dl, 2), I, b2)], each=2)
-            Tl = new("f", 288)
-            tt(Tl, dl, ohs[h], ALU.mult)
-            pw = flagwrap(sub(P7, 256, 256 + HS), I3k, hv(m2n, h), hv(spare[1], h))
-            tw = new("f", 6)
-            tt(tw, pw, sub(hv(sh, h), 15, HS, 16), ALU.max)
-            ts(sub(offL[h], 12, 18), tw, B, ALU.add)
-            scatter(HL, offL[h], Tl, Lf[h])
-            tt(hv(tw2, h, 6), pw, sub(hv(s0, h), 15, HS, 16), ALU.max)
-            tt(hv(tw2, 2 + h, 6), pw, sub(hv(s1, h), 15, HS, 16), ALU.max)
-        ts(offW, tw2, BE, ALU.add)
-        e0c, x0c = new("f", 32), new("b", 32)
+        ns2 = dedupe(hb2, hm, vb2, dead1)
+        failed, pos, m2n, paid = new("b", NS), new("b", NS), new("b", NS), new("b", NS)
+        e1b, e2b, tw2 = new("h", NS), new("h", NS), new("f", 24)
+        gather("a", e1b, FT, e1u)
+        j1u = slots(nf1)
+
+        def pay(a, b):
+            n, k = b - a, (b - a) // 16
+            Lf, ohs, Tl, offL = new("f", 3 * n), new("b", 3 * n), new("f", 3 * n), new("u", 3 * k)
+            gather("a", sub(e2b, a, b), FT, w16_(e2u, a, b, 1))
+            ts(sub(ohs, 0, n), sub(ones, 0, n), sub(rm, t, t + 1), ALU.mult)
+            gather("a", sub(ohs, n, 2 * n), rm, w16_(j1u, a, b, 1))
+            gather("a", sub(ohs, 2 * n, 3 * n), rm, slots(w16_(nf2, a, b, 17)))
+            for i, Lh in enumerate((L0h, L1h, L2h)):
+                act(sub(Lf, n * i, n * i + n), sub(Lh, a, b), ACT.Copy)
+            cn, cq = sub(M1, 0, n), sub(M1, n, 2 * n)
+            g2, n2 = sub(ge2, a, b), sub(ns2, a, b)
+            mm([(cn, nI2k, n2), (cn, blk, g2)])
+            mm([(cq, nI2k, sub(ns1, a, b)), (cq, I3k, sub(dead1, a, b)), (cq, nI2k, n2), (cq, blk, g2)])
+            ts(sub(m2n, a, b), cn, need, ALU.is_ge, -1.0, ALU.mult)
+            ts(sub(paid, a, b), cq, need, ALU.is_ge)
+            pA, pC, l0 = sub(BK[1], 0, n), sub(BK[1], n, 2 * n), sub(L0h, a, b)
+            mm([(pA, I, sub(e1b, a, b)), (pA, nrs[t], l0), (pC, I, sub(e2b, a, b)), (pC, nrs[t], l0)], each=2)
+            y1, y2 = new("h", n), new("h", n)
+            tt(y1, pA, sub(paid, a, b), ALU.mult)
+            tt(y2, pC, sub(m2n, a, b), ALU.mult)
+            dl = [sub(BK[2], n * i, n * i + n) for i in range(3)]
+            mm([(dl[2], rs[t], l0), (dl[2], nI, sub(e2b, a, b)), (dl[1], nI, y1), (dl[1], nI, y2)], each=2)
+            mm([(dl[0], I, y1)])
+            tt(Tl, sub(BK[2], 0, 3 * n), ohs, ALU.mult)
+            pw = flagwrap(sub(M1, 2 * n, 3 * n), I3k, sub(m2n, a, b), sub(spare[1], a, b))
+            tw = new("f", k)
+            tt(tw, pw, sub(sh, a + 15, b, 16), ALU.max)
+            copy(sub(offL, 0, k), sub(ho32, 12 * t + a // 16, 12 * t + b // 16))
+            ts(sub(offL, k, 2 * k), w16_(twM, a, b, 1), B, ALU.add)
+            ts(sub(offL, 2 * k, 3 * k), tw, B, ALU.add)
+            scatter(HL, offL, Tl, Lf)
+            tt(w16_(tw2, a, b, 1), pw, sub(s0, a + 15, b, 16), ALU.max)
+            tt(w16_(tw2, NS + a, NS + b, 1), pw, sub(u1, a * 17 // 16 + 16, b * 17 // 16, 17), ALU.max)
+
+        for h, (a, b) in enumerate(PARTS):
+            pick(a, b, d2[h], w16_(nf2, a, b, 17), w16_(u2, a, b, 17), w16_(e2u, a, b, 1), BE)
+            gtt(sub(ge2, a, b), Xg, w16_(e2u, a, b, 1), sub(dm, a, b), ALU.is_ge)
+            gather("a", sub(h3w, a, b), Wg, w16_(e2u, a, b, 1))
+            cp = sub(M0, a, b)
+            mm([(cp, I2k, sub(ns2, a, b)), (cp, blk, sub(ge2, a, b))])
+            ts(sub(failed, a, b), cp, need, ALU.is_lt)
+            scan(sub(pos, a, b), sub(failed, a, b), sub(failed, a, b), sub(pos, a - 1, a) if a else 0.0, ALU.add, ALU.max)
+            for pa, pb in PAY[:-1]:
+                if pb == b:
+                    pay(pa, pb)
+        mAs, mAr, acc = new("u", 8), new("u", 8), new("f", 2)
+        memset(mAs, 0)
+        dh = sub(BK[0], 0, NS)
+        mm([(dh, I, sub(h3w, 0, NS)), (dh, nI, sub(h3w, 1, 193))])
+        act(sub(DH, 1, 193), dh, ACT.Copy)
+        for c in range(2):
+            ts(sub(NFH, 208 * c + 1, 208 * c + NS), sub(pos, 0, NS - 1), sub(kcol, c, c + 1), ALU.is_gt)
+            act(sub(junk, NS * c, NS * c + NS), pos, ACT.Sign, bias=sub(kcol, c, c + 1), scale=-1.0, acc=sub(acc, c, c + 1))
+        for c in range(2):
+            scan(sub(UH, 208 * c, 208 * c + 193), DH, sub(NFH, 208 * c, 208 * c + 193), 0.0, ALU.add, ALU.mult)
+        sidx = sub(mAs, 2, 4)
+        ts(sidx, acc, 0.5, ALU.mult, 96.0, ALU.add)
+        copy(sub(mAs, 0, 2), sub(UH, 192, 416, 208))
+        message(mAs, mAr, t, 2)
+        e0c, mBs, mBr = new("f", 32), new("f", 4), new("f", 4)
+        memset(mBs, 0.0)
         gather("a", e0c, e0b, sidx)
-        gather("a", x0c, x0w, sidx)
         esc, _u = wrap(e0c, ME, None)
-        tc, offa = new("f", 2), new("u", 2)
+        ts(sub(mBs, 0, 2), esc, BE + B, ALU.add)
+        message(mBs, mBr, t, 3)
+        pay(*PAY[-1])
+        tc, offo, offW = new("f", 2), new("u", 2), new("u", 24)
         tt(tc, esc, C4, ALU.min)
-        ts(offa, tc, BE, ALU.add)
-        x0m, dmm, h3m = sub(m1r, 0, 32), sub(m1r, 32, 64), sub(m1r, 64, 96)
-        _s, h3u = wrap(h3m, MH, B)
-        if t == 0:
-            _s, su = wrap(dmm, MH, B)
-            dmm = new("b", 32)
-            gather("a", dmm, DR, su)
-        nv = 16 * XSPLIT
-        xb = BK[2]
-        mm([(xb, one1, zrow)] + [(sub(xb, j, 512, 16), nI, x0m) for j in range(16)], last=False)
-        key = sub(P4, 0, 128)
-        mm([(key, one1, part(q128, 0, 1))], last=False)
-        Lxu, Lxf = new("u", 32), new("f", 32)
+        ts(offo, tc, BE, ALU.add)
+        scatter(FT, offo, own)
+        ts(offW, tw2, BE, ALU.add)
+        h3u, su = sub(mAr, 0, 2), sub(mAr, 2, 4)
+        x0m, dmm = new("b", 32), new("b", 32)
+        Lxu, Lxh = new("u", 32), new("h", 32)
         gather("v", Lxu, HLg, h3u)
-        gather("a", Lxf, HLg, h3u)
+        gather("a", x0m, sub(PRR[t], 0, 208), su)
+        copy(Lxh, Lxu)
+        gather("a", dmm, sub(PRR[t], 208, 416), su)
         if t == RO - 1:
             dma("s", lambda E, A, T: E.dma_start(T.yl[:], A(HLg)), [HLg], [], 393216)
+        nv = 16 * XSPLIT
+        xb = BK[0]
+        mm([(xb, one1, zrow)])
+        ops[-1]["fn"] = lambda E, A, xb=xb: E.matmul(A(xb), A(one1), A(zrow), True, False)
+        mm([(sub(xb, j, 512, 16), nI, x0m) for j in range(16)], first=False, last=False)
         gather("v", sub(Ag, 0, nv), Xg, sub(Lxu, 0, XSPLIT))
         gather("a", sub(Ag, nv, 512), Xg, sub(Lxu, XSPLIT, 32))
         mm([(xb, I, sub(Ag, 0, 512))], first=False)
-        act(sub(Ab, 0, 512), xb, ACT.Abs)
-        mm([(sub(key, j, 128, 16, 0, 32), sub(Ab, j, 512, 16), G8) for j in range(16)] + [(key, one1, sub(zrow, 0, 128))], first=False)
-        prodx = new("h", 32)
-        oh, fp = pick(0, 32, Lxf, prodx)
-        ftri = sub(P7, 0, 64)
-        mm([(sub(ftri, 0, 32), blk, prodx), (sub(ftri, 0, 32), I, sub(TRI, 0, 32)),
-            (sub(ftri, 32, 64), blk, prodx), (sub(ftri, 32, 64), I, sub(TRI, 32, 64))], each=2)
-        fs, fu = wrap(fp, ME, BE)
-        gex, dif = new("b", 32), new("b", 32)
-        gtt(gex, Xg, fu, dmm, ALU.is_ge)
-        Eo, E1, E2 = new("b", 64), new("b", 64), new("b", 64)
+        act(grid("ab3", 17, 0, 32, 1, 0, 16), xb, ACT.Abs)
+        nfx, ux, fu = new("b", 34), new("f", 34), new("u", 2)
+        pick(0, 32, steps(Lxh, 24, drow[1]), nfx, ux, fu, -B)
+        fall, mCs, mCr = new("f", 32), new("b", 32), new("b", 32)
+        gtt(sub(gex, 0, 32), Xg, fu, dmm, ALU.is_ge)
+        gather("a", fall, FT, fu, ACT.Relu, B)
+        gather("a", mCs, Xg, fu)
+        message(mCs, mCr, t, 4)
+        pv, flag, fin = sub(KB[turn["k"] % 2], 0, 66), new("b", 66), new("f", 66)
+        mm([x for c in range(2) for x in ((sub(pv, 33 * c, 33 * c + 33), I, sub(TRI, 33 * c, 33 * c + 33)),
+                                          (sub(pv, 33 * c, 33 * c + 33), nblk, gex))], each=2)
         for c in range(2):
-            ts(sub(Eo, 32 * c, 32 * c + 32), fp, sub(esc, 16 * c, 16 * c + 1), ALU.subtract, BE, ALU.is_equal)
-        pv, pg = sub(P5, 0, 32), sub(P6, 0, 32)
-        base = [(nblk, gex), (blk32, sub(Eo, 0, 32)), (blk32, sub(Eo, 32, 64))]
-        mm([(pv, l, r) for l, r in base])
-        mm([(pg, l, r) for l, r in base], last=False)
+            ts(sub(TE, 33 * c, 33 * c + 32), fall, sub(ux, 17 * c + 16, 17 * c + 17), ALU.is_equal, room, ALU.mult)
+        tt(flag, pv, TE, ALU.is_le)
+        scan(fin, D0, flag, 0.0, ALU.mult, ALU.subtract)
+        mDs, mDr, offb = new("u", 8), new("u", 8), new("u", 2)
+        memset(mDs, 0)
         for c in range(2):
-            ts(sub(E1, 32 * c, 32 * c + 32), sub(ftri, 32 * c, 32 * c + 32), sub(fs, 16 * c, 16 * c + 1), ALU.subtract, BE, ALU.is_equal)
-        gtt(dif, Xg, fu, x0m, ALU.subtract)
-        vs, _u = wrap(pv, MH, None)
+            ts(sub(mDs, c, c + 1), sub(fin, 33 * c + 32, 33 * c + 33), sub(mBr, c, c + 1), ALU.add, sub(SP, c, c + 1), ALU.min)
+        message(mDs, mDr, t, 5)
         for c in range(2):
-            ts(sub(E2, 32 * c, 32 * c + 32), sub(E1, 32 * c, 32 * c + 32), sub(vs, 16 * c, 16 * c + 1), ALU.mult, nneedB, ALU.is_le)
-        mm([(pg, blk32, sub(E2, 0, 32)), (pg, blk32, sub(E2, 32, 64))], first=False)
-        grant = new("b", 32)
-        m2s, m2r = new("b", 32), new("b", 32)
-        ts(grant, pg, nneed, ALU.is_le)
-        tt(m2s, grant, dif, ALU.mult)
-        message(m2s, m2r, t, 1)
-        pw = flagwrap(sub(P7, 256, 288), nI3k, grant, sub(spare[2], 0, 32))
-        tb, offb = new("f", 2), new("u", 2)
-        tt(tb, pw, fs, ALU.max)
-        ts(offb, tb, BE, ALU.add)
+            ts(sub(offb, c, c + 1), sub(fin, 33 * c + 32, 33 * c + 33), sub(ux, 17 * c + 16, 17 * c + 17), ALU.add, sub(SP, c, c + 1), ALU.min)
         scatter(X, offb, x0m)
         scatter(W, sub(offW, 0, 12), hb2)
         scatter(W, sub(offW, 12, 24), hb1)
         if t == RO - 1:
             dma("s", lambda E, A, T: E.dma_start(T.yw[:], T.af[0:128:16, W[1]:W[1] + NP]), [Wg], [], 65536)
         else:
-            pc = sub(P5, 256, 256 + NS)
-            mm([(pc, o16, m1n), (pc, o16, m2n)])
-            cnt, ci, cj, bf_, nd = new("f", 1), new("i", 1), new("i", 1), new("f", 1), new("f", 3)
-            act(hv(junk, 0, NS), pc, ACT.Copy, scale=-1.0, acc=cnt)
+            scatter(FT, offo, e0c)
+            pc = sub(M0, 256, 256 + NS)
+            mm([(pc, o16, paid)])
+            cnt, ci, cj, bf_, nd = new("f", 1), new("i", 1), new("i", 1), new("f", 1), new("f", 2)
+            act(sub(junk, 0, NS), pc, ACT.Copy, acc=cnt)
             copy(ci, cnt)
             ts(cj, ci, 1, ALU.bitwise_and)
             copy(bf_, cj)
             ts(sub(nd, 0, 1), bf_, 9.0, ALU.add)
-            ts(sub(nd, 1, 2), bf_, -1.0, ALU.mult, -9.0, ALU.add)
-            ts(sub(nd, 2, 3), bf_, -1.0, ALU.mult, -9.0 - B, ALU.add)
-            need, nneed, nneedB = sub(nd, 0, 1), sub(nd, 1, 2), sub(nd, 2, 3)
-        scatter(X, offa, x0c, m2r)
+            ts(sub(nd, 1, 2), bf_, -1.0, ALU.mult, 55.0, ALU.add)
+            need, room = sub(nd, 0, 1), sub(nd, 1, 2)
+        scatter(X, sub(mDr, 0, 2), mCr)
     for k, eng in enumerate(("s", "a")):
         dma(eng, lambda E, A, T, k=k: E.dma_start(T.yx[64 * k:64 * k + 64, :], A(part(Xg, 64 * k, 64 * k + 64))), [Xg], [], 262144)
-    return ops, size
+    return ops, size, sent
 
 
 def depend(ops):
@@ -565,16 +628,16 @@ def depend(ops):
         for wr, vs in ((False, op["r"]), (True, op["w"])):
             for v in vs:
                 if is_ps(v):
-                    for bk in range(v[1] // 512, (v[2] - 1) // 512 + 1):
-                        acc.append(((v[0], bk), 0, 1, wr, 1))
+                    acc.append(((v[0], 0), 0, 1, wr, 1))
                 else:
                     acc.append((v[0], v[1], v[2], wr, v[3]))
         deps = set()
         for key, lo, hi, wr, st in acc:
             for (m, l2, h2, w2, s2) in log.get(key, []):
                 clash = wr or w2 or (key[0][0] == "p" and ops[m]["eng"] != op["eng"])
-                if l2 < hi and lo < h2 and clash and m != n and not (st == s2 and (lo - l2) % st):
+                if l2 < hi and lo < h2 and clash and m != n and not (st == s2 and st and (lo - l2) % st):
                     deps.add(m)
+        op["soft"] = {m for m in deps if ops[m]["eng"] == op["eng"] == "t" or ops[m]["kind"] == op["kind"] == "send"}
         for key, lo, hi, wr, st in acc:
             lst = log.setdefault(key, [])
             if wr and st == 1:
@@ -592,7 +655,7 @@ def schedule(ops, seed, jitter):
             dur[i], occ[i] = bus, 60
         else:
             dur[i], occ[i] = op["cost"], 0 if op["eng"] == "x" else op["cost"]
-    pred = [[(d, 0 if op["eng"] == "t" and ops[d]["eng"] == "t" else HOP) for d in op["deps"]] for op in ops]
+    pred = [[(d, 0 if d in op["soft"] else HOP) for d in op["deps"]] for op in ops]
     loads = [i for i, op in enumerate(ops) if op["eng"] == "s" and not op["deps"]]
     for a, b in zip(loads, loads[1:]):
         pred[b].append((a, occ[a] - dur[a]))
@@ -631,7 +694,7 @@ def schedule(ops, seed, jitter):
         for i in order:
             e = ops[i]["eng"]
             t = max([free[e]] + [fin[d] + (hop if h == HOP else h) for d, h in pred[i]])
-            fin[i] = t + (fly if e == "x" else dur[i] * slow if ops[i]["extra"] == "index" else dur[i])
+            fin[i] = t + (dur[i] + fly - FLY if e == "x" else dur[i] * slow if ops[i]["extra"] == "index" else dur[i])
             free[e] = fin[i] if occ[i] == dur[i] else t + occ[i]
         return max(fin)
 
@@ -713,7 +776,7 @@ def signals(ops, order):
         ws = {}
         for d in sorted(op["deps"], key=lambda d: -token[d][1]):
             s, c = token[d]
-            if e == "t" and s == "t":
+            if d in op["soft"]:
                 continue
             if k.get(s, 0) < c:
                 ws[s] = max(ws.get(s, 0), c)
@@ -733,18 +796,18 @@ def signals(ops, order):
     return token, waits, used, val, nd
 
 
-OPS, SIZE = plan()
+OPS, SIZE, SENT = plan()
 depend(OPS)
 ORDER, START, FIN = schedule(OPS, SEED, JITTER)
 TOKEN, WAITS, USED, VAL, NDMA = signals(OPS, ORDER)
 
 SCRATCH = {ARENA[k][0]: ("sbuf", [128, SIZE[k]], ARENA[k][1]) for k in ARENA}
-SCRATCH["pa"] = ("psum", [128, 1024], "float32")
-SCRATCH["pb"] = ("psum", [128, 1024], "float32")
-for _k in (4, 5, 6, 7):
+SCRATCH["ab3"] = ("sbuf", [128, NS, 17], "bfloat16")
+SCRATCH["tt3"] = ("sbuf", [128, 26, 16], "float16")
+for _k in range(7):
     SCRATCH["p%d" % _k] = ("psum", [128, 512], "float32")
-SEMAPHORES = (["qv", "qa", "qt", "qg"] + ["d%d" % k for k in range(NDMA)]
-              + ["%s%d%d" % (a, t, k) for a in "rl" for t, k in ((0, 0), (0, 1), (0, 2), (1, 0), (1, 1))])
+SCRATCH["pd"] = ("psum", [128, 15, 34], "float32")
+SEMAPHORES = ["qv", "qa", "qt", "qg"] + ["d%d" % k for k in range(NDMA)] + ["%s%d%d" % (a, t, k) for a in "rl" for t, k in SENT]
 
 
 def rank_program(g, core, T, topo):
@@ -755,13 +818,15 @@ def rank_program(g, core, T, topo):
     Q = {"v": g.vector, "a": g.scalar, "t": g.tensor, "g": g, "s": g.sync}
 
     def A(v):
+        if len(v) > 6:
+            return T[v[0]][v[4]:v[5], v[6][0], v[6][1]]
         if v[3] == 1:
             return T[v[0]][v[4]:v[5], v[1]:v[2]]
         return T[v[0]][v[4]:v[5], v[1]:v[2]:v[3]]
 
-    def peer(t, k):
+    def peer(t, back):
         d = 1 + t % (n - 1)
-        return T.cores[(rank + d) % n] if k != 1 else T.cores[(rank - d) % n]
+        return T.cores[(rank - d) % n] if back else T.cores[(rank + d) % n]
 
     def amount(s, c):
         if s in ("v", "a", "t", "g"):
@@ -770,8 +835,8 @@ def rank_program(g, core, T, topo):
             return T.sem[s], 16
         t, k = int(s[1]), int(s[2])
         if s[0] == "r":
-            return T.sem[s], len(topo.engines(peer(t, 0 if k == 1 else 1), core))
-        return T.sem[s], len(topo.engines(core, peer(t, k)))
+            return T.sem[s], len(topo.engines(peer(t, k not in BACK), core))
+        return T.sem[s], len(topo.engines(core, peer(t, k in BACK)))
 
     waited = set()
     for i in ORDER:
@@ -791,7 +856,7 @@ def rank_program(g, core, T, topo):
             op["fn"](E, A, T).then_inc(T.sem[TOKEN[i][0]], 16)
         else:
             src, dst, t, k = op["extra"]
-            to = peer(t, k)
+            to = peer(t, k in BACK)
             rid, pid = topo.addr(to, core)
             g.remote_dma(A(dst), A(src), T.sem["r%d%d" % (t, k)], T.sem["l%d%d" % (t, k)], pid, rid, topo.mask(core, to))
     for i in ORDER:

@@ -9,12 +9,18 @@ HOP = 240
 PE = 2.0
 FLY = 3000
 PARTS = ((0, 64), (64, 128), (128, 192))
-PIECES = {(1, 0): "w32 a32", (1, 1): "v40 a24", (1, 2): "v40 a24", (2, 0): "v40 a24", (2, 1): "v40 a24", (2, 2): "v32 a32"}
-FOLD = (("g", 0, 40), ("v", 64, 168))
-CASES = ((200, 3000, 1.25),)
+PIECES = {(1, 0): "w32 w32", (1, 1): "v32 m32", (1, 2): "v32 w32", (2, 0): "v32 w32", (2, 1): "v32 m32", (2, 2): "v32 w16 m16"}
+FOLD = (("g", 0, 32), ("v", 64, 160))
 PAY = ((0, 128), (128, 192))
+SLACK = 100
+OPEN = (((0, 64), (64, 192)), ((0, 192),))
+JUDGE = (((0, 128), (128, 192)), ((0, 128), (128, 192)))
+TURN = ((0, 64), (64, 192))
+VIA = True
+LEAD = 0
 XSPLIT = 16
-SEED, JITTER, PASSES = 1, 200, 3200
+SWEEPS, WIDE = 6, 10000
+SEED, JITTER, PASSES = 4, 200, 1500
 ARENA = {"f": ("af", "float32"), "b": ("ab", "bfloat16"), "h": ("ah", "float16"), "u": ("au", "uint16"), "i": ("ai", "int32")}
 BACK = (4, 5)
 
@@ -40,8 +46,11 @@ def is_ps(v):
 
 
 def plan():
-    ops = []
+    ops, lead = [], [0]
     size = {k: 0 for k in ARENA}
+
+    def ahead(h):
+        lead[0] = 0 if h is None else LEAD * (len(PARTS) - 1 - h)
 
     def new(k, n):
         lo = size[k]
@@ -53,7 +62,14 @@ def plan():
 
     def add(eng, fn, r, w, cost, kind="c", extra=None):
         r = [v for v in r if isinstance(v, tuple)]
-        ops.append({"eng": eng, "fn": fn, "r": r, "w": list(w), "cost": cost, "kind": kind, "extra": extra})
+        ops.append({"eng": eng, "fn": fn, "r": r, "w": list(w), "cost": cost, "kind": kind, "extra": extra, "lead": lead[0]})
+
+    def either(first):
+        a, v = ops.pop(), ops[-1]
+        v["alt"] = {"v": (v["fn"], v["cost"]), "a": (a["fn"], a["cost"])}
+        v["r"] = v["r"] + [x for x in a["r"] if x not in v["r"]]
+        v["eng"] = first
+        v["fn"], v["cost"] = v["alt"][first]
 
     def S(A, s):
         return A(s) if isinstance(s, tuple) else s
@@ -94,17 +110,28 @@ def plan():
             return E.activation(A(o), A(i), f, **kw)
         add("a", fn, [i, bias, scale], [o] + ([acc] if acc else []), max(64, width(o)) + 30)
 
+    def move(o, i, scale=None, first="a"):
+        if scale is None:
+            copy(o, i)
+        else:
+            ts(o, i, scale, ALU.mult)
+        act(o, i, ACT.Copy, scale=scale)
+        either(first)
+
     def gcost(n):
         return 60 + int(1.56 * n)
 
-    def gather(eng, o, win, off, f=None, bias=None):
-        if eng == "v":
-            fn = lambda E, A: E.tensor_copy(A(o), A(win).indirect(A(off)))
-        elif bias is None:
-            fn = lambda E, A: E.activation(A(o), A(win).indirect(A(off)), ACT.Copy)
+    def gather(eng, o, win, off, bias=None):
+        if bias is None:
+            fv = lambda E, A: E.tensor_copy(A(o), A(win).indirect(A(off)))
+            fa = lambda E, A: E.activation(A(o), A(win).indirect(A(off)), ACT.Copy)
         else:
-            fn = lambda E, A: E.activation(A(o), A(win).indirect(A(off)), f, bias=bias)
-        add(eng, fn, [win, off], [o], gcost(width(o)), extra="index")
+            fv = lambda E, A: E.tensor_scalar(A(o), A(win).indirect(A(off)), bias, 0.0, ALU.add, ALU.max)
+            fa = lambda E, A: E.activation(A(o), A(win).indirect(A(off)), ACT.Relu, bias=bias)
+        add("v", fv, [win, off], [o], gcost(width(o)), extra="index")
+        if eng != "v":
+            add("a", fa, [win, off], [o], gcost(width(o)) + 18, extra="index")
+            either("a" if eng == "a" else "v")
 
     def gtt(o, win, off, b, op):
         add("v", lambda E, A: E.tensor_tensor(A(o), A(win).indirect(A(off)), A(b), op), [win, off, b], [o], gcost(width(o)), extra="index")
@@ -117,7 +144,9 @@ def plan():
         add("v", fn, [off, i, b], [win], 60 + int(3.8 * width(i)), extra="index")
 
     def mark(win, off, i):
+        scatter(win, off, i)
         add("a", lambda E, A: E.activation(A(win).indirect(A(off)), A(i), ACT.Tanh), [off, i], [win], 80 + int(3.8 * width(i)), extra="index")
+        either("a")
 
     def mm(items, first=True, last=True, each=0):
         def fn(E, A):
@@ -166,15 +195,11 @@ def plan():
     Xg, HLg, Wg, Vg = sub(X, 0, NP), sub(HL, 0, NH), sub(W, 0, NP), sub(V, 0, NH)
     dma("s", lambda E, A, T: E.dma_start(A(wr32), T.wr[:]), [], [wr32], 65536)
     dma("a", lambda E, A, T: E.dma_start(A(ho32), T.ho[:]), [], [ho32], 12288)
-
-    def load_dm(t):
-        o = sub(PRE[t], 208, 208 + NS)
-        dma("s" if t else "a", lambda E, A, T: E.dma_start(A(o), T.dm[:, NS * t:NS * (t + 1)]), [], [o], 49152)
-    load_dm(0)
     dma("s", lambda E, A, T: E.dma_start(A(hl32), T.hl[:]), [], [hl32], 393216)
     dma("s", lambda E, A, T: E.dma_start(A(Xg), T.xs[:]), [], [Xg], 524288)
-    load_dm(1)
     for t in range(RO):
+        o = sub(PRE[t], 208, 208 + NS)
+        dma("s", lambda E, A, T, o=o, t=t: E.dma_start(A(o), T.dm[:, NS * t:NS * (t + 1)]), [], [o], 49152)
         memset(sub(PRE[t], 400, 416), 512.0)
         memset(sub(PRE[t], NS, 208), 0.0)
     message(sub(PRE[0], 208, 416), sub(PRR[0], 208, 416), 0, 0)
@@ -184,11 +209,13 @@ def plan():
     o128 = sub(ones, 0, 128)
 
     def fill(o, c):
+        memset(o, float(c))
         act(o, sub(ones, 0, width(o)), ACT.Copy, scale=float(c))
+        either("a")
 
     def scaled(m, c):
         o = new("b", width(m))
-        act(o, m, ACT.Copy, scale=c)
+        move(o, m, c)
         return o
     kg, qb, kc = new("b", 128), new("b", NS), new("b", 128)
     iota(kg, [[-16, 8], [0, 16]], 0, 1)
@@ -197,12 +224,12 @@ def plan():
     iota(pid, [[0, 1]], 0, 1)
     selW = part(new("b", 512), 0, 32)
     asel(selW, part(ones, 0, 32), [[-1, 4], [-4, 8], [0, 16]], ALU.is_equal, 0, 1)
-    q128 = sub(qb, 0, 128)
     rs = [new("b", 128) for t in range(RO)]
-    I, blk, c16, kb = new("b", 128), new("b", 128), new("f", 16), new("b", 32)
+    Ipad, blk, c16, kb = new("b", 160), new("b", 128), new("f", 16), new("b", 32)
+    asel(Ipad, sub(ones, 0, 160), [[-1, 160]], ALU.is_equal, 16, 1)
+    I = sub(Ipad, 16, 144)
     for t in range(RO):
         ts(rs[t], kg, float(t), ALU.is_equal)
-    tt(I, kg, q128, ALU.is_equal)
     ts(kc, kg, 0.0, ALU.max, 15.0, ALU.min)
     tt(blk, kg, kc, ALU.is_equal)
     ts(c16, sub(qb, 0, 16), 16.0, ALU.mult)
@@ -216,23 +243,25 @@ def plan():
     ts(mt2, qb, pm, ALU.is_lt, -B, ALU.mult)
     ts(mt, qb, pm, ALU.is_equal, B, ALU.mult)
     tt(ME, mt2, mt, ALU.add)
-    copy(MH, ME)
+    move(MH, ME)
     ts(sub(MH, 15, NS, 16), sub(MH, 15, NS, 16), -2 * B, ALU.add)
     ts(sub(ME, 15, NS, 16), sub(ME, 15, NS, 16), -B - BE, ALU.add)
     wr16 = part(new("h", 512), 0, 32)
     copy(wr16, wr32)
     for q, bank in enumerate(BK + KB[:1]):
         mm([(bank, sub(selW, 128 * q, 128 * q + 128), wr16)])
-        act(sub(W, 512 * q, 512 * q + 512), bank, ACT.Copy)
+        if q == 0:
+            act(sub(V, 0, 480), sub(ones, 0, 480), ACT.Tanh, scale=0.0)
+            ops[-1]["cost"] += 1600
+        move(sub(W, 512 * q, 512 * q + 512), bank)
+        ops[-1]["r"].append(sub(V, 0, 1))
     copy(HLg, hl32)
-    act(sub(V, 0, 480), sub(ones, 0, 480), ACT.Tanh, scale=0.0)
-    ops[-1]["cost"] += 1600
     fill(sub(V, 480, 960), 0)
     fill(sub(HL, NH, 1152), 0)
     fill(sub(W, NP, NP + NS), 0)
-    memset(sub(X, NP, NP + 64), 0.0)
+    fill(sub(X, NP, NP + 64), 0)
     tin = [new("f", NS) for t in range(RO)]
-    fill(tin[0], 1)
+    fill(tin[0], 0.5)
     fill(tin[1], 4)
     nI, bigI = scaled(I, -1.0), new("b", 128)
     I2k, nI2k, I3k = scaled(I, 2048.0), scaled(I, -2048.0), scaled(I, 3072.0)
@@ -240,13 +269,13 @@ def plan():
     nblk = scaled(blk, -1.0)
     nrs = [scaled(rs[t], -1.0) for t in range(RO)]
     o16 = new("b", 128)
-    memset(o16, 0.0625)
+    fill(o16, 0.0625)
     rm = new("f", 16)
     ts(rm, sub(qb, 0, 16), pm, ALU.is_equal)
     half, wb, thr = new("b", NS), new("f", NS), new("f", NS)
-    memset(half, 0.5)
+    fill(half, 0.5)
     scan(wb, half, sub(ones, 0, NS), 2.0 ** 97, ALU.mult, ALU.mult)
-    act(thr, wb, ACT.Copy, scale=2.5)
+    move(thr, wb, 2.5)
     w16, w0, wcol = new("f", 16), new("f", 1), new("f", 12)
     tt(w16, sub(wb, 0, 16), rm, ALU.mult)
     add("v", lambda E, A: E.tensor_reduce(A(w0), A(w16), AxisListType.X, ALU.add), [w16], [w0], 64)
@@ -260,11 +289,14 @@ def plan():
     for n, c in enumerate((768.0 - 2048.0, 960.0)):
         ts(spare[n], srow, c, ALU.add)
     zrow = part(new("b", 512), 0, 1)
-    memset(zrow, 0.0)
+    memset(sub(zrow, 0, 144), 0.0)
+    memset(sub(zrow, 144, 512), 0.0)
     one1 = part(o128, 0, 1)
+    brow = part(new("b", NS), 0, 1)
+    memset(brow, B)
     Z = new("b", 143)
-    memset(Z, 0.0)
-    act(sub(Z, 15, 143, 16), sub(blk, 0, 128, 16), ACT.Copy, scale=16.0)
+    fill(Z, 0)
+    move(sub(Z, 15, 143, 16), sub(blk, 0, 128, 16), 16.0)
     odi, odd, evn = new("i", 1), new("f", 2), new("f", 2)
     ts(odi, pid, 4, ALU.arith_shift_right, 1, ALU.bitwise_and)
     copy(sub(odd, 0, 1), odi)
@@ -272,44 +304,43 @@ def plan():
     ts(sub(evn, 0, 1), sub(odd, 0, 1), -1.0, ALU.mult, 1.0, ALU.add)
     ts(sub(evn, 1, 2), sub(odd, 0, 1), -1.0, ALU.add)
     IS = new("b", 640)
-    memset(IS, 0.0)
     for n in range(4):
-        act(sub(IS, 160 * n + 16, 160 * n + 144), I, ACT.Copy, scale=sub((evn, odd)[n // 2], n % 2, n % 2 + 1))
+        move(sub(IS, 160 * n, 160 * n + 160), Ipad, sub((evn, odd)[n // 2], n % 2, n % 2 + 1))
     p32i, p32, sq, R = new("i", 1), new("f", 1), new("b", 512), new("b", 512)
     ts(p32i, pid, 31, ALU.bitwise_and)
     copy(p32, p32i)
     iota(sq, [[1, 32], [0, 16]], 0, 0)
     ts(R, sq, p32, ALU.is_equal, -1.0, ALU.mult)
+    R2 = scaled(R, -2.0) if any("m" in x for x in PIECES.values()) else None
     top = 17 * max(b - a for a, b in PARTS) // 16
     RK, DJ = new("b", top), new("b", 204)
-    memset(RK, -1.0)
+    fill(RK, -1)
     memset(sub(RK, 0, top, 17), 131072.0)
-    memset(DJ, -1.0)
+    fill(DJ, -1)
     memset(sub(DJ, 16, 204, 17), 15.0)
     drow = [part(new("b", top), 0, 1) for n in range(2)]
     for n, c in enumerate((-BE, B)):
         memset(drow[n], 0.0)
         memset(sub(drow[n], 16, top, 17), c)
-    memset(grid("ab3", 17, 0, NS, 1, 16, 17), 255.0)
+    memset(grid("ab3", 17, 0, NS, 1, 16, 17), 1024.0)
     iota(FT, [[1, NP + 64]], 0, 0)
     C4, SP, kcol, TRI, tri, D0, d0 = new("f", 2), new("f", 2), new("f", 2), new("b", 66), new("b", 66), new("b", 66), new("b", 66)
     ts(C4, sub(sw, 0, 2), 2048.0 - BE, ALU.add)
     ts(SP, sub(sw, 0, 2), 2048.0, ALU.add)
     ts(kcol, sub(sw, 0, 2), 0.5, ALU.add)
-    memset(tri, 128.0)
-    memset(d0, 4095.0)
+    fill(tri, 128)
+    fill(d0, 4096)
     for c in range(2):
         ts(sub(tri, 33 * c, 33 * c + 32), kb, sub(sw, c, c + 1), ALU.is_gt, 128.0, ALU.mult)
         ts(sub(d0, 33 * c, 33 * c + 32), kb, sub(sw, c, c + 1), ALU.is_equal, -2.0, ALU.mult)
     ts(TRI, tri, 64.0, ALU.add)
     ts(D0, d0, 1.0, ALU.add)
-    memset(sub(D0, 32, 66, 33), B)
     memset(sub(D0, 0, 66, 33), 0.0)
     gex, TE, own = new("b", 33), new("b", 66), new("f", 32)
     memset(sub(gex, 32, 33), 0.0)
     memset(sub(TE, 32, 66, 33), 0.0)
-    memset(own, 4000.0)
-    NFH, DH, UH = new("b", 416), new("h", 193), new("h", 416)
+    fill(own, 4000)
+    NFH, DH, UH = new("b", 416), new("h", 193), new("f", 416)
     memset(sub(NFH, 0, 416, 208), 0.0)
     memset(sub(NFH, 192, 416, 208), 1.0)
     memset(sub(DH, 0, 1), 0.0)
@@ -317,6 +348,9 @@ def plan():
     Ag, XE = new("b", 3072), new("b", 3072)
     Ebuf = new("b", 1248)
     junk = new("b", 2 * NS)
+    e0b, h3w = new("f", 208), new("h", 193)
+    fill(sub(e0b, NS, 208), 4000)
+    memset(sub(h3w, NS, 193), 0.0)
 
     def wrap(src, M, off, s=None, u=None):
         n = width(src)
@@ -335,21 +369,22 @@ def plan():
         mm([(o, one1, row), (o, scale, flag)])
         return wrap(o, MH, None)[0]
 
-    def dedupe(hb, hcols, vb, dead):
-        Sp = sub(M1, 0, NS)
-        items, pos, hc = [], 0, new("f", 12)
-        ts(hc, hcols, B, ALU.add)
+    def dedupe(hb, hcol, vb, dead, parts):
+        es, pos, ns = [], 0, new("b", NS)
         for c in range(12):
-            e = sub(Ebuf, pos, pos + NS - 16 * c)
+            e = sub(Ebuf, pos - 16 * c, pos + NS - 16 * c)
             pos += NS - 16 * c
-            ts(e, sub(hb, 16 * c, NS), sub(hc, c, c + 1), ALU.is_equal, sub(wcol, c, c + 1), ALU.mult)
-            items.append((sub(Sp, 16 * c, NS), blk, e))
-        items.append((Sp, bigI, vb))
-        if dead is not None:
-            items.append((Sp, bigI, dead))
-        mm(items)
-        ns = new("b", NS)
-        tt(ns, Sp, thr, ALU.is_ge)
+            ts(sub(e, 16 * c, NS), sub(hb, 16 * c, NS), hcol(c), ALU.is_equal, sub(wcol, c, c + 1), ALU.mult)
+            es.append(e)
+        for a, b in parts:
+            items = [(sub(M1, max(a, 16 * c), b), blk, sub(es[c], max(a, 16 * c), b)) for c in range(b // 16)]
+            ends = [(sub(M1, a, b), bigI, sub(x, a, b)) for x in (vb, dead) if x]
+            if a:
+                mm(items[:a // 16] + ends[:-1], last=False)
+                mm(items[a // 16:] + ends[-1:], first=False)
+            else:
+                mm(items + ends)
+            tt(sub(ns, a, b), sub(M1, a, b), sub(thr, a, b), ALU.is_ge)
         return ns
 
     def steps(Lh, r0, row):
@@ -366,7 +401,7 @@ def plan():
                                   grid("tt3", 16, r0 + b, r0 + 2 * n, 2, 0, 16)))
         mm(items + [(whole, one1, sub(zrow, 0, 34 * n))])
         d = new("f", 34 * n)
-        act(d, whole, ACT.Copy)
+        move(d, whole)
         return d
 
     def pick(a, b, d, nf, u, eu, off):
@@ -385,18 +420,23 @@ def plan():
             end = a + int(word[1:])
             while a < end:
                 b = min(end, (a - a0) // 32 * 32 + 32 + a0)
-                lu, src = sub(Lu, a, b), sub(Ag, 16 * a, 16 * b)
+                lu, src, out = sub(Lu, a, b), sub(Ag, 16 * a, 16 * b), grid("ab3", 17, a, b, 1, 0, 16)
                 if word[0] == "v":
                     gtt(src, Xg, lu, sub(XE, 16 * a, 16 * b), ALU.subtract)
+                    act(out, src, ACT.Abs)
                 else:
                     q = (a - a0) // 32 * 32
                     o = sub(BK[turn["s"] % 3], 0, 16 * (b - a))
                     turn["s"] += 1
-                    mm([(o, part(x0T[h], q, q + 32), sub(R, 16 * (a - a0 - q), 16 * (b - a0 - q), 1, q, q + 32))], last=False)
-                    gather("a" if word[0] == "a" else "v", src, Xg, lu)
-                    mm([(o, I, src)], first=False)
-                    src = o
-                act(grid("ab3", 17, a, b, 1, 0, 16), src, ACT.Abs)
+                    xt = x0T[a // 32]
+                    fold = sub(R if word[0] == "w" else R2, 16 * (a - a0 - q), 16 * (b - a0 - q), 1, xt[4], xt[5])
+                    mm([(o, xt, fold)], last=False)
+                    gather("a" if q else "w", src, Xg, lu)
+                    mm([(o, I if word[0] == "w" else nI, src)], first=False)
+                    if word[0] == "w":
+                        act(out, o, ACT.Abs)
+                    else:
+                        tt(out, o, src, ALU.max)
                 a = b
 
     def slots(nf):
@@ -415,74 +455,91 @@ def plan():
         vbias = (-0.1, -0.9)[t]
         mark(V, h0, tin[t])
         HLs = hl32 if t == 0 else HLg
-        L0h = new("h", NS)
-        gather("v", L0h, HLs, h0)
-        e0p = sub(M0, 0, NS)
-        mm([(e0p, rs[t], L0h)])
-        s0 = new("f", NS)
-        e0u = wrap(e0p, ME, BE, s0)[1]
-        e0b = new("f", 208)
-        memset(sub(e0b, NS, 208), 4000.0)
-        act(sub(e0b, 0, NS), e0p, ACT.Copy)
-        hb1 = new("h", NS)
-        gather("v", hb1, Wg, e0u)
-        hs1, h1u = wrap(hb1, MH, B)
+        L0h, s0, s1, hbb = new("h", NS), new("f", NS), new("f", NS), new("h", 2 * NS)
+        hb2, hb1, hs1 = sub(hbb, 0, NS), sub(hbb, NS, 2 * NS), sub(s1, 15, NS, 16)
         L1u, L1h, L2u, L2h = new("u", NS), new("h", NS), new("u", NS), new("h", NS)
-        gather("v", L1u, HLs, h1u)
-        copy(L1h, L1u)
+        e0u, h1u = new("u", 12), new("u", 12)
+        for n, (a, b) in enumerate(OPEN[t]):
+            gather("a" if t else "v", sub(L0h, a, b), HLs, w16_(h0, a, b, 1))
+            e0p = sub((M0, M1)[n % 2], a, b)
+            mm([(e0p, rs[t], sub(L0h, a, b))])
+            wrap(e0p, ME, BE, sub(s0, a, b), w16_(e0u, a, b, 1))
+            move(sub(e0b, a, b), e0p)
+            gather("a" if t else "w", sub(hb1, a, b), Wg, w16_(e0u, a, b, 1))
+            wrap(sub(hb1, a, b), MH, B, sub(s1, a, b), w16_(h1u, a, b, 1))
+            gather("v", sub(L1u, a, b), HLs, w16_(h1u, a, b, 1))
+            copy(sub(L1h, a, b), sub(L1u, a, b))
+        if t and VIA:
+            W16, Wu, LW = new("h", NP), new("u", NP // 16), new("f", NP)
+            for a in range(0, NP, 512):
+                move(sub(W16, a, a + 512), sub(W, a, a + 512))
+            wp = sub(BK[1], 0, 128)
+            mm([(wp, sub(Z, 15 - p, 143 - p), sub(W16, p, NP, 16)) for p in range(16)])
+            ts(Wu, wp, 1.0 / 256, ALU.mult)
+            for a in range(0, NP, 256):
+                gather("a", sub(LW, a, a + 256), HLg, w16_(Wu, a, a + 256, 1))
         d1 = [steps(sub(L1h, a, b), a // 16, drow[0]) for a, b in PARTS]
         vb1 = new("b", NS)
-        gather("a", vb1, Vg, h1u, ACT.Relu, vbias)
-        ns1 = dedupe(hb1, hs1, vb1, None)
+        gather("a", vb1, Vg, h1u, vbias)
+        hc = new("f", 12)
+        ts(hc, hs1, B, ALU.add)
+        ns1 = dedupe(hb1, lambda c: sub(hc, c, c + 1), vb1, None, ((0, NS),))
         pw = flagwrap(sub(M1, 256, 256 + NS), I2k, ns1, spare[0])
         twM, offM = new("f", 12), new("u", 12)
         tt(twM, pw, hs1, ALU.max)
         ts(offM, twM, B, ALU.add)
         mark(V, offM, tin[t])
         x0T = []
-        for a, b in PARTS:
+        for n, (a, b) in enumerate(TURN):
             gather("a", sub(x0, a, b), Xg, w16_(e0u, a, b, 1))
-            o, xt = part(sub(M0, 0, 128), 0, b - a), part(new("b", 128), 0, b - a)
+            o, xt = part(sub(KB[n % 2], 0, 128), 0, b - a), part(new("b", 128), 0, b - a)
             mm([(o, sub(x0, a, b), I)])
-            act(xt, o, ACT.Copy)
-            x0T.append(xt)
+            move(xt, o)
+            x0T += [part(xt, q, q + 32) for q in range(0, b - a, 32)]
         for eng, a, b in FOLD:
+            ahead(a * len(PARTS) // NS if eng == "v" else None)
             for j in range(16):
                 o = sub(XE, 16 * a + j, 16 * b, 16)
                 if eng == "g":
                     asel(o, sub(x0, a, b), [[0, b - a]], ALU.is_ge, 0, 0)
                 else:
-                    copy(o, sub(x0, a, b))
+                    move(o, sub(x0, a, b), first="v")
+        ahead(None)
         if t == 0:
             message(sub(PRE[t], 0, 208), sub(PRR[t], 0, 208), t, 1)
         else:
             message(PRE[t], PRR[t], t, 1)
-        hb2, sh, h3w = new("h", NS), new("f", NS), new("h", 193)
+        sh = new("f", NS)
         nf1, nf2, u1, u2 = new("b", 204), new("b", 204), new("f", 204), new("f", 204)
         e1u, e2u, h2u = new("u", 12), new("u", 12), new("u", 12)
         ge1, ge2, vb2 = new("b", NS), new("b", NS), new("b", NS)
-        memset(sub(h3w, NS, 193), 0.0)
         d2 = []
         for h in range(len(PARTS)):
+            ahead(h)
             distances(1, h, L1u, x0T)
         for h, (a, b) in enumerate(PARTS):
+            ahead(h)
             pick(a, b, d1[h], w16_(nf1, a, b, 17), w16_(u1, a, b, 17), w16_(e1u, a, b, 1), BE)
-            gather("v", sub(hb2, a, b), Wg, w16_(e1u, a, b, 1))
+            gather("w", sub(hb2, a, b), Wg, w16_(e1u, a, b, 1))
             wrap(sub(hb2, a, b), MH, B, sub(sh, a, b), w16_(h2u, a, b, 1))
-            gather("v", sub(L2u, a, b), HLs, w16_(h2u, a, b, 1))
+            if t and VIA:
+                gather("v", sub(L2u, a, b), LW, w16_(e1u, a, b, 1))
+            else:
+                gather("v", sub(L2u, a, b), HLs, w16_(h2u, a, b, 1))
             copy(sub(L2h, a, b), sub(L2u, a, b))
             d2.append(steps(sub(L2h, a, b), 12 + a // 16, drow[0]))
             distances(2, h, L2u, x0T)
-        gtt(ge1, Xg, e1u, dm, ALU.is_ge)
-        cp = sub(M0, 0, NS)
-        mm([(cp, blk, ge1), (cp, I2k, ns1)])
-        dead1 = new("b", NS)
-        ts(dead1, cp, need, ALU.is_ge)
-        hm = sub(M1, 256, 256 + NS)
-        mm([(hm, I, hb2), (hm, I2k, dead1)])
-        hm = wrap(hm, MH, None)[0]
-        gather("a", vb2, Vg, h2u, ACT.Relu, vbias)
-        ns2 = dedupe(hb2, hm, vb2, dead1)
+        ahead(None)
+        dead1, hm = new("b", NS), new("f", NS)
+        for a, b in JUDGE[0]:
+            gtt(sub(ge1, a, b), Xg, w16_(e1u, a, b, 1), sub(dm, a, b), ALU.is_ge)
+            cp, hp = sub(M0, a, b), sub(M0, 256 + a, 256 + b)
+            mm([(cp, I2k, sub(ns1, a, b)), (cp, blk, sub(ge1, a, b))])
+            ts(sub(dead1, a, b), cp, need, ALU.is_ge)
+            mm([(hp, one1, sub(brow, a, b)), (hp, I, sub(hb2, a, b)), (hp, I2k, sub(dead1, a, b))])
+            wrap(hp, MH, None, sub(hm, a, b))
+        gather("a", vb2, Vg, h2u, vbias)
+        ns2 = dedupe(hb2, lambda c: sub(hm, 16 * c + 15, 16 * c + 16), vb2, dead1, JUDGE[1])
         failed, pos, m2n, paid = new("b", NS), new("b", NS), new("b", NS), new("b", NS)
         e1b, e2b, tw2 = new("h", NS), new("h", NS), new("f", 24)
         gather("a", e1b, FT, e1u)
@@ -492,11 +549,11 @@ def plan():
             n, k = b - a, (b - a) // 16
             Lf, ohs, Tl, offL = new("f", 3 * n), new("b", 3 * n), new("f", 3 * n), new("u", 3 * k)
             gather("a", sub(e2b, a, b), FT, w16_(e2u, a, b, 1))
-            ts(sub(ohs, 0, n), sub(ones, 0, n), sub(rm, t, t + 1), ALU.mult)
+            move(sub(ohs, 0, n), sub(ones, 0, n), sub(rm, t, t + 1))
             gather("a", sub(ohs, n, 2 * n), rm, w16_(j1u, a, b, 1))
             gather("a", sub(ohs, 2 * n, 3 * n), rm, slots(w16_(nf2, a, b, 17)))
             for i, Lh in enumerate((L0h, L1h, L2h)):
-                act(sub(Lf, n * i, n * i + n), sub(Lh, a, b), ACT.Copy)
+                move(sub(Lf, n * i, n * i + n), sub(Lh, a, b))
             cn, cq = sub(M1, 0, n), sub(M1, n, 2 * n)
             g2, n2 = sub(ge2, a, b), sub(ns2, a, b)
             mm([(cn, nI2k, n2), (cn, blk, g2)])
@@ -524,6 +581,7 @@ def plan():
 
         for h, (a, b) in enumerate(PARTS):
             pick(a, b, d2[h], w16_(nf2, a, b, 17), w16_(u2, a, b, 17), w16_(e2u, a, b, 1), BE)
+        for a, b in JUDGE[1]:
             gtt(sub(ge2, a, b), Xg, w16_(e2u, a, b, 1), sub(dm, a, b), ALU.is_ge)
             gather("a", sub(h3w, a, b), Wg, w16_(e2u, a, b, 1))
             cp = sub(M0, a, b)
@@ -535,14 +593,20 @@ def plan():
                     pay(pa, pb)
         mAs, mAr, acc = new("u", 8), new("u", 8), new("f", 2)
         memset(mAs, 0)
-        dh = sub(BK[0], 0, NS)
-        mm([(dh, I, sub(h3w, 0, NS)), (dh, nI, sub(h3w, 1, 193))])
-        act(sub(DH, 1, 193), dh, ACT.Copy)
+        cut = PARTS[-1][0]
+        for a, b in ((0, cut), (cut, 193)):
+            lo = max(a, 1)
+            dh = sub(BK[0], lo, b)
+            mm([(dh, I, sub(h3w, lo - 1, b - 1)), (dh, nI, sub(h3w, lo, b))])
+            move(sub(DH, lo, b), dh)
+            for c in range(2):
+                e = min(b, NS)
+                ts(sub(NFH, 208 * c + lo, 208 * c + e), sub(pos, lo - 1, e - 1), sub(kcol, c, c + 1), ALU.is_gt)
+            for c in range(2):
+                scan(sub(UH, 208 * c + a, 208 * c + b), sub(DH, a, b), sub(NFH, 208 * c + a, 208 * c + b),
+                     sub(UH, 208 * c + a - 1, 208 * c + a) if a else 0.0, ALU.add, ALU.mult)
         for c in range(2):
-            ts(sub(NFH, 208 * c + 1, 208 * c + NS), sub(pos, 0, NS - 1), sub(kcol, c, c + 1), ALU.is_gt)
             act(sub(junk, NS * c, NS * c + NS), pos, ACT.Sign, bias=sub(kcol, c, c + 1), scale=-1.0, acc=sub(acc, c, c + 1))
-        for c in range(2):
-            scan(sub(UH, 208 * c, 208 * c + 193), DH, sub(NFH, 208 * c, 208 * c + 193), 0.0, ALU.add, ALU.mult)
         sidx = sub(mAs, 2, 4)
         ts(sidx, acc, 0.5, ALU.mult, 96.0, ALU.add)
         copy(sub(mAs, 0, 2), sub(UH, 192, 416, 208))
@@ -554,11 +618,14 @@ def plan():
         ts(sub(mBs, 0, 2), esc, BE + B, ALU.add)
         message(mBs, mBr, t, 3)
         pay(*PAY[-1])
-        tc, offo, offW = new("f", 2), new("u", 2), new("u", 24)
+        tc, offo = new("f", 2), new("u", 2)
         tt(tc, esc, C4, ALU.min)
         ts(offo, tc, BE, ALU.add)
         scatter(FT, offo, own)
+        offW = new("u", 24)
         ts(offW, tw2, BE, ALU.add)
+        for n in range(2):
+            scatter(W, sub(offW, 12 * n, 12 * n + 12), sub(hbb, NS * n, NS * n + NS))
         h3u, su = sub(mAr, 0, 2), sub(mAr, 2, 4)
         x0m, dmm = new("b", 32), new("b", 32)
         Lxu, Lxh = new("u", 32), new("h", 32)
@@ -568,10 +635,10 @@ def plan():
         gather("a", dmm, sub(PRR[t], 208, 416), su)
         if t == RO - 1:
             dma("s", lambda E, A, T: E.dma_start(T.yl[:], A(HLg)), [HLg], [], 393216)
+            dma("s", lambda E, A, T: E.dma_start(T.yw[:], T.af[0:128:16, W[1]:W[1] + NP]), [Wg], [], 65536)
         nv = 16 * XSPLIT
         xb = BK[0]
-        mm([(xb, one1, zrow)])
-        ops[-1]["fn"] = lambda E, A, xb=xb: E.matmul(A(xb), A(one1), A(zrow), True, False)
+        mm([(xb, one1, zrow)], last=False)
         mm([(sub(xb, j, 512, 16), nI, x0m) for j in range(16)], first=False, last=False)
         gather("v", sub(Ag, 0, nv), Xg, sub(Lxu, 0, XSPLIT))
         gather("a", sub(Ag, nv, 512), Xg, sub(Lxu, XSPLIT, 32))
@@ -581,7 +648,7 @@ def plan():
         pick(0, 32, steps(Lxh, 24, drow[1]), nfx, ux, fu, -B)
         fall, mCs, mCr = new("f", 32), new("b", 32), new("b", 32)
         gtt(sub(gex, 0, 32), Xg, fu, dmm, ALU.is_ge)
-        gather("a", fall, FT, fu, ACT.Relu, B)
+        gather("a", fall, FT, fu, B)
         gather("a", mCs, Xg, fu)
         message(mCs, mCr, t, 4)
         pv, flag, fin = sub(KB[turn["k"] % 2], 0, 66), new("b", 66), new("f", 66)
@@ -599,11 +666,7 @@ def plan():
         for c in range(2):
             ts(sub(offb, c, c + 1), sub(fin, 33 * c + 32, 33 * c + 33), sub(ux, 17 * c + 16, 17 * c + 17), ALU.add, sub(SP, c, c + 1), ALU.min)
         scatter(X, offb, x0m)
-        scatter(W, sub(offW, 0, 12), hb2)
-        scatter(W, sub(offW, 12, 24), hb1)
-        if t == RO - 1:
-            dma("s", lambda E, A, T: E.dma_start(T.yw[:], T.af[0:128:16, W[1]:W[1] + NP]), [Wg], [], 65536)
-        else:
+        if t < RO - 1:
             scatter(FT, offo, e0c)
             pc = sub(M0, 256, 256 + NS)
             mm([(pc, o16, paid)])
@@ -634,7 +697,7 @@ def depend(ops):
         deps = set()
         for key, lo, hi, wr, st in acc:
             for (m, l2, h2, w2, s2) in log.get(key, []):
-                clash = wr or w2 or (key[0][0] == "p" and ops[m]["eng"] != op["eng"])
+                clash = wr or w2 or (key[0][0] == "p" and (ops[m]["eng"] != op["eng"] or "alt" in op or "alt" in ops[m]))
                 if l2 < hi and lo < h2 and clash and m != n and not (st == s2 and st and (lo - l2) % st):
                     deps.add(m)
         op["soft"] = {m for m in deps if ops[m]["eng"] == op["eng"] == "t" or ops[m]["kind"] == op["kind"] == "send"}
@@ -648,105 +711,218 @@ def depend(ops):
 
 def schedule(ops, seed, jitter):
     n = len(ops)
-    dur, occ, bus = [0] * n, [0] * n, 1900
+    dur0, occ0, bus = [0] * n, [0] * n, 1900
     for i, op in enumerate(ops):
         if op["kind"] == "dma":
             bus = (bus if not op["deps"] else 1900) + op["cost"] // 200
-            dur[i], occ[i] = bus, 60
+            dur0[i], occ0[i] = bus, 60
         else:
-            dur[i], occ[i] = op["cost"], 0 if op["eng"] == "x" else op["cost"]
-    pred = [[(d, 0 if d in op["soft"] else HOP) for d in op["deps"]] for op in ops]
+            dur0[i], occ0[i] = op["cost"], 0 if op["eng"] == "x" else op["cost"]
+    pred, above = [], []
+    for op in ops:
+        cover = 0
+        for d in op["deps"]:
+            cover |= above[d]
+        pred.append([(d, 0 if d in op["soft"] else HOP) for d in op["deps"] if not cover >> d & 1])
+        for d in op["deps"]:
+            cover |= 1 << d
+        above.append(cover)
     loads = [i for i, op in enumerate(ops) if op["eng"] == "s" and not op["deps"]]
     for a, b in zip(loads, loads[1:]):
-        pred[b].append((a, occ[a] - dur[a]))
+        pred[b].append((a, occ0[a] - dur0[a]))
     succ = [[] for _ in ops]
     for i in range(n):
         for d, h in pred[i]:
             succ[d].append((i, h))
+    alt = [{e: c for e, (fn, c) in op["alt"].items()} if "alt" in op else None for op in ops]
+    slack = [dur0[i] - occ0[i] for i in range(n)]
+    r = [seed]
 
-    def place(rank, before, after, back):
-        left = [len(b) for b in before]
-        ready = sorted((rank[i], i) for i in range(n) if left[i] == 0)
-        busy = {e: [] for e in "vatgsx"}
-        start = [0] * n
+    def rnd(m):
+        r[0] = (r[0] * 1103515245 + 12345) % 2147483648
+        return (r[0] >> 8) % m
+
+    def gap(lst, at, need):
+        k, hi = 0, len(lst)
+        m = hi
+        while k < hi:
+            mid = (k + hi) // 2
+            if lst[mid][1] <= at:
+                k = mid + 1
+            else:
+                hi = mid
+        while k < m and at + need > lst[k][0]:
+            at = lst[k][1]
+            k += 1
+        return k, at
+
+    def place(stretch, rank, eng, free=()):
+        inside, before, after, head, busy0, back = stretch
+        left = {i: len(before[i]) for i in inside}
+        ready = sorted((rank[i], i) for i in inside if not left[i])
+        busy = {e: list(b) for e, b in busy0.items()}
+        start, fin, eng = {}, {}, dict(eng)
         while ready:
             i = ready.pop(0)[1]
-            t = max([0] + [start[d] + dur[d] + h for d, h in before[i]])
-            lead = dur[i] - occ[i] if back else 0
-            if occ[i]:
-                lst, k = busy[ops[i]["eng"]], 0
-                for a, b in lst:
-                    if t + lead + occ[i] <= a:
-                        break
-                    t = max(t, b - lead)
-                    k += 1
-                lst.insert(k, (t + lead, t + lead + occ[i]))
-            start[i] = t
+            t = head[i]
+            for d, h in before[i]:
+                if fin[d] + h > t:
+                    t = fin[d] + h
+            if alt[i]:
+                if i in free:
+                    eng[i] = min("va", key=lambda e: gap(busy[e], t, alt[i][e])[1] + alt[i][e])
+                d = occ = alt[i][eng[i]]
+            else:
+                d, occ = dur0[i], occ0[i]
+            if occ:
+                lead = slack[i] if back else 0
+                lst = busy[eng[i]]
+                k, at = gap(lst, t + lead, occ)
+                t = at - lead
+                lst.insert(k, (at, at + occ))
+            start[i], fin[i] = t, t + d
             for s, h in after[i]:
                 left[s] -= 1
                 if left[s] == 0:
                     ready.append((rank[s], s))
                     ready.sort()
-        return start
+        return start, fin, eng
 
-    def replay(order, hop, fly, slow):
-        fin, free = [0] * n, {e: 0 for e in "vatgsx"}
+    every = list(range(n))
+    none = {e: [] for e in "vatgsx"}
+    whole = (every, pred, succ, [0] * n, none, False)
+    turned = (every, succ, pred, [0] * n, none, True)
+
+    def improve(now, t0, t1, passes):
+        st0, fin0, eng0 = now
+        order = sorted(every, key=lambda i: (st0[i], i))
+        inside = [i for i in order if t0 <= st0[i] < t1]
+        here = set(inside)
+        far, nxt, tail = {}, {}, {}
+        for i in reversed(order):
+            if st0[i] >= t1:
+                e = eng0[i]
+                far[i] = max([fin0[i] - st0[i] + max([h + far[s] for s, h in succ[i]] + [0])]
+                             + ([fin0[i] - st0[i] - slack[i] + far[nxt[e]]] if e in nxt and e != "x" else []))
+                nxt[e] = i
+        before = {i: [(d, h) for d, h in pred[i] if d in here] for i in inside}
+        after = {i: [(s, h) for s, h in succ[i] if s in here] for i in inside}
+        head = {i: max([fin0[d] + h for d, h in pred[i] if d not in here] + [0]) for i in inside}
+        for i in inside:
+            tail[i] = max([h + far[s] for s, h in succ[i] if s in far] + [0])
+        queue = {e: far[nxt[e]] if e in nxt and e != "x" else 0 for e in "vatgsx"}
+        busy = {e: [] for e in "vatgsx"}
         for i in order:
-            e = ops[i]["eng"]
-            t = max([free[e]] + [fin[d] + (hop if h == HOP else h) for d, h in pred[i]])
-            fin[i] = t + (dur[i] + fly - FLY if e == "x" else dur[i] * slow if ops[i]["extra"] == "index" else dur[i])
-            free[e] = fin[i] if occ[i] == dur[i] else t + occ[i]
-        return max(fin)
+            if st0[i] < t0 and eng0[i] != "x":
+                busy[eng0[i]].append((st0[i], fin0[i] - slack[i]))
+        for e in busy:
+            busy[e] = busy[e][-40:]
+            if busy[e]:
+                busy[e].insert(0, (-1, busy[e][0][0]))
+        ends0 = {(e, b): -1 for e in busy for a, b in busy[e]}
+        stretch = (inside, before, after, head, busy, False)
+        flex = [i for i in inside if alt[i]]
 
-    def score(start, bound=None):
-        span = max(start[i] + dur[i] for i in range(n))
-        if bound is not None and span > bound + 900:
-            return None
-        order = sorted(range(n), key=lambda i: (start[i], i))
-        return (span + sum(replay(order, *c) for c in CASES)) / (1.0 + len(CASES)) + sum(start) / (20.0 * n), span
-
-    prio, r = [0] * n, [seed]
-
-    def rnd(m):
-        r[0] = (r[0] * 1103515245 + 12345) % 2147483648
-        return (r[0] >> 8) % m
-    for i in range(n - 1, -1, -1):
-        prio[i] = dur[i] + max([prio[s] + h for s, h in succ[i]] + [0])
-    start = place([-p for p in prio], pred, succ, False)
-    best = (score(start), start)
-    for it in range(PASSES):
-        if it % 50 < 2:
-            back = place([-(best[1][i] + dur[i]) for i in range(n)], succ, pred, True)
-            rank = [-(back[i] + dur[i]) + rnd(jitter + 1) for i in range(n)]
-        elif it % 3:
-            st = best[1]
-            ends = {(ops[i]["eng"], st[i] + occ[i]): i for i in range(n) if occ[i]}
-            i, held = max(range(n), key=lambda c: st[c] + dur[c]), []
-            while st[i] > 0:
-                tight = [d for d, h in pred[i] if st[d] + dur[d] + h == st[i]]
-                if tight:
-                    i = tight[rnd(len(tight))]
-                else:
-                    p = ends[ops[i]["eng"], st[i]]
-                    held.append((p, i))
-                    i = p
-            rank = list(st)
-            for _ in range(1 + rnd(2)):
-                p, i = held[rnd(len(held))]
+        def score(x):
+            st, fin, eng = x
+            top, last = 0, -1
+            for i in inside:
+                v = max(fin[i] + tail[i], fin[i] - slack[i] + queue[eng[i]])
+                if v > top:
+                    top, last = v, i
+            return top + sum(st.values()) / (20.0 * n), last
+        x = ({i: st0[i] for i in inside}, {i: fin0[i] for i in inside}, {i: eng0[i] for i in inside})
+        top = best = (score(x), x)
+        for it in range(passes):
+            st, fin, eng = best[1]
+            free, held, rank = (), [], dict(st)
+            if it % 3:
+                ends = dict(ends0)
+                for i in inside:
+                    ends[eng[i], fin[i] - slack[i]] = i
+                i = best[0][1]
+                while st[i] > head[i]:
+                    tight = [d for d, h in before[i] if fin[d] + h == st[i]]
+                    if tight:
+                        i = tight[rnd(len(tight))]
+                    else:
+                        p = ends[eng[i], st[i]]
+                        if p < 0:
+                            break
+                        held.append((p, i))
+                        i = p
+            if held:
+                for _ in range(1 + rnd(2)):
+                    p, i = held[rnd(len(held))]
+                    how = rnd(5)
+                    if how == 0:
+                        rank[p] = st[i] + 1 + rnd(600)
+                    elif how == 1:
+                        rank[i] = st[p] - 1 - rnd(600)
+                    elif how == 4:
+                        near = [c for c in flex if eng[c] == eng[i] and st[i] - 3000 < st[c] <= st[i]]
+                        if near:
+                            c = near[rnd(len(near))]
+                            eng = dict(eng)
+                            eng[c] = "v" if eng[c] == "a" else "a"
+                    else:
+                        todo, gain, reach = [i if how == 2 else p], 100 + rnd(1500), st[p] - 500 - rnd(6000)
+                        seen = set(todo)
+                        while todo:
+                            c = todo.pop()
+                            rank[c] -= gain
+                            for d, h in before[c]:
+                                if d not in seen and st[d] > reach:
+                                    seen.add(d)
+                                    todo.append(d)
+            else:
+                mid, wide, amp = t0 + rnd(t1 - t0), 500 + rnd(4000), 200 + rnd(2500)
+                for i in inside:
+                    if abs(st[i] - mid) < wide and rnd(4) == 0:
+                        rank[i] += rnd(amp)
                 if rnd(2):
-                    rank[p] = st[i] + 1 + rnd(600)
-                else:
-                    rank[i] = st[p] - 1 - rnd(600)
-        else:
-            mid, wide, amp = rnd(int(best[0][1])), 1000 + rnd(5000), 200 + rnd(2500)
-            rank = [b + (rnd(amp) if abs(b - mid) < wide and rnd(4) == 0 else 0) for b in best[1]]
-        start = place(rank, pred, succ, False)
-        sc = score(start, best[0][1])
-        if sc is not None and sc[0] <= best[0][0]:
-            best = (sc, start)
-    start = best[1]
-    order = sorted(range(n), key=lambda i: (start[i], i))
-    return order, start, [start[i] + dur[i] for i in range(n)]
+                    free = {c for c in flex if abs(st[c] - mid) < wide and rnd(3) == 0}
+            x = place(stretch, rank, eng, free)
+            sc = score(x)
+            if sc[0] <= best[0][0] + SLACK * (1.0 - it / passes):
+                best = (sc, x)
+                if sc[0] < top[0][0]:
+                    top = best
+        rank, eng = dict(st0), dict(eng0)
+        rank.update(top[1][0])
+        for i in far:
+            rank[i] += 100000
+        eng.update(top[1][2])
+        return place(whole, rank, eng)
+
+    def span(x):
+        return max(x[1].values())
+
+    def turn(x, rounds):
+        for _ in range(rounds):
+            back = place(turned, {i: -f for i, f in x[1].items()}, x[2])[1]
+            y = place(whole, {i: -b + rnd(jitter + 1) for i, b in back.items()}, x[2])
+            if span(y) < span(x):
+                x = y
+        return x
+    prio = [0] * n
+    for i in range(n - 1, -1, -1):
+        prio[i] = dur0[i] + max([prio[s] + h for s, h in succ[i]] + [0])
+    now = turn(place(whole, [-p - op["lead"] for p, op in zip(prio, ops)], {i: op["eng"] for i, op in enumerate(ops)}), 30)
+    for sweep in range(SWEEPS):
+        t0 = -(sweep % 2) * (WIDE // 4)
+        while t0 < span(now) - 8000:
+            x = improve(now, max(t0, 0), t0 + WIDE, PASSES)
+            if span(x) <= span(now) + 30:
+                now = x
+            t0 += WIDE // 2
+        now = turn(now, 10)
+    start, fin, eng = now
+    for i in every:
+        if alt[i]:
+            ops[i]["eng"] = eng[i]
+            ops[i]["fn"], ops[i]["cost"] = ops[i]["alt"][eng[i]]
+    return sorted(every, key=lambda i: (start[i], i)), [start[i] for i in every], [fin[i] for i in every]
 
 
 def signals(ops, order):
@@ -802,7 +978,7 @@ ORDER, START, FIN = schedule(OPS, SEED, JITTER)
 TOKEN, WAITS, USED, VAL, NDMA = signals(OPS, ORDER)
 
 SCRATCH = {ARENA[k][0]: ("sbuf", [128, SIZE[k]], ARENA[k][1]) for k in ARENA}
-SCRATCH["ab3"] = ("sbuf", [128, NS, 17], "bfloat16")
+SCRATCH["ab3"] = ("sbuf", [128, NS, 17], "float16")
 SCRATCH["tt3"] = ("sbuf", [128, 26, 16], "float16")
 for _k in range(7):
     SCRATCH["p%d" % _k] = ("psum", [128, 512], "float32")

from concourse.mybir import AluOpType, AxisListType, ActivationFunctionType

ALU = AluOpType
ACT = ActivationFunctionType
NP, NH, NS, RO, CAP = 2048, 768, 192, 2, 32
B = 4096.0
BE = 5184.0
HOP = 240
PE = 2.0
FLY = 3000
PARTS = ((0, 64), (64, 128), (128, 192))
PIECES = {(1, 0): "w32 w32", (1, 1): "v32 m32", (1, 2): "v32 w32", (2, 0): "v32 w32", (2, 1): "v32 m32", (2, 2): "v32 w16 m16"}
FOLD = (("g", 0, 32), ("v", 64, 160))
PAY = ((0, 128), (128, 192))
SLACK = 100
OPEN = (((0, 64), (64, 192)), ((0, 192),))
JUDGE = (((0, 128), (128, 192)), ((0, 128), (128, 192)))
TURN = ((0, 64), (64, 192))
VIA = True
LEAD = 0
XSPLIT = 16
SWEEPS, WIDE = 6, 10000
SEED, JITTER, PASSES = 4, 200, 1500
ARENA = {"f": ("af", "float32"), "b": ("ab", "bfloat16"), "h": ("ah", "float16"), "u": ("au", "uint16"), "i": ("ai", "int32")}
BACK = (4, 5)


def sub(v, a, b, step=1, p0=None, p1=None):
    return (v[0], v[1] + a, v[1] + b, step, v[4] if p0 is None else p0, v[5] if p1 is None else p1)


def part(v, p0, p1):
    return (v[0], v[1], v[2], v[3], p0, p1)


def grid(name, row, a, b, step, c0, c1):
    return (name, row * a, row * b, 0, 0, 128, (slice(a, b, step), slice(c0, c1)), (b - a + step - 1) // step * (c1 - c0))


def width(v):
    return v[7] if len(v) > 6 else (v[2] - v[1] + v[3] - 1) // v[3]


def is_ps(v):
    return v[0][0] == "p"


def plan():
    ops, lead = [], [0]
    size = {k: 0 for k in ARENA}

    def ahead(h):
        lead[0] = 0 if h is None else LEAD * (len(PARTS) - 1 - h)

    def new(k, n):
        lo = size[k]
        size[k] = lo + (n + 15) // 16 * 16
        return (ARENA[k][0], lo, lo + n, 1, 0, 128)

    def two(*vs):
        return all(v[0] in ("ab", "ah", "au", "ab3", "tt3") for v in vs)

    def add(eng, fn, r, w, cost, kind="c", extra=None):
        r = [v for v in r if isinstance(v, tuple)]
        ops.append({"eng": eng, "fn": fn, "r": r, "w": list(w), "cost": cost, "kind": kind, "extra": extra, "lead": lead[0]})

    def either(first):
        a, v = ops.pop(), ops[-1]
        v["alt"] = {"v": (v["fn"], v["cost"]), "a": (a["fn"], a["cost"])}
        v["r"] = v["r"] + [x for x in a["r"] if x not in v["r"]]
        v["eng"] = first
        v["fn"], v["cost"] = v["alt"][first]

    def S(A, s):
        return A(s) if isinstance(s, tuple) else s

    def vcost(n, half):
        return max(64, n // 2 if half else n)

    def memset(o, c):
        add("v", lambda E, A: E.memset(A(o), c), [], [o], vcost(width(o), two(o)))

    def copy(o, i):
        add("v", lambda E, A: E.tensor_copy(A(o), A(i)), [i], [o], vcost(width(o), two(o, i)))

    def ts(o, i, s1, op0, s2=None, op1=None):
        if op1 is None:
            fn = lambda E, A: E.tensor_scalar(A(o), A(i), S(A, s1), None, op0)
        else:
            fn = lambda E, A: E.tensor_scalar(A(o), A(i), S(A, s1), S(A, s2), op0, op1)
        add("v", fn, [i, s1, s2], [o], vcost(width(o), two(o, i)))

    def tt(o, a, b, op):
        n = width(o) * (1 if is_ps(a) or is_ps(b) else 2)
        add("v", lambda E, A: E.tensor_tensor(A(o), A(a), A(b), op), [a, b], [o], max(64, n))

    def scan(o, d0, d1, init, op0, op1):
        add("v", lambda E, A: E.tensor_tensor_scan(A(o), A(d0), A(d1), S(A, init), op0, op1), [d0, d1, init], [o],
            vcost(width(o), two(o, d0, d1)))

    def act(o, i, f, bias=None, scale=None, acc=None):
        def fn(E, A):
            kw = {}
            if bias is not None:
                kw["bias"] = S(A, bias)
            if scale is not None:
                kw["scale"] = S(A, scale)
            if acc is not None:
                kw["accum_out"] = A(acc)
            return E.activation(A(o), A(i), f, **kw)
        add("a", fn, [i, bias, scale], [o] + ([acc] if acc else []), max(64, width(o)) + 30)

    def move(o, i, scale=None, first="a"):
        if scale is None:
            copy(o, i)
        else:
            ts(o, i, scale, ALU.mult)
        act(o, i, ACT.Copy, scale=scale)
        either(first)

    def gcost(n):
        return 60 + int(1.56 * n)

    def gather(eng, o, win, off, bias=None):
        if bias is None:
            fv = lambda E, A: E.tensor_copy(A(o), A(win).indirect(A(off)))
            fa = lambda E, A: E.activation(A(o), A(win).indirect(A(off)), ACT.Copy)
        else:
            fv = lambda E, A: E.tensor_scalar(A(o), A(win).indirect(A(off)), bias, 0.0, ALU.add, ALU.max)
            fa = lambda E, A: E.activation(A(o), A(win).indirect(A(off)), ACT.Relu, bias=bias)
        add("v", fv, [win, off], [o], gcost(width(o)), extra="index")
        if eng != "v":
            add("a", fa, [win, off], [o], gcost(width(o)) + 18, extra="index")
            either("a" if eng == "a" else "v")

    def gtt(o, win, off, b, op):
        add("v", lambda E, A: E.tensor_tensor(A(o), A(win).indirect(A(off)), A(b), op), [win, off, b], [o], gcost(width(o)), extra="index")

    def scatter(win, off, i, b=None):
        if b is None:
            fn = lambda E, A: E.tensor_copy(A(win).indirect(A(off)), A(i))
        else:
            fn = lambda E, A: E.tensor_tensor(A(win).indirect(A(off)), A(i), A(b), ALU.add)
        add("v", fn, [off, i, b], [win], 60 + int(3.8 * width(i)), extra="index")

    def mark(win, off, i):
        scatter(win, off, i)
        add("a", lambda E, A: E.activation(A(win).indirect(A(off)), A(i), ACT.Tanh), [off, i], [win], 80 + int(3.8 * width(i)), extra="index")
        either("a")

    def mm(items, first=True, last=True, each=0):
        def fn(E, A):
            ins = None
            for n, (o, l, r) in enumerate(items):
                if each:
                    st, sp = n % each == 0, n % each == each - 1
                else:
                    st, sp = first and n == 0, last and n == len(items) - 1
                ins = E.matmul(A(o), A(l), A(r), st, sp)
            return ins
        c = int(sum(max(min(64, width(l)), width(r)) for o, l, r in items) / PE) + 40
        add("t", fn, [x for o, l, r in items for x in (l, r)], [o for o, l, r in items], c)

    def iota(o, pat, base, cm):
        if o[0] == "ai":
            fn = lambda E, A: E.iota(A(o), pat, base, cm)
        else:
            fn = lambda E, A: E.iota(A(o), pat, base, cm, allow_small_or_imprecise_dtypes=True)
        add("g", fn, [], [o], 150 + 2 * width(o))

    def asel(o, i, pat, op, base, cm):
        add("g", lambda E, A: E.affine_select(A(o), A(i), pat, op, 0.0, base, cm), [i], [o], 200 + 2 * width(o))

    def dma(eng, fn, r, w, nbytes):
        add(eng, fn, r, w, nbytes, kind="dma")

    sent = []

    def message(src, dst, t, k):
        tok = ("msg", len(sent), len(sent) + 1, 1, 0, 128)
        add("g", None, [src, ("msg", 0, 1, 1, 0, 128) if len(sent) == 1 else None], [tok], 500 if sent else 3000, kind="send",
            extra=(src, dst, t, k))
        add("x", None, [tok], [dst], FLY + 2 * width(src), kind="recv", extra=(t, k))
        sent.append((t, k))

    BK = [("p%d" % k, 0, 512, 1, 0, 128) for k in range(3)]
    KB = [("p%d" % k, 0, 512, 1, 0, 128) for k in (3, 4)]
    M0, M1 = [("p%d" % k, 0, 512, 1, 0, 128) for k in (5, 6)]
    turn = {"s": 0, "k": 0}

    ho32, wr32, hl32 = new("i", 24), part(new("i", 512), 0, 32), new("i", NH)
    X = new("b", NP + 64)
    PRE, PRR = [new("b", 416) for t in range(RO)], [new("b", 416) for t in range(RO)]
    HL, W, V, FT = new("f", 1152), new("f", NP + NS), new("f", NH + NS), new("f", NP + 64)
    Xg, HLg, Wg, Vg = sub(X, 0, NP), sub(HL, 0, NH), sub(W, 0, NP), sub(V, 0, NH)
    dma("s", lambda E, A, T: E.dma_start(A(wr32), T.wr[:]), [], [wr32], 65536)
    dma("a", lambda E, A, T: E.dma_start(A(ho32), T.ho[:]), [], [ho32], 12288)
    dma("s", lambda E, A, T: E.dma_start(A(hl32), T.hl[:]), [], [hl32], 393216)
    dma("s", lambda E, A, T: E.dma_start(A(Xg), T.xs[:]), [], [Xg], 524288)
    for t in range(RO):
        o = sub(PRE[t], 208, 208 + NS)
        dma("s", lambda E, A, T, o=o, t=t: E.dma_start(A(o), T.dm[:, NS * t:NS * (t + 1)]), [], [o], 49152)
        memset(sub(PRE[t], 400, 416), 512.0)
        memset(sub(PRE[t], NS, 208), 0.0)
    message(sub(PRE[0], 208, 416), sub(PRR[0], 208, 416), 0, 0)

    ones = new("b", 512)
    memset(ones, 1.0)
    o128 = sub(ones, 0, 128)

    def fill(o, c):
        memset(o, float(c))
        act(o, sub(ones, 0, width(o)), ACT.Copy, scale=float(c))
        either("a")

    def scaled(m, c):
        o = new("b", width(m))
        move(o, m, c)
        return o
    kg, qb, kc = new("b", 128), new("b", NS), new("b", 128)
    iota(kg, [[-16, 8], [0, 16]], 0, 1)
    iota(qb, [[0, 12], [1, 16]], 0, 0)
    pid, pmi, pm = new("i", 1), new("i", 1), new("f", 1)
    iota(pid, [[0, 1]], 0, 1)
    selW = part(new("b", 512), 0, 32)
    asel(selW, part(ones, 0, 32), [[-1, 4], [-4, 8], [0, 16]], ALU.is_equal, 0, 1)
    rs = [new("b", 128) for t in range(RO)]
    Ipad, blk, c16, kb = new("b", 160), new("b", 128), new("f", 16), new("b", 32)
    asel(Ipad, sub(ones, 0, 160), [[-1, 160]], ALU.is_equal, 16, 1)
    I = sub(Ipad, 16, 144)
    for t in range(RO):
        ts(rs[t], kg, float(t), ALU.is_equal)
    ts(kc, kg, 0.0, ALU.max, 15.0, ALU.min)
    tt(blk, kg, kc, ALU.is_equal)
    ts(c16, sub(qb, 0, 16), 16.0, ALU.mult)
    copy(sub(kb, 0, 16), sub(qb, 0, 16))
    ts(sub(kb, 16, 32), sub(qb, 0, 16), 16.0, ALU.add)
    ts(pmi, pid, 15, ALU.bitwise_and)
    copy(pm, pmi)
    ho16 = new("u", 24)
    copy(ho16, ho32)
    MH, ME, mt, mt2 = new("f", NS), new("f", NS), new("b", NS), new("b", NS)
    ts(mt2, qb, pm, ALU.is_lt, -B, ALU.mult)
    ts(mt, qb, pm, ALU.is_equal, B, ALU.mult)
    tt(ME, mt2, mt, ALU.add)
    move(MH, ME)
    ts(sub(MH, 15, NS, 16), sub(MH, 15, NS, 16), -2 * B, ALU.add)
    ts(sub(ME, 15, NS, 16), sub(ME, 15, NS, 16), -B - BE, ALU.add)
    wr16 = part(new("h", 512), 0, 32)
    copy(wr16, wr32)
    for q, bank in enumerate(BK + KB[:1]):
        mm([(bank, sub(selW, 128 * q, 128 * q + 128), wr16)])
        if q == 0:
            act(sub(V, 0, 480), sub(ones, 0, 480), ACT.Tanh, scale=0.0)
            ops[-1]["cost"] += 1600
        move(sub(W, 512 * q, 512 * q + 512), bank)
        ops[-1]["r"].append(sub(V, 0, 1))
    copy(HLg, hl32)
    fill(sub(V, 480, 960), 0)
    fill(sub(HL, NH, 1152), 0)
    fill(sub(W, NP, NP + NS), 0)
    fill(sub(X, NP, NP + 64), 0)
    tin = [new("f", NS) for t in range(RO)]
    fill(tin[0], 0.5)
    fill(tin[1], 4)
    nI, bigI = scaled(I, -1.0), new("b", 128)
    I2k, nI2k, I3k = scaled(I, 2048.0), scaled(I, -2048.0), scaled(I, 3072.0)
    ts(bigI, I, 2.0 ** 60, ALU.mult, 2.0 ** 60, ALU.mult)
    nblk = scaled(blk, -1.0)
    nrs = [scaled(rs[t], -1.0) for t in range(RO)]
    o16 = new("b", 128)
    fill(o16, 0.0625)
    rm = new("f", 16)
    ts(rm, sub(qb, 0, 16), pm, ALU.is_equal)
    half, wb, thr = new("b", NS), new("f", NS), new("f", NS)
    fill(half, 0.5)
    scan(wb, half, sub(ones, 0, NS), 2.0 ** 97, ALU.mult, ALU.mult)
    move(thr, wb, 2.5)
    w16, w0, wcol = new("f", 16), new("f", 1), new("f", 12)
    tt(w16, sub(wb, 0, 16), rm, ALU.mult)
    add("v", lambda E, A: E.tensor_reduce(A(w0), A(w16), AxisListType.X, ALU.add), [w16], [w0], 64)
    ts(w0, w0, 2.0 ** -66, ALU.mult)
    ts(wcol, sub(wb, 0, NS, 16), 2.0 ** -30, ALU.mult, w0, ALU.mult)
    sw = new("b", 12)
    ts(sw, sub(c16, 0, 12), pm, ALU.add)
    srow = part(new("b", NS), 0, 1)
    iota(srow, [[1, NS]], 0, 0)
    spare = [part(new("h", NS), 0, 1) for n in range(2)]
    for n, c in enumerate((768.0 - 2048.0, 960.0)):
        ts(spare[n], srow, c, ALU.add)
    zrow = part(new("b", 512), 0, 1)
    memset(sub(zrow, 0, 144), 0.0)
    memset(sub(zrow, 144, 512), 0.0)
    one1 = part(o128, 0, 1)
    brow = part(new("b", NS), 0, 1)
    memset(brow, B)
    Z = new("b", 143)
    fill(Z, 0)
    move(sub(Z, 15, 143, 16), sub(blk, 0, 128, 16), 16.0)
    odi, odd, evn = new("i", 1), new("f", 2), new("f", 2)
    ts(odi, pid, 4, ALU.arith_shift_right, 1, ALU.bitwise_and)
    copy(sub(odd, 0, 1), odi)
    ts(sub(odd, 1, 2), sub(odd, 0, 1), -1.0, ALU.mult)
    ts(sub(evn, 0, 1), sub(odd, 0, 1), -1.0, ALU.mult, 1.0, ALU.add)
    ts(sub(evn, 1, 2), sub(odd, 0, 1), -1.0, ALU.add)
    IS = new("b", 640)
    for n in range(4):
        move(sub(IS, 160 * n, 160 * n + 160), Ipad, sub((evn, odd)[n // 2], n % 2, n % 2 + 1))
    p32i, p32, sq, R = new("i", 1), new("f", 1), new("b", 512), new("b", 512)
    ts(p32i, pid, 31, ALU.bitwise_and)
    copy(p32, p32i)
    iota(sq, [[1, 32], [0, 16]], 0, 0)
    ts(R, sq, p32, ALU.is_equal, -1.0, ALU.mult)
    R2 = scaled(R, -2.0) if any("m" in x for x in PIECES.values()) else None
    top = 17 * max(b - a for a, b in PARTS) // 16
    RK, DJ = new("b", top), new("b", 204)
    fill(RK, -1)
    memset(sub(RK, 0, top, 17), 131072.0)
    fill(DJ, -1)
    memset(sub(DJ, 16, 204, 17), 15.0)
    drow = [part(new("b", top), 0, 1) for n in range(2)]
    for n, c in enumerate((-BE, B)):
        memset(drow[n], 0.0)
        memset(sub(drow[n], 16, top, 17), c)
    memset(grid("ab3", 17, 0, NS, 1, 16, 17), 1024.0)
    iota(FT, [[1, NP + 64]], 0, 0)
    C4, SP, kcol, TRI, tri, D0, d0 = new("f", 2), new("f", 2), new("f", 2), new("b", 66), new("b", 66), new("b", 66), new("b", 66)
    ts(C4, sub(sw, 0, 2), 2048.0 - BE, ALU.add)
    ts(SP, sub(sw, 0, 2), 2048.0, ALU.add)
    ts(kcol, sub(sw, 0, 2), 0.5, ALU.add)
    fill(tri, 128)
    fill(d0, 4096)
    for c in range(2):
        ts(sub(tri, 33 * c, 33 * c + 32), kb, sub(sw, c, c + 1), ALU.is_gt, 128.0, ALU.mult)
        ts(sub(d0, 33 * c, 33 * c + 32), kb, sub(sw, c, c + 1), ALU.is_equal, -2.0, ALU.mult)
    ts(TRI, tri, 64.0, ALU.add)
    ts(D0, d0, 1.0, ALU.add)
    memset(sub(D0, 0, 66, 33), 0.0)
    gex, TE, own = new("b", 33), new("b", 66), new("f", 32)
    memset(sub(gex, 32, 33), 0.0)
    memset(sub(TE, 32, 66, 33), 0.0)
    fill(own, 4000)
    NFH, DH, UH = new("b", 416), new("h", 193), new("f", 416)
    memset(sub(NFH, 0, 416, 208), 0.0)
    memset(sub(NFH, 192, 416, 208), 1.0)
    memset(sub(DH, 0, 1), 0.0)
    need, room = 9.0, 55.0
    Ag, XE = new("b", 3072), new("b", 3072)
    Ebuf = new("b", 1248)
    junk = new("b", 2 * NS)
    e0b, h3w = new("f", 208), new("h", 193)
    fill(sub(e0b, NS, 208), 4000)
    memset(sub(h3w, NS, 193), 0.0)

    def wrap(src, M, off, s=None, u=None):
        n = width(src)
        if s is None:
            s = new("f", n)
        scan(s, src, sub(M, 0, n), -B, ALU.max, ALU.add)
        sw_ = sub(s, 15, n, 16)
        if off is None:
            return sw_, None
        if u is None:
            u = new("u", n // 16)
        ts(u, sw_, off, ALU.add)
        return sw_, u

    def flagwrap(o, scale, flag, row):
        mm([(o, one1, row), (o, scale, flag)])
        return wrap(o, MH, None)[0]

    def dedupe(hb, hcol, vb, dead, parts):
        es, pos, ns = [], 0, new("b", NS)
        for c in range(12):
            e = sub(Ebuf, pos - 16 * c, pos + NS - 16 * c)
            pos += NS - 16 * c
            ts(sub(e, 16 * c, NS), sub(hb, 16 * c, NS), hcol(c), ALU.is_equal, sub(wcol, c, c + 1), ALU.mult)
            es.append(e)
        for a, b in parts:
            items = [(sub(M1, max(a, 16 * c), b), blk, sub(es[c], max(a, 16 * c), b)) for c in range(b // 16)]
            ends = [(sub(M1, a, b), bigI, sub(x, a, b)) for x in (vb, dead) if x]
            if a:
                mm(items[:a // 16] + ends[:-1], last=False)
                mm(items[a // 16:] + ends[-1:], first=False)
            else:
                mm(items + ends)
            tt(sub(ns, a, b), sub(M1, a, b), sub(thr, a, b), ALU.is_ge)
        return ns

    def steps(Lh, r0, row):
        n = width(Lh) // 32
        t3 = grid("tt3", 16, r0, r0 + 2 * n, 1, 0, 16)
        add("v", lambda E, A: E.transpose(A(t3), A(Lh)), [Lh], [t3], vcost(32 * n, True))
        whole = grid("pd", 34, 0, n, 1, 0, 34)
        items = [(whole, one1, sub(row, 0, 34 * n))]
        for a in range(2):
            for b in range(2):
                for s in range(2):
                    lo = 160 * (2 * a + s) + 16 * (1 + a - b)
                    items.append((grid("pd", 34, 0, n, 1, 17 * a + 1 - s, 17 * a + 17 - s), sub(IS, lo, lo + 128),
                                  grid("tt3", 16, r0 + b, r0 + 2 * n, 2, 0, 16)))
        mm(items + [(whole, one1, sub(zrow, 0, 34 * n))])
        d = new("f", 34 * n)
        move(d, whole)
        return d

    def pick(a, b, d, nf, u, eu, off):
        n = 17 * (b - a) // 16
        key, sm = sub(KB[turn["k"] % 2], 0, n), new("f", n)
        turn["k"] += 1
        mm([(key, sub(Z, 15 - p, 143 - p), grid("ab3", 17, a + p, b, 16, 0, 17)) for p in range(16)])
        scan(sm, sub(RK, 0, n), key, 0.0, ALU.add, ALU.min)
        tt(nf, key, sm, ALU.not_equal)
        scan(u, d, nf, 0.0, ALU.add, ALU.mult)
        ts(eu, sub(u, 16, n, 17), off, ALU.add)

    def distances(step, h, Lu, x0T):
        a = a0 = PARTS[h][0]
        for word in PIECES[step, h].split():
            end = a + int(word[1:])
            while a < end:
                b = min(end, (a - a0) // 32 * 32 + 32 + a0)
                lu, src, out = sub(Lu, a, b), sub(Ag, 16 * a, 16 * b), grid("ab3", 17, a, b, 1, 0, 16)
                if word[0] == "v":
                    gtt(src, Xg, lu, sub(XE, 16 * a, 16 * b), ALU.subtract)
                    act(out, src, ACT.Abs)
                else:
                    q = (a - a0) // 32 * 32
                    o = sub(BK[turn["s"] % 3], 0, 16 * (b - a))
                    turn["s"] += 1
                    xt = x0T[a // 32]
                    fold = sub(R if word[0] == "w" else R2, 16 * (a - a0 - q), 16 * (b - a0 - q), 1, xt[4], xt[5])
                    mm([(o, xt, fold)], last=False)
                    gather("a" if q else "w", src, Xg, lu)
                    mm([(o, I if word[0] == "w" else nI, src)], first=False)
                    if word[0] == "w":
                        act(out, o, ACT.Abs)
                    else:
                        tt(out, o, src, ALU.max)
                a = b

    def slots(nf):
        n = width(nf)
        uj, ju = new("b", n), new("u", n // 17)
        scan(uj, sub(DJ, 0, n), nf, 0.0, ALU.add, ALU.mult)
        copy(ju, sub(uj, 16, n, 17))
        return ju

    def w16_(v, a, b, n=16):
        return sub(v, a * n // 16, b * n // 16)

    for t in range(RO):
        h0 = sub(ho16, 12 * t, 12 * t + 12)
        x0, dm = sub(PRE[t], 0, NS), sub(PRE[t], 208, 208 + NS)
        vbias = (-0.1, -0.9)[t]
        mark(V, h0, tin[t])
        HLs = hl32 if t == 0 else HLg
        L0h, s0, s1, hbb = new("h", NS), new("f", NS), new("f", NS), new("h", 2 * NS)
        hb2, hb1, hs1 = sub(hbb, 0, NS), sub(hbb, NS, 2 * NS), sub(s1, 15, NS, 16)
        L1u, L1h, L2u, L2h = new("u", NS), new("h", NS), new("u", NS), new("h", NS)
        e0u, h1u = new("u", 12), new("u", 12)
        for n, (a, b) in enumerate(OPEN[t]):
            gather("a" if t else "v", sub(L0h, a, b), HLs, w16_(h0, a, b, 1))
            e0p = sub((M0, M1)[n % 2], a, b)
            mm([(e0p, rs[t], sub(L0h, a, b))])
            wrap(e0p, ME, BE, sub(s0, a, b), w16_(e0u, a, b, 1))
            move(sub(e0b, a, b), e0p)
            gather("a" if t else "w", sub(hb1, a, b), Wg, w16_(e0u, a, b, 1))
            wrap(sub(hb1, a, b), MH, B, sub(s1, a, b), w16_(h1u, a, b, 1))
            gather("v", sub(L1u, a, b), HLs, w16_(h1u, a, b, 1))
            copy(sub(L1h, a, b), sub(L1u, a, b))
        if t and VIA:
            W16, Wu, LW = new("h", NP), new("u", NP // 16), new("f", NP)
            for a in range(0, NP, 512):
                move(sub(W16, a, a + 512), sub(W, a, a + 512))
            wp = sub(BK[1], 0, 128)
            mm([(wp, sub(Z, 15 - p, 143 - p), sub(W16, p, NP, 16)) for p in range(16)])
            ts(Wu, wp, 1.0 / 256, ALU.mult)
            for a in range(0, NP, 256):
                gather("a", sub(LW, a, a + 256), HLg, w16_(Wu, a, a + 256, 1))
        d1 = [steps(sub(L1h, a, b), a // 16, drow[0]) for a, b in PARTS]
        vb1 = new("b", NS)
        gather("a", vb1, Vg, h1u, vbias)
        hc = new("f", 12)
        ts(hc, hs1, B, ALU.add)
        ns1 = dedupe(hb1, lambda c: sub(hc, c, c + 1), vb1, None, ((0, NS),))
        pw = flagwrap(sub(M1, 256, 256 + NS), I2k, ns1, spare[0])
        twM, offM = new("f", 12), new("u", 12)
        tt(twM, pw, hs1, ALU.max)
        ts(offM, twM, B, ALU.add)
        mark(V, offM, tin[t])
        x0T = []
        for n, (a, b) in enumerate(TURN):
            gather("a", sub(x0, a, b), Xg, w16_(e0u, a, b, 1))
            o, xt = part(sub(KB[n % 2], 0, 128), 0, b - a), part(new("b", 128), 0, b - a)
            mm([(o, sub(x0, a, b), I)])
            move(xt, o)
            x0T += [part(xt, q, q + 32) for q in range(0, b - a, 32)]
        for eng, a, b in FOLD:
            ahead(a * len(PARTS) // NS if eng == "v" else None)
            for j in range(16):
                o = sub(XE, 16 * a + j, 16 * b, 16)
                if eng == "g":
                    asel(o, sub(x0, a, b), [[0, b - a]], ALU.is_ge, 0, 0)
                else:
                    move(o, sub(x0, a, b), first="v")
        ahead(None)
        if t == 0:
            message(sub(PRE[t], 0, 208), sub(PRR[t], 0, 208), t, 1)
        else:
            message(PRE[t], PRR[t], t, 1)
        sh = new("f", NS)
        nf1, nf2, u1, u2 = new("b", 204), new("b", 204), new("f", 204), new("f", 204)
        e1u, e2u, h2u = new("u", 12), new("u", 12), new("u", 12)
        ge1, ge2, vb2 = new("b", NS), new("b", NS), new("b", NS)
        d2 = []
        for h in range(len(PARTS)):
            ahead(h)
            distances(1, h, L1u, x0T)
        for h, (a, b) in enumerate(PARTS):
            ahead(h)
            pick(a, b, d1[h], w16_(nf1, a, b, 17), w16_(u1, a, b, 17), w16_(e1u, a, b, 1), BE)
            gather("w", sub(hb2, a, b), Wg, w16_(e1u, a, b, 1))
            wrap(sub(hb2, a, b), MH, B, sub(sh, a, b), w16_(h2u, a, b, 1))
            if t and VIA:
                gather("v", sub(L2u, a, b), LW, w16_(e1u, a, b, 1))
            else:
                gather("v", sub(L2u, a, b), HLs, w16_(h2u, a, b, 1))
            copy(sub(L2h, a, b), sub(L2u, a, b))
            d2.append(steps(sub(L2h, a, b), 12 + a // 16, drow[0]))
            distances(2, h, L2u, x0T)
        ahead(None)
        dead1, hm = new("b", NS), new("f", NS)
        for a, b in JUDGE[0]:
            gtt(sub(ge1, a, b), Xg, w16_(e1u, a, b, 1), sub(dm, a, b), ALU.is_ge)
            cp, hp = sub(M0, a, b), sub(M0, 256 + a, 256 + b)
            mm([(cp, I2k, sub(ns1, a, b)), (cp, blk, sub(ge1, a, b))])
            ts(sub(dead1, a, b), cp, need, ALU.is_ge)
            mm([(hp, one1, sub(brow, a, b)), (hp, I, sub(hb2, a, b)), (hp, I2k, sub(dead1, a, b))])
            wrap(hp, MH, None, sub(hm, a, b))
        gather("a", vb2, Vg, h2u, vbias)
        ns2 = dedupe(hb2, lambda c: sub(hm, 16 * c + 15, 16 * c + 16), vb2, dead1, JUDGE[1])
        failed, pos, m2n, paid = new("b", NS), new("b", NS), new("b", NS), new("b", NS)
        e1b, e2b, tw2 = new("h", NS), new("h", NS), new("f", 24)
        gather("a", e1b, FT, e1u)
        j1u = slots(nf1)

        def pay(a, b):
            n, k = b - a, (b - a) // 16
            Lf, ohs, Tl, offL = new("f", 3 * n), new("b", 3 * n), new("f", 3 * n), new("u", 3 * k)
            gather("a", sub(e2b, a, b), FT, w16_(e2u, a, b, 1))
            move(sub(ohs, 0, n), sub(ones, 0, n), sub(rm, t, t + 1))
            gather("a", sub(ohs, n, 2 * n), rm, w16_(j1u, a, b, 1))
            gather("a", sub(ohs, 2 * n, 3 * n), rm, slots(w16_(nf2, a, b, 17)))
            for i, Lh in enumerate((L0h, L1h, L2h)):
                move(sub(Lf, n * i, n * i + n), sub(Lh, a, b))
            cn, cq = sub(M1, 0, n), sub(M1, n, 2 * n)
            g2, n2 = sub(ge2, a, b), sub(ns2, a, b)
            mm([(cn, nI2k, n2), (cn, blk, g2)])
            mm([(cq, nI2k, sub(ns1, a, b)), (cq, I3k, sub(dead1, a, b)), (cq, nI2k, n2), (cq, blk, g2)])
            ts(sub(m2n, a, b), cn, need, ALU.is_ge, -1.0, ALU.mult)
            ts(sub(paid, a, b), cq, need, ALU.is_ge)
            pA, pC, l0 = sub(BK[1], 0, n), sub(BK[1], n, 2 * n), sub(L0h, a, b)
            mm([(pA, I, sub(e1b, a, b)), (pA, nrs[t], l0), (pC, I, sub(e2b, a, b)), (pC, nrs[t], l0)], each=2)
            y1, y2 = new("h", n), new("h", n)
            tt(y1, pA, sub(paid, a, b), ALU.mult)
            tt(y2, pC, sub(m2n, a, b), ALU.mult)
            dl = [sub(BK[2], n * i, n * i + n) for i in range(3)]
            mm([(dl[2], rs[t], l0), (dl[2], nI, sub(e2b, a, b)), (dl[1], nI, y1), (dl[1], nI, y2)], each=2)
            mm([(dl[0], I, y1)])
            tt(Tl, sub(BK[2], 0, 3 * n), ohs, ALU.mult)
            pw = flagwrap(sub(M1, 2 * n, 3 * n), I3k, sub(m2n, a, b), sub(spare[1], a, b))
            tw = new("f", k)
            tt(tw, pw, sub(sh, a + 15, b, 16), ALU.max)
            copy(sub(offL, 0, k), sub(ho32, 12 * t + a // 16, 12 * t + b // 16))
            ts(sub(offL, k, 2 * k), w16_(twM, a, b, 1), B, ALU.add)
            ts(sub(offL, 2 * k, 3 * k), tw, B, ALU.add)
            scatter(HL, offL, Tl, Lf)
            tt(w16_(tw2, a, b, 1), pw, sub(s0, a + 15, b, 16), ALU.max)
            tt(w16_(tw2, NS + a, NS + b, 1), pw, sub(u1, a * 17 // 16 + 16, b * 17 // 16, 17), ALU.max)

        for h, (a, b) in enumerate(PARTS):
            pick(a, b, d2[h], w16_(nf2, a, b, 17), w16_(u2, a, b, 17), w16_(e2u, a, b, 1), BE)
        for a, b in JUDGE[1]:
            gtt(sub(ge2, a, b), Xg, w16_(e2u, a, b, 1), sub(dm, a, b), ALU.is_ge)
            gather("a", sub(h3w, a, b), Wg, w16_(e2u, a, b, 1))
            cp = sub(M0, a, b)
            mm([(cp, I2k, sub(ns2, a, b)), (cp, blk, sub(ge2, a, b))])
            ts(sub(failed, a, b), cp, need, ALU.is_lt)
            scan(sub(pos, a, b), sub(failed, a, b), sub(failed, a, b), sub(pos, a - 1, a) if a else 0.0, ALU.add, ALU.max)
            for pa, pb in PAY[:-1]:
                if pb == b:
                    pay(pa, pb)
        mAs, mAr, acc = new("u", 8), new("u", 8), new("f", 2)
        memset(mAs, 0)
        cut = PARTS[-1][0]
        for a, b in ((0, cut), (cut, 193)):
            lo = max(a, 1)
            dh = sub(BK[0], lo, b)
            mm([(dh, I, sub(h3w, lo - 1, b - 1)), (dh, nI, sub(h3w, lo, b))])
            move(sub(DH, lo, b), dh)
            for c in range(2):
                e = min(b, NS)
                ts(sub(NFH, 208 * c + lo, 208 * c + e), sub(pos, lo - 1, e - 1), sub(kcol, c, c + 1), ALU.is_gt)
            for c in range(2):
                scan(sub(UH, 208 * c + a, 208 * c + b), sub(DH, a, b), sub(NFH, 208 * c + a, 208 * c + b),
                     sub(UH, 208 * c + a - 1, 208 * c + a) if a else 0.0, ALU.add, ALU.mult)
        for c in range(2):
            act(sub(junk, NS * c, NS * c + NS), pos, ACT.Sign, bias=sub(kcol, c, c + 1), scale=-1.0, acc=sub(acc, c, c + 1))
        sidx = sub(mAs, 2, 4)
        ts(sidx, acc, 0.5, ALU.mult, 96.0, ALU.add)
        copy(sub(mAs, 0, 2), sub(UH, 192, 416, 208))
        message(mAs, mAr, t, 2)
        e0c, mBs, mBr = new("f", 32), new("f", 4), new("f", 4)
        memset(mBs, 0.0)
        gather("a", e0c, e0b, sidx)
        esc, _u = wrap(e0c, ME, None)
        ts(sub(mBs, 0, 2), esc, BE + B, ALU.add)
        message(mBs, mBr, t, 3)
        pay(*PAY[-1])
        tc, offo = new("f", 2), new("u", 2)
        tt(tc, esc, C4, ALU.min)
        ts(offo, tc, BE, ALU.add)
        scatter(FT, offo, own)
        offW = new("u", 24)
        ts(offW, tw2, BE, ALU.add)
        for n in range(2):
            scatter(W, sub(offW, 12 * n, 12 * n + 12), sub(hbb, NS * n, NS * n + NS))
        h3u, su = sub(mAr, 0, 2), sub(mAr, 2, 4)
        x0m, dmm = new("b", 32), new("b", 32)
        Lxu, Lxh = new("u", 32), new("h", 32)
        gather("v", Lxu, HLg, h3u)
        gather("a", x0m, sub(PRR[t], 0, 208), su)
        copy(Lxh, Lxu)
        gather("a", dmm, sub(PRR[t], 208, 416), su)
        if t == RO - 1:
            dma("s", lambda E, A, T: E.dma_start(T.yl[:], A(HLg)), [HLg], [], 393216)
            dma("s", lambda E, A, T: E.dma_start(T.yw[:], T.af[0:128:16, W[1]:W[1] + NP]), [Wg], [], 65536)
        nv = 16 * XSPLIT
        xb = BK[0]
        mm([(xb, one1, zrow)], last=False)
        mm([(sub(xb, j, 512, 16), nI, x0m) for j in range(16)], first=False, last=False)
        gather("v", sub(Ag, 0, nv), Xg, sub(Lxu, 0, XSPLIT))
        gather("a", sub(Ag, nv, 512), Xg, sub(Lxu, XSPLIT, 32))
        mm([(xb, I, sub(Ag, 0, 512))], first=False)
        act(grid("ab3", 17, 0, 32, 1, 0, 16), xb, ACT.Abs)
        nfx, ux, fu = new("b", 34), new("f", 34), new("u", 2)
        pick(0, 32, steps(Lxh, 24, drow[1]), nfx, ux, fu, -B)
        fall, mCs, mCr = new("f", 32), new("b", 32), new("b", 32)
        gtt(sub(gex, 0, 32), Xg, fu, dmm, ALU.is_ge)
        gather("a", fall, FT, fu, B)
        gather("a", mCs, Xg, fu)
        message(mCs, mCr, t, 4)
        pv, flag, fin = sub(KB[turn["k"] % 2], 0, 66), new("b", 66), new("f", 66)
        mm([x for c in range(2) for x in ((sub(pv, 33 * c, 33 * c + 33), I, sub(TRI, 33 * c, 33 * c + 33)),
                                          (sub(pv, 33 * c, 33 * c + 33), nblk, gex))], each=2)
        for c in range(2):
            ts(sub(TE, 33 * c, 33 * c + 32), fall, sub(ux, 17 * c + 16, 17 * c + 17), ALU.is_equal, room, ALU.mult)
        tt(flag, pv, TE, ALU.is_le)
        scan(fin, D0, flag, 0.0, ALU.mult, ALU.subtract)
        mDs, mDr, offb = new("u", 8), new("u", 8), new("u", 2)
        memset(mDs, 0)
        for c in range(2):
            ts(sub(mDs, c, c + 1), sub(fin, 33 * c + 32, 33 * c + 33), sub(mBr, c, c + 1), ALU.add, sub(SP, c, c + 1), ALU.min)
        message(mDs, mDr, t, 5)
        for c in range(2):
            ts(sub(offb, c, c + 1), sub(fin, 33 * c + 32, 33 * c + 33), sub(ux, 17 * c + 16, 17 * c + 17), ALU.add, sub(SP, c, c + 1), ALU.min)
        scatter(X, offb, x0m)
        if t < RO - 1:
            scatter(FT, offo, e0c)
            pc = sub(M0, 256, 256 + NS)
            mm([(pc, o16, paid)])
            cnt, ci, cj, bf_, nd = new("f", 1), new("i", 1), new("i", 1), new("f", 1), new("f", 2)
            act(sub(junk, 0, NS), pc, ACT.Copy, acc=cnt)
            copy(ci, cnt)
            ts(cj, ci, 1, ALU.bitwise_and)
            copy(bf_, cj)
            ts(sub(nd, 0, 1), bf_, 9.0, ALU.add)
            ts(sub(nd, 1, 2), bf_, -1.0, ALU.mult, 55.0, ALU.add)
            need, room = sub(nd, 0, 1), sub(nd, 1, 2)
        scatter(X, sub(mDr, 0, 2), mCr)
    for k, eng in enumerate(("s", "a")):
        dma(eng, lambda E, A, T, k=k: E.dma_start(T.yx[64 * k:64 * k + 64, :], A(part(Xg, 64 * k, 64 * k + 64))), [Xg], [], 262144)
    return ops, size, sent


def depend(ops):
    log = {}
    for n, op in enumerate(ops):
        acc = []
        for wr, vs in ((False, op["r"]), (True, op["w"])):
            for v in vs:
                if is_ps(v):
                    acc.append(((v[0], 0), 0, 1, wr, 1))
                else:
                    acc.append((v[0], v[1], v[2], wr, v[3]))
        deps = set()
        for key, lo, hi, wr, st in acc:
            for (m, l2, h2, w2, s2) in log.get(key, []):
                clash = wr or w2 or (key[0][0] == "p" and (ops[m]["eng"] != op["eng"] or "alt" in op or "alt" in ops[m]))
                if l2 < hi and lo < h2 and clash and m != n and not (st == s2 and st and (lo - l2) % st):
                    deps.add(m)
        op["soft"] = {m for m in deps if ops[m]["eng"] == op["eng"] == "t" or ops[m]["kind"] == op["kind"] == "send"}
        for key, lo, hi, wr, st in acc:
            lst = log.setdefault(key, [])
            if wr and st == 1:
                lst[:] = [x for x in lst if not (lo <= x[1] and x[2] <= hi)]
            lst.append((n, lo, hi, wr, st))
        op["deps"] = sorted(deps)


def schedule(ops, seed, jitter):
    n = len(ops)
    dur0, occ0, bus = [0] * n, [0] * n, 1900
    for i, op in enumerate(ops):
        if op["kind"] == "dma":
            bus = (bus if not op["deps"] else 1900) + op["cost"] // 200
            dur0[i], occ0[i] = bus, 60
        else:
            dur0[i], occ0[i] = op["cost"], 0 if op["eng"] == "x" else op["cost"]
    pred, above = [], []
    for op in ops:
        cover = 0
        for d in op["deps"]:
            cover |= above[d]
        pred.append([(d, 0 if d in op["soft"] else HOP) for d in op["deps"] if not cover >> d & 1])
        for d in op["deps"]:
            cover |= 1 << d
        above.append(cover)
    loads = [i for i, op in enumerate(ops) if op["eng"] == "s" and not op["deps"]]
    for a, b in zip(loads, loads[1:]):
        pred[b].append((a, occ0[a] - dur0[a]))
    succ = [[] for _ in ops]
    for i in range(n):
        for d, h in pred[i]:
            succ[d].append((i, h))
    alt = [{e: c for e, (fn, c) in op["alt"].items()} if "alt" in op else None for op in ops]
    slack = [dur0[i] - occ0[i] for i in range(n)]
    r = [seed]

    def rnd(m):
        r[0] = (r[0] * 1103515245 + 12345) % 2147483648
        return (r[0] >> 8) % m

    def gap(lst, at, need):
        k, hi = 0, len(lst)
        m = hi
        while k < hi:
            mid = (k + hi) // 2
            if lst[mid][1] <= at:
                k = mid + 1
            else:
                hi = mid
        while k < m and at + need > lst[k][0]:
            at = lst[k][1]
            k += 1
        return k, at

    def place(stretch, rank, eng, free=()):
        inside, before, after, head, busy0, back = stretch
        left = {i: len(before[i]) for i in inside}
        ready = sorted((rank[i], i) for i in inside if not left[i])
        busy = {e: list(b) for e, b in busy0.items()}
        start, fin, eng = {}, {}, dict(eng)
        while ready:
            i = ready.pop(0)[1]
            t = head[i]
            for d, h in before[i]:
                if fin[d] + h > t:
                    t = fin[d] + h
            if alt[i]:
                if i in free:
                    eng[i] = min("va", key=lambda e: gap(busy[e], t, alt[i][e])[1] + alt[i][e])
                d = occ = alt[i][eng[i]]
            else:
                d, occ = dur0[i], occ0[i]
            if occ:
                lead = slack[i] if back else 0
                lst = busy[eng[i]]
                k, at = gap(lst, t + lead, occ)
                t = at - lead
                lst.insert(k, (at, at + occ))
            start[i], fin[i] = t, t + d
            for s, h in after[i]:
                left[s] -= 1
                if left[s] == 0:
                    ready.append((rank[s], s))
                    ready.sort()
        return start, fin, eng

    every = list(range(n))
    none = {e: [] for e in "vatgsx"}
    whole = (every, pred, succ, [0] * n, none, False)
    turned = (every, succ, pred, [0] * n, none, True)

    def improve(now, t0, t1, passes):
        st0, fin0, eng0 = now
        order = sorted(every, key=lambda i: (st0[i], i))
        inside = [i for i in order if t0 <= st0[i] < t1]
        here = set(inside)
        far, nxt, tail = {}, {}, {}
        for i in reversed(order):
            if st0[i] >= t1:
                e = eng0[i]
                far[i] = max([fin0[i] - st0[i] + max([h + far[s] for s, h in succ[i]] + [0])]
                             + ([fin0[i] - st0[i] - slack[i] + far[nxt[e]]] if e in nxt and e != "x" else []))
                nxt[e] = i
        before = {i: [(d, h) for d, h in pred[i] if d in here] for i in inside}
        after = {i: [(s, h) for s, h in succ[i] if s in here] for i in inside}
        head = {i: max([fin0[d] + h for d, h in pred[i] if d not in here] + [0]) for i in inside}
        for i in inside:
            tail[i] = max([h + far[s] for s, h in succ[i] if s in far] + [0])
        queue = {e: far[nxt[e]] if e in nxt and e != "x" else 0 for e in "vatgsx"}
        busy = {e: [] for e in "vatgsx"}
        for i in order:
            if st0[i] < t0 and eng0[i] != "x":
                busy[eng0[i]].append((st0[i], fin0[i] - slack[i]))
        for e in busy:
            busy[e] = busy[e][-40:]
            if busy[e]:
                busy[e].insert(0, (-1, busy[e][0][0]))
        ends0 = {(e, b): -1 for e in busy for a, b in busy[e]}
        stretch = (inside, before, after, head, busy, False)
        flex = [i for i in inside if alt[i]]

        def score(x):
            st, fin, eng = x
            top, last = 0, -1
            for i in inside:
                v = max(fin[i] + tail[i], fin[i] - slack[i] + queue[eng[i]])
                if v > top:
                    top, last = v, i
            return top + sum(st.values()) / (20.0 * n), last
        x = ({i: st0[i] for i in inside}, {i: fin0[i] for i in inside}, {i: eng0[i] for i in inside})
        top = best = (score(x), x)
        for it in range(passes):
            st, fin, eng = best[1]
            free, held, rank = (), [], dict(st)
            if it % 3:
                ends = dict(ends0)
                for i in inside:
                    ends[eng[i], fin[i] - slack[i]] = i
                i = best[0][1]
                while st[i] > head[i]:
                    tight = [d for d, h in before[i] if fin[d] + h == st[i]]
                    if tight:
                        i = tight[rnd(len(tight))]
                    else:
                        p = ends[eng[i], st[i]]
                        if p < 0:
                            break
                        held.append((p, i))
                        i = p
            if held:
                for _ in range(1 + rnd(2)):
                    p, i = held[rnd(len(held))]
                    how = rnd(5)
                    if how == 0:
                        rank[p] = st[i] + 1 + rnd(600)
                    elif how == 1:
                        rank[i] = st[p] - 1 - rnd(600)
                    elif how == 4:
                        near = [c for c in flex if eng[c] == eng[i] and st[i] - 3000 < st[c] <= st[i]]
                        if near:
                            c = near[rnd(len(near))]
                            eng = dict(eng)
                            eng[c] = "v" if eng[c] == "a" else "a"
                    else:
                        todo, gain, reach = [i if how == 2 else p], 100 + rnd(1500), st[p] - 500 - rnd(6000)
                        seen = set(todo)
                        while todo:
                            c = todo.pop()
                            rank[c] -= gain
                            for d, h in before[c]:
                                if d not in seen and st[d] > reach:
                                    seen.add(d)
                                    todo.append(d)
            else:
                mid, wide, amp = t0 + rnd(t1 - t0), 500 + rnd(4000), 200 + rnd(2500)
                for i in inside:
                    if abs(st[i] - mid) < wide and rnd(4) == 0:
                        rank[i] += rnd(amp)
                if rnd(2):
                    free = {c for c in flex if abs(st[c] - mid) < wide and rnd(3) == 0}
            x = place(stretch, rank, eng, free)
            sc = score(x)
            if sc[0] <= best[0][0] + SLACK * (1.0 - it / passes):
                best = (sc, x)
                if sc[0] < top[0][0]:
                    top = best
        rank, eng = dict(st0), dict(eng0)
        rank.update(top[1][0])
        for i in far:
            rank[i] += 100000
        eng.update(top[1][2])
        return place(whole, rank, eng)

    def span(x):
        return max(x[1].values())

    def turn(x, rounds):
        for _ in range(rounds):
            back = place(turned, {i: -f for i, f in x[1].items()}, x[2])[1]
            y = place(whole, {i: -b + rnd(jitter + 1) for i, b in back.items()}, x[2])
            if span(y) < span(x):
                x = y
        return x
    prio = [0] * n
    for i in range(n - 1, -1, -1):
        prio[i] = dur0[i] + max([prio[s] + h for s, h in succ[i]] + [0])
    now = turn(place(whole, [-p - op["lead"] for p, op in zip(prio, ops)], {i: op["eng"] for i, op in enumerate(ops)}), 30)
    for sweep in range(SWEEPS):
        t0 = -(sweep % 2) * (WIDE // 4)
        while t0 < span(now) - 8000:
            x = improve(now, max(t0, 0), t0 + WIDE, PASSES)
            if span(x) <= span(now) + 30:
                now = x
            t0 += WIDE // 2
        now = turn(now, 10)
    start, fin, eng = now
    for i in every:
        if alt[i]:
            ops[i]["eng"] = eng[i]
            ops[i]["fn"], ops[i]["cost"] = ops[i]["alt"][eng[i]]
    return sorted(every, key=lambda i: (start[i], i)), [start[i] for i in every], [fin[i] for i in every]


def signals(ops, order):
    token, known, after, count, nd = {}, {e: {} for e in "vatgs"}, {}, {e: 0 for e in "vatg"}, 0
    waits = {}
    seq = {e: 0 for e in "vatg"}
    for i in order:
        op = ops[i]
        if op["kind"] == "c":
            seq[op["eng"]] += 1
            token[i] = (op["eng"], seq[op["eng"]])
        elif op["kind"] == "dma":
            token[i] = ("d%d" % nd, 1)
            nd += 1
        elif op["kind"] == "recv":
            token[i] = ("r%d%d" % op["extra"], 1)
        else:
            token[i] = ("l%d%d" % op["extra"][2:], 1)
    used = set()
    for i in order:
        op = ops[i]
        e = op["eng"]
        if e == "x":
            after[i] = {token[i][0]: 1}
            continue
        k = known[e]
        ws = {}
        for d in sorted(op["deps"], key=lambda d: -token[d][1]):
            s, c = token[d]
            if d in op["soft"]:
                continue
            if k.get(s, 0) < c:
                ws[s] = max(ws.get(s, 0), c)
                used.add(d)
                for s2, c2 in after[d].items():
                    if k.get(s2, 0) < c2:
                        k[s2] = c2
        waits[i] = ws
        a = dict(k)
        a[token[i][0]] = token[i][1]
        after[i] = a
    val = {}
    for i in order:
        if ops[i]["kind"] == "c" and i in used:
            count[ops[i]["eng"]] += 1
            val[token[i]] = count[ops[i]["eng"]]
    return token, waits, used, val, nd


OPS, SIZE, SENT = plan()
depend(OPS)
ORDER, START, FIN = schedule(OPS, SEED, JITTER)
TOKEN, WAITS, USED, VAL, NDMA = signals(OPS, ORDER)

SCRATCH = {ARENA[k][0]: ("sbuf", [128, SIZE[k]], ARENA[k][1]) for k in ARENA}
SCRATCH["ab3"] = ("sbuf", [128, NS, 17], "float16")
SCRATCH["tt3"] = ("sbuf", [128, 26, 16], "float16")
for _k in range(7):
    SCRATCH["p%d" % _k] = ("psum", [128, 512], "float32")
SCRATCH["pd"] = ("psum", [128, 15, 34], "float32")
SEMAPHORES = ["qv", "qa", "qt", "qg"] + ["d%d" % k for k in range(NDMA)] + ["%s%d%d" % (a, t, k) for a in "rl" for t, k in SENT]


def rank_program(g, core, T, topo):
    rank = T.rank_of(core)
    if rank is None:
        return
    n = len(T.cores)
    Q = {"v": g.vector, "a": g.scalar, "t": g.tensor, "g": g, "s": g.sync}

    def A(v):
        if len(v) > 6:
            return T[v[0]][v[4]:v[5], v[6][0], v[6][1]]
        if v[3] == 1:
            return T[v[0]][v[4]:v[5], v[1]:v[2]]
        return T[v[0]][v[4]:v[5], v[1]:v[2]:v[3]]

    def peer(t, back):
        d = 1 + t % (n - 1)
        return T.cores[(rank - d) % n] if back else T.cores[(rank + d) % n]

    def amount(s, c):
        if s in ("v", "a", "t", "g"):
            return T.sem["q" + s], VAL[(s, c)]
        if s[0] == "d":
            return T.sem[s], 16
        t, k = int(s[1]), int(s[2])
        if s[0] == "r":
            return T.sem[s], len(topo.engines(peer(t, k not in BACK), core))
        return T.sem[s], len(topo.engines(core, peer(t, k in BACK)))

    waited = set()
    for i in ORDER:
        op = OPS[i]
        if op["kind"] == "recv":
            continue
        E = Q[op["eng"]]
        for s, c in WAITS[i].items():
            sem, v = amount(s, c)
            E.wait_ge(sem, v)
            waited.add(s)
        if op["kind"] == "c":
            ins = op["fn"](E, A)
            if i in USED:
                ins.then_inc(T.sem["q" + op["eng"]], 1)
        elif op["kind"] == "dma":
            op["fn"](E, A, T).then_inc(T.sem[TOKEN[i][0]], 16)
        else:
            src, dst, t, k = op["extra"]
            to = peer(t, k in BACK)
            rid, pid = topo.addr(to, core)
            g.remote_dma(A(dst), A(src), T.sem["r%d%d" % (t, k)], T.sem["l%d%d" % (t, k)], pid, rid, topo.mask(core, to))
    for i in ORDER:
        s = TOKEN[i][0]
        if OPS[i]["kind"] != "c" and s not in waited:
            sem, v = amount(s, 1)
            g.sync.wait_ge(sem, v)
